import numpy as np, ml_dtypes
CORES = [40,41,42,43,44,45,46,47]
N = 8
import mx_ref
BF = ml_dtypes.bfloat16
def gentries(a):
    return np.ascontiguousarray(a.reshape(8, 16, -1).transpose(0, 2, 1)).reshape(8, -1)
def gtable(e):
    e = np.asarray(e); return np.ascontiguousarray(e.reshape(8, -1, 16).transpose(0, 2, 1)).reshape(128, -1).astype(np.int32)
def gcols(t, e):
    v = np.concatenate([t.reshape(8, 16, -1, 4), np.zeros((8, 16, 1, 4), BF)], axis=2)
    return np.ascontiguousarray(np.stack([v[g][:, e[g]] for g in range(8)])).reshape(128, -1)
def gpick(z, e):
    return np.concatenate([z[16 * g:16 * g + 16][:, e[g]] for g in range(8)])
def tile(rs):
    return np.stack(rs, axis=2).reshape(128, -1).astype(BF)
def pick(q, e):
    c = np.concatenate([q[0].reshape(128, -1, 4), np.zeros((128, 1, 4), np.uint8)], axis=1); s = np.concatenate([q[1], np.ones((16, 1), np.uint8)], axis=1)
    return (np.ascontiguousarray(c[:, e].reshape(128, -1)), np.ascontiguousarray(s[:, e]))
def join(*qs):
    return (np.concatenate([q[0] for q in qs], axis=1), np.concatenate([q[1] for q in qs], axis=1))
def put(q, e, v):
    c, s = q[0].reshape(128, -1, 4).copy(), q[1].copy(); c[:, e] = v[0].reshape(128, -1, 4); s[:, e] = v[1]
    return (c.reshape(128, -1), s)
def pk(c, s):
    return (np.ascontiguousarray(c), mx_ref.live(s))
def emit(q):
    return q[0], q[1]
def packed(v, rng):
    q = [mx_ref.quantize(np.ascontiguousarray(v[r])) for r in range(N)]
    return np.stack([a for a, b in q]), np.stack([mx_ref.plane(b, rng) for a, b in q])
def values_of_codes():
    e, c = np.zeros((128, 128, 4), np.float32), np.zeros((128, 2, 4), np.uint8)
    e[np.arange(128), np.arange(128), 0] = 1
    c[:127, :, 0] = np.arange(256).reshape(2, 128).T[:127]
    return mx_ref.matmul(mx_ref.quantize(e.reshape(128, 512).astype(BF)), (c.reshape(128, 8), np.full((16, 2), 127, np.uint8))).T.reshape(-1).astype(np.float64)
CODE_VALUE, SCALE_VALUE = values_of_codes(), 2.0 ** (np.arange(256) - 127.0)
def decode(q):
    return (CODE_VALUE[q[0]].reshape(16, 8, -1, 4) * SCALE_VALUE[q[1]][:, None, :, None] + 0.0).reshape(128, -1).astype(np.float32)
def f(rng, *shape):
    return mx_ref.flush((rng.standard_normal(shape, dtype=np.float32) * np.exp2(rng.integers(-2, 3, shape[:-1] + (1,)))).astype(BF))
def wide(rng, *shape, cols=0):
    v = rng.standard_normal(shape, dtype=np.float32) * np.exp2(rng.integers(-12, 13, shape)).astype(np.float32)
    if cols: v *= np.repeat(np.exp2(rng.integers(-cols, cols + 1, shape[:-2] + (1, shape[-1] // 4))) * (rng.random(shape[:-2] + (1, shape[-1] // 4)) > 0.0625), 4, axis=-1).astype(np.float32)
    return mx_ref.flush(v.astype(BF))
C, B = 320, 160
STEP = [1, 2, 4]
def big(v):
    v = v.astype(np.float32)
    v[np.abs(v) < np.float32(2.0 ** -16)] = 0
    return v.astype(BF)
def numbers_of(rng):
    return {"x": big(f(rng, N, 128, 4 * C)), "u": np.array(f(rng, N, 128, 512)), "v": np.array(f(rng, N, 128, 512))}
def layers(rng):
    k = np.stack([np.exp2(rng.permutation(128) % 5 - 2.0) for r in range(N)])[:, :, None].astype(np.float32)
    return big(rng.standard_normal((N, 128, 2048), dtype=np.float32) * k).reshape(N, 8, 16, 4, 8, 16, 4)
def weights(rng, w):
    c, p = packed(np.ascontiguousarray(w).reshape(N, 128, 2048), rng)
    return {"wc": c, "ws": p}
def still(w, parts):
    for i in parts:
        w[:, :, i] = 0
        w[:, :, :, :, :, i] = 0
    return w
def lists(rng, how, label):
    o, m = np.zeros((N, 8, C), int), np.zeros((N, 8, C), int)
    i = np.arange(B)
    for r in range(N):
        for g in range(8):
            e = rng.permutation(C)
            s, t = [(e[:B], e[B:]), (i, C - 1 - i), (i, B + i), (2 * i, 2 * i + 1), (2 * i + 1, (2 * i + 2) % C), (B + i, B - 1 - i)][how[r, g]]
            j, k = [(rng.permutation(B), rng.permutation(B)), (i, i), (B - 1 - i, B - 1 - i)][label[r, g]]
            o[r, g, s] = j
            o[r, g, t] = B + k
            m[r, g, j] = B + k
            m[r, g, B + k] = j
    return {"o": np.stack([gtable(o[r]) for r in range(N)]), "m": np.stack([gtable(m[r]) for r in range(N)])}
NONE = np.zeros((N, 8), int)
def setup_inputs(rng):
    return {**numbers_of(rng), **lists(rng, NONE, NONE), **weights(rng, layers(rng))}
def setup_inputs_ties(rng):
    d = numbers_of(rng)
    x = d["x"].reshape(N, 8, 16, C, 4)
    x[:, :, 0] = 0
    x[:, :, 0, :, 0] = rng.integers(0, 3, (N, 8, C)).astype(np.float32).astype(BF)
    u = d["u"].reshape(N, 128, 128, 4)
    u[:, :, ::16] = 0
    z = rng.permutation(N)
    for r in range(N):
        for h in range(0, 128, 16): u[r, h, h, 0] = 0.0 if z[r] == 0 else -1.0 if z[r] == 1 else 1.0
    how = (rng.permutation(N)[:, None] + np.arange(8)) % 6
    return {"x": x.reshape(N, 128, 4 * C), "u": u.reshape(N, 128, 512), "v": d["v"], **lists(rng, how, NONE), **weights(rng, still(layers(rng), [0]))}
def setup_inputs_near(rng):
    d = numbers_of(rng)
    x = d["x"].astype(np.float32).reshape(N, 8, 16, C, 4)
    x[:, :, 0] = 0
    x[:, :, 8:] = 0
    u = d["u"].reshape(N, 128, 128, 4)
    u[:, :, ::16] = 0
    z = rng.permutation(N) % 4
    for r in range(N):
        s = rng.integers(0, 16, (8, C))
        c = rng.integers(0, 2, (8, C)) * 2.0 - 1.0
        k = 1.0 if z[r] == 0 else 2.0 ** -30
        if z[r] < 3:
            x[r, :, 0, :, 0] = c if z[r] < 2 else c * (rng.random((8, C)) < 0.25)
            x[r, :, 8] = ((s[:, :, None] >> np.arange(4)) & 1) * np.exp2(np.arange(4) - 23.0)
        else:
            x[r, :, 10, :, 0] = (s % 2) * 1.125 * 2.0 ** -29
            x[r, :, 12, :, 0] = (1 - s % 2) * 2.0 ** -29
        if z[r] < 2: x[r, :, 11, :, 0] = 2.0 ** -10
        for h in range(0, 128, 16):
            if z[r] < 3:
                u[r, h, h, 0] = 1.0 if z[r] == 2 else k
                u[r, h + 8, h] = k
                u[r, h + 11, h, 0] = k
            else:
                u[r, h + 10, h, 0] = 1.125 * k
                u[r, h + 12, h, 0] = 1.25 * k
    return {"x": x.reshape(N, 128, 4 * C).astype(BF), "u": u.reshape(N, 128, 512), "v": d["v"], **lists(rng, NONE, NONE), **weights(rng, still(layers(rng), [0, 8, 9, 10, 11, 12, 13, 14, 15]))}
def setup_inputs_fine(rng):
    d = numbers_of(rng)
    e = rng.integers(8, 15, (N, 8, 16, C, 4))
    e[:, :, 1] = (8 + (np.arange(N)[:, None] + np.arange(8)) % 7)[:, :, None, None]
    x = (1.125 + 0.25 * rng.integers(0, 4, (N, 8, 16, C, 4))) * np.exp2(-e.astype(np.float64))
    x[:, :, ::8, :, 0] = 1.96875
    x *= rng.integers(0, 2, x.shape) * 2.0 - 1.0
    x *= np.exp2(rng.integers(-2, 3, (N, 1, 1, C, 1)).astype(np.float64))
    u = d["u"].reshape(N, 128, 128, 4)
    u[:, :, ::16] = 0
    for h in range(0, 128, 16): u[:, h + 1, h] = 1.0
    w = layers(rng)
    w[:, :, ::8, :, :, :, 0] = 0
    return {"x": x.astype(np.float32).reshape(N, 128, 4 * C).astype(BF), "u": u.reshape(N, 128, 512), "v": d["v"], **lists(rng, NONE, NONE), **weights(rng, w)}
def setup_inputs_ends(rng):
    d = numbers_of(rng)
    z = rng.permutation(N) % 4
    how = np.stack([rng.permutation(np.array([0, 1, 2, 2, 2, 3, 4, 5])) for r in range(N)])
    l = lists(rng, how, np.repeat(1 + z[:, None] % 2, 8, axis=1))
    x = d["x"].reshape(N, 8, 16, C, 4)
    u = d["u"].reshape(N, 128, 128, 4)
    v = d["v"]
    w = layers(rng).reshape(N, 128, 2048)
    for r in range(N):
        c = (1.0 - 2.0 * (np.argsort(gentries(l["o"][r]), axis=1) % 2)) * [2.0 ** 19, -2.0 ** -29, 0.0, 0.0][z[r]]
        if z[r] < 2:
            u[r, :, ::16] = 0
            for h in range(0, 128, 16): u[r, h:h + 16, h] = [2.0 ** 30, 2.0 ** -30][z[r]]
        else:
            k = 5.0 - 2.0 * z[r]
            c = np.full((8, C), k * 2.0 ** 19)
            u[r, :, ::16] = k * 2.0 ** 30
            v[r] = k * 2.0 ** 30
            w[r] = 2.0
        if z[r] == 1: w[r] = 0
        x[r] = c[:, None, :, None].astype(np.float32).astype(BF)
    v = (np.where(v < 0, -1.0, 1.0) * np.where(rng.permutation(N) % 2, 2.0 ** -30, 2.0 ** 30)[:, None, None]).astype(np.float32).astype(BF)
    return {"x": x.reshape(N, 128, 4 * C), "u": u.reshape(N, 128, 512), "v": v, **l, **weights(rng, w)}
def setup_inputs_spread(rng):
    d = setup_inputs(rng)
    d["x"] = big(wide(rng, N, 128, 4 * C, cols=4))
    return d
def check_inputs(d):
    b = []
    for k, lo, hi in (("x", 2.0 ** -29, 2.0 ** 19), ("u", 2.0 ** -30, 2.0 ** 30), ("v", 2.0 ** -30, 2.0 ** 30)):
        a = np.abs(d[k].astype(np.float32))
        if not (np.isfinite(a).all() and ((a == 0) | (a >= lo) & (a <= hi)).all()): b.append("a value of " + k)
    none, least, most = [emit(mx_ref.quantize(np.full((128, 16), k, np.float32).astype(BF)))[1][0, 0] for k in (0.0, 2.0 ** -30, 2.0 ** 30)]
    i = np.arange(C)
    for r in range(N):
        o, m = gentries(d["o"][r]), gentries(d["m"][r])
        if (np.sort(o, axis=1) != i).any(): b.append("o: not every item once")
        if (np.sort(m, axis=1) != i).any() or (np.take_along_axis(m, m, axis=1) != i).any() or (m[:, :B] < B).any(): b.append("m: not mates of births and deaths")
        if ((d["wc"][r] == 0x7F) | (d["wc"][r] == 0xFF)).any(): b.append("wc: a code that is no number")
        s = mx_ref.live(d["ws"][r])
        if ((s != none) & ((s < least) | (s > most))).any(): b.append("ws: a scale out of range")
        elif not (np.sum(np.abs(decode(pk(d["wc"][r], d["ws"][r])).astype(np.float64)).reshape(128, 512, 4), axis=(0, 2)) <= 1024).all(): b.append("W: a column's sum of sizes")
    return b
def of(a, i):
    return np.take_along_axis(a, i, axis=2)
def reference(x, u, v, o, m, wc, ws):
    qu = [mx_ref.quantize(u[r]) for r in range(N)]
    lay = [pk(wc[r], ws[r]) for r in range(N)]
    now = [x[r] for r in range(N)]
    at = np.stack([gentries(o[r]) for r in range(N)])
    mate = np.stack([gentries(m[r]) for r in range(N)])
    for t in range(3):
        k = t % 2
        q = [mx_ref.quantize(now[r]) for r in range(N)]
        held = [decode(q[r]).astype(BF) for r in range(N)]
        s = np.stack([mx_ref.matmul(qu[r], q[r])[::16] for r in range(N)]) + np.float32(0.0)
        place = np.argsort(at, axis=2)
        lo, hi = np.minimum(place, of(place, mate)), np.maximum(place, of(place, mate))
        a, b = at[:, :, k:C - 1:2].copy(), at[:, :, k + 1::2].copy()
        turn = (of(s, a) > of(s, b)) & (of(mate, a) != b)
        nest = (of(lo, a) < of(lo, b)) & (of(hi, b) < of(hi, a)) | (of(lo, b) < of(lo, a)) & (of(hi, a) < of(hi, b))
        switch = turn & nest & ((a < B) == (b < B))
        at2 = at.copy()
        at2[:, :, k:C - 1:2] = np.where(turn, b, a)
        at2[:, :, k + 1::2] = np.where(turn, a, b)
        c = np.zeros((N, 8, C), np.int64) + np.arange(C)
        np.put_along_axis(c, a, np.where(switch, b, a), axis=2)
        np.put_along_axis(c, b, np.where(switch, a, b), axis=2)
        mate2 = of(c, of(mate, c))
        place2 = np.argsort(at2, axis=2)
        gives = of(mate2, at2)[:, :, :B]
        sent = [mx_ref.quantize(gcols(held[r], gives[r])) for r in range(N)]
        met = np.where(place2 < B, place2, B + mate2)
        for r in range(N):
            own = gcols(held[r], mate[r])
            both = np.concatenate([decode(sent[r ^ STEP[t]]).astype(BF), held[r]], axis=1)
            z = mx_ref.quantize(((own.astype(np.float32) + gcols(both, met[r]).astype(np.float32)) * np.float32(0.5)).astype(BF))
            now[r] = tile([gpick(mx_ref.matmul(pick(lay[r], np.arange(128 * i, 128 * i + 128)), z) * np.float32(0.0078125), mate2[r]) + own[:, i::4].astype(np.float32) for i in range(4)])
        at, mate = at2, mate2
    y, om = np.zeros((N, 128, C), np.float32), np.zeros((N, 8, 2 * C), np.float32)
    oc, osc = np.zeros((N, 128, 4 * C), np.uint8), np.zeros((N, 16, C), np.uint8)
    for r in range(N):
        q = mx_ref.quantize(now[r])
        y[r] = mx_ref.matmul(mx_ref.quantize(v[r]), q)
        om[r] = np.concatenate([at[r], mate[r]], axis=1)
        oc[r], osc[r] = emit(q)
    return {"y": y, "om": om, "oc": oc, "osc": osc}

@@ -1,0 +1,600 @@
+import math
+import numpy as np
+from concourse.mybir import dt, AluOpType as OP, ActivationFunctionType as AF
+
+C, B = 320, 160
+STEP = [1, 2, 4]
+EW = 176
+WD = C + EW
+NE = [160, 162, 160]
+F8, BF, F32, U16, U8, I32 = "float8_e4m3fn_x4", "bfloat16", "float32", "uint16", "uint8", "int32"
+CYCLE = 0.00104
+LW = 640
+PB = 839
+
+SCRATCH = {
+    "oi": ("sbuf", [128, 20], I32), "mi": ("sbuf", [128, 20], I32),
+    "x0": ("sbuf", [128, 4 * C], BF), "ut": ("sbuf", [128, 512], BF), "vt": ("sbuf", [128, 512], BF),
+    "wq": ("sbuf", [128, 512], F8), "wp": ("sbuf", [128, 512], U8),
+    "uq": ("sbuf", [128, 128], F8), "up": ("sbuf", [128, 128], U8),
+    "uq16": ("sbuf", [128, 128], F8), "up16": ("sbuf", [128, 128], U8),
+    "vq": ("sbuf", [128, 128], F8), "vp": ("sbuf", [128, 128], U8),
+    "ect": ("sbuf", [128, 516], BF), "ones": ("sbuf", [128, 516], BF),
+    "eq": ("sbuf", [128, 512], F8), "ep": ("sbuf", [128, 512], U8),
+    "iota": ("sbuf", [128, C], BF), "cw": ("sbuf", [128, C], BF), "bw": ("sbuf", [128, B + 8], F32),
+    "j16": ("sbuf", [128, C], BF), "mask": ("sbuf", [128, LW], BF), "hold": ("sbuf", [128, LW], BF),
+    "pcol": ("sbuf", [128, 8], I32), "pcol2": ("sbuf", [128, 8], I32), "uli": ("sbuf", [128, 8], I32), "ulu": ("sbuf", [128, 8], U16),
+    "kpat": ("sbuf", [128, 20], F32),
+    "tb": ("sbuf", [128, 3000], F32), "ub": ("sbuf", [128, 1000], U16),
+    "mrow": ("sbuf", [128, C], BF), "orow": ("sbuf", [128, C], BF), "prow": ("sbuf", [128, C], BF),
+    "wf": ("sbuf", [128, 4 * WD], BF),
+    "ah": ("sbuf", [128, 4 * C], BF), "af": ("sbuf", [128, 4 * C], BF),
+    "et": ("sbuf", [128, 4 * 192], BF), "zt": ("sbuf", [128, 4 * C], BF), "xt": ("sbuf", [128, 4 * C], BF),
+    "zq": ("sbuf", [128, C], F8), "zp": ("sbuf", [128, C], U8),
+    "xq": ("sbuf", [128, C], F8), "xp": ("sbuf", [128, C], U8),
+    "gs": ("sbuf", [128, 4 * C], F32), "sc": ("sbuf", [128, C], F32), "sb": ("sbuf", [128, B], F32),
+    "ysb": ("sbuf", [128, C], F32), "romo": ("sbuf", [128, C], F32), "romm": ("sbuf", [128, C], F32),
+}
+for _t in range(3):
+    for _n, _d in (("qe", F8), ("pe", U8), ("lq", F8), ("lp", U8)):
+        SCRATCH[_n + str(_t)] = ("sbuf", [128, EW], _d)
+    for _n, _w, _d in (("dl", 56, U16), ("tp", 352, BF), ("dr", 352, BF), ("er", 352, BF), ("bd", B, F32),
+                       ("st", 80, I32), ("sh", 80, I32), ("cur", 80, I32), ("fg", 2 * LW, BF), ("fs", 2 * LW, BF)):
+        SCRATCH[_n + str(_t)] = ("sbuf", [128, _w], _d)
+for _k in range(10):
+    SCRATCH["ra%d" % _k] = ("sbuf", [128, C], BF)
+    SCRATCH["rs%d" % _k] = ("sbuf", [128, C], BF)
+for _k in range(8):
+    SCRATCH["ps%d" % _k] = ("psum", [128, 512], F32)
+SEMAPHORES = ["vs", "ss", "ts", "gs"] + ["d%d" % k for k in range(16)] + ["arr%d" % k for k in range(3)] + ["loc%d" % k for k in range(3)]
+
+
+def rank_program(g, core, T, topo):
+    rank = T.rank_of(core)
+    if rank is None:
+        return
+    queue = {"v": g.vector, "s": g.scalar, "t": g.tensor, "g": g, "y": g.sync}
+    semof = {"v": "vs", "s": "ss", "t": "ts", "g": "gs"}
+    count = {}
+    clock = {q: {} for q in queue}
+    snap = {}
+    log = {}
+    ndma = [0]
+
+    def V(name, lo=0, hi=None, step=1):
+        return (name, lo, SCRATCH[name][1][1] if hi is None else hi, step)
+
+    def ap(v):
+        return T[v[0]][:, v[1]:v[2]:v[3]] if v[3] != 1 else T[v[0]][:, v[1]:v[2]]
+
+    def by(v):
+        return ap(v).bitcast(dt.uint8)
+
+    def ind(win, off):
+        return ap(win).indirect(ap(off))
+
+    def clash(a, b):
+        if a[1] >= b[2] or b[1] >= a[2]: return False
+        if a[3] == b[3] and a[3] > 1: return (a[1] - b[1]) % a[3] == 0
+        return True
+
+    def know(q, sem, val):
+        if clock[q].get(sem, 0) >= val: return
+        queue[q].wait_ge(T.sem[sem], val)
+        for s, n in list(snap.get((sem, val), {}).items()) + [(sem, val)]:
+            if clock[q].get(s, 0) < n: clock[q][s] = n
+
+    def order(q, reads, writes):
+        need = {}
+        for vs, isw in ((reads, False), (writes, True)):
+            for v in vs:
+                psum = v[0][:2] == "ps"
+                for (w, sem, val, oldw, oq) in log.get(v[0], ()):
+                    if (isw or oldw or (psum and oq != q)) and (psum or clash(v, w)):
+                        if need.get(sem, 0) < val: need[sem] = val
+        for sem, val in sorted(need.items(), key=lambda k: -k[1]):
+            know(q, sem, val)
+
+    def note(q, sem, val, reads, writes):
+        snap[(sem, val)] = dict(clock.get(q, {}))
+        for vs, isw in ((reads, False), (writes, True)):
+            for v in vs:
+                old = log.setdefault(v[0], [])
+                if isw:
+                    old[:] = [r for r in old if not (v[3] == 1 and v[1] <= r[0][1] and r[0][2] <= v[2])]
+                old.append((v, sem, val, isw, q))
+
+    calls = []
+
+    def put(q, issue, reads, writes, cost, late=0.0):
+        calls.append((q, issue, reads, writes, cost, late))
+
+    def run(q, fn, reads, writes, kind=""):
+        def issue():
+            order(q, reads, writes)
+            s = semof[q]
+            count[s] = count.get(s, 0) + 1
+            fn().then_inc(T.sem[s], 1)
+            note(q, s, count[s], reads, writes)
+        o = writes[0]
+        n = (o[2] - o[1] + o[3] - 1) // o[3]
+        narrow = all(SCRATCH[v[0]][2] in (BF, U16) for v in reads + writes)
+        psum = any(v[0][:2] == "ps" for v in reads)
+        if kind == "ind": c = 0.055 + 1.56 * CYCLE * n
+        elif kind == "scat": c = 3.5 * CYCLE * n
+        elif kind == "q": c = 0.015 + 4 * 0.00028 * n
+        elif q == "t": c = (n + 16) * CYCLE * 1.2
+        elif q == "g": c = 0.17 + 2 * CYCLE * n
+        elif q == "s": c = CYCLE * max(n, 64) + 0.1
+        else: c = CYCLE * max(64, n * (2 if kind == "tt" and not psum else 0.5 if narrow else 1))
+        put(q, issue, reads, writes, c)
+
+    def dma(q, pairs, reads, writes):
+        def issue():
+            order(q, reads, writes)
+            s = "d%d" % ndma[0]
+            ndma[0] += 1
+            for o, i in pairs:
+                queue[q].dma_start(o, i).then_inc(T.sem[s], 16)
+            count[s] = 16 * len(pairs)
+            note(q, s, count[s], reads, writes)
+        big = writes and SCRATCH[writes[0][0]][1][1] > 500
+        put(q, issue, reads, writes, 0.07 * len(pairs), 4.0 if big else 2.2)
+
+    def copy(out, a):
+        run("v", lambda: g.vector.tensor_copy(ap(out), ap(a)), [a], [out])
+
+    def tt(out, a, b, op):
+        run("v", lambda: g.vector.tensor_tensor(ap(out), ap(a), ap(b), op), [a, b], [out], "tt")
+
+    def ts(out, a, s1, op0, s2=None, op1=None):
+        if op1 is None:
+            run("v", lambda: g.vector.tensor_scalar(ap(out), ap(a), s1, None, op0), [a], [out])
+        else:
+            run("v", lambda: g.vector.tensor_scalar(ap(out), ap(a), s1, s2, op0, op1), [a], [out])
+
+    def tsp(out, a, col, op):
+        run("v", lambda: g.vector.tensor_scalar(ap(out), ap(a), ap(col), None, op), [a, col], [out])
+
+    def tti(out, win, off, b, op):
+        run("v", lambda: g.vector.tensor_tensor(ap(out), ind(win, off), ap(b), op), [win, off, b], [out], "ind")
+
+    def tsi(out, win, off, s1, op0):
+        run("v", lambda: g.vector.tensor_scalar(ap(out), ind(win, off), s1, None, op0), [win, off], [out], "ind")
+
+    def fill(out, c):
+        run("v", lambda: g.vector.memset(ap(out), c), [], [out])
+
+    def act(out, a, scale=1.0):
+        run("s", lambda: g.scalar.activation(ap(out), ap(a), AF.Copy, scale=scale), [a], [out])
+
+    def acti(out, win, off, scale=1.0):
+        run("s", lambda: g.scalar.activation(ap(out), ind(win, off), AF.Copy, scale=scale), [win, off], [out], "ind")
+
+    def actb(out, win, off, bias):
+        run("s", lambda: g.scalar.activation(ap(out), ind(win, off), AF.Identity, bias=bias), [win, off], [out], "ind")
+
+    def quant(q, p, a):
+        run("v", lambda: g.vector.quantize_mx(ap(q), ap(p), ap(a)), [a], [q, p], "q")
+
+    def mm(out, l, lp, r, rp):
+        run("t", lambda: g.tensor.matmul_mx(ap(out), ap(l), ap(lp), ap(r), ap(rp), True, True), [l, lp, r, rp], [out])
+
+    def iota(out, pattern, base, cm):
+        run("g", lambda: g.iota(ap(out), pattern, base, cm, allow_small_or_imprecise_dtypes=True), [], [out])
+
+    ntb, nub, nrow = [0], [0], [0]
+
+    def tmp(n):
+        ntb[0] += n
+        return V("tb", ntb[0] - n, ntb[0])
+
+    def lst(n):
+        nub[0] += n + n % 2
+        return V("ub", nub[0] - n - n % 2, nub[0] - n % 2)
+
+    def sub(v, lo, hi, step=1):
+        if v[3] == 1: return (v[0], v[1] + lo, v[1] + hi, step)
+        return (v[0], v[1] + lo * v[3], min(v[2], v[1] + (hi - 1) * v[3] + 1), v[3] * step)
+
+    def tab(v, lo, hi):
+        return (v[0], v[1] + 16 * lo + 15, v[1] + 16 * hi, 16)
+
+    def scan(out, data):
+        h = V("hold", 0, data[2] - data[1])
+        run("v", lambda: g.vector.tensor_tensor_scan(ap(out), ap(h), ap(data), 0.0, OP.mult, OP.add), [h, data], [out])
+
+    def lookup(raw, out, win, off):
+        tti(raw, win, off, V("mask", 0, raw[2] - raw[1]), OP.mult)
+        scan(out, raw)
+
+    def look20(win, off):
+        k = nrow[0]
+        nrow[0] += 1
+        lookup(V("ra%d" % k), V("rs%d" % k), win, off)
+        return tab(V("rs%d" % k), 0, 20)
+
+    def win0(name):
+        return V(name, 16, 16 + C)
+
+    def first_of(name, k):
+        return V(name, 16 - k, 16 - k + C - 1, 2)
+
+    def second_of(name, k):
+        return V(name, 17 - k, 17 - k + C - 1, 2)
+
+    def wf(b):
+        return V("wf", b * WD, (b + 1) * WD)
+
+    def wfF(b):
+        return V("wf", b * WD, b * WD + C)
+
+    def el(b):
+        return (b, 4 * C - 3 + b, 4)
+
+    def cols(name, b, n=128):
+        return V(name, n * b, n * b + n)
+
+    dma("y", [(T.oi[:], T.o[:]), (T.mi[:], T.m[:])], [], [V("oi"), V("mi")])
+    dma("s", [(T.x0[:], T.x[:])], [], [V("x0")])
+    dma("y", [(T.ut[:], T.u[:])], [], [V("ut")])
+    dma("y", [(by(V("wq")), T.wc[:]), (T.wp[:], T.ws[:])], [], [V("wq"), V("wp")])
+    dma("y", [(T.vt[:], T.v[:])], [], [V("vt")])
+
+    iota(V("pcol"), [[0, 8]], 0, 1)
+    iota(V("kpat"), [[32, 10], [1, 2]], 0, 0)
+    iota(V("j16"), [[0, C // 16], [1, 16]], 0, 0)
+    iota(V("iota"), [[1, C]], -B, 0)
+    iota(V("uli"), [[16, 8]], 0, 0)
+    fill(V("ones"), 1.0)
+    run("g", lambda: g.affine_select(T.ect[:], T.ones[:], [[1, 516]], OP.is_equal, 0.0, -3, -4), [V("ones")], [V("ect")])
+    iota(V("cw"), [[1024, C]], -1024 * B, 0)
+    pm, pm2 = tmp(1), tmp(1)
+    ts(V("pcol2"), V("pcol"), 15, OP.bitwise_and)
+    copy(pm, V("pcol2", 0, 1))
+    ts(pm2, pm, 2.0, OP.mult)
+    K = [tmp(20), tmp(20)]
+    tsp(K[0], V("kpat"), pm2, OP.add)
+    ts(K[1], K[0], -1.0, OP.add)
+    ku0, first = lst(20), tmp(10)
+    copy(ku0, K[0])
+    ts(first, sub(K[1], 0, 20, 2), 0.0, OP.is_lt)
+    last, K2 = tmp(20), tmp(20)
+    ts(last, K[1], 0.0, OP.is_lt, float(C), OP.mult)
+    tt(K2, K[1], last, OP.add)
+    for t in range(3):
+        kA = sub(K[t % 2], 0, 20, 2)
+        ts(V("dl%d" % t, 0, 6), sub(kA, 0, 6), 0.0, OP.max)
+        ts(V("dl%d" % t, 26, 36), kA, 0.0, OP.max)
+    tsp(V("mask", 0, C), V("j16"), pm, OP.is_equal)
+    run("s", lambda: g.scalar.activation(ap(V("hold", 0, C)), T.j16[:], AF.Sign), [V("j16")], [V("hold", 0, C)])
+    act(V("mask", C, LW), V("mask", 0, C))
+    act(V("hold", C, LW), V("hold", 0, C))
+    for v, z in ((V("bw", 0, B + 1), -1e29), (V("bw", B + 1, B + 8), 1e29)):
+        run("s", lambda v=v, z=z: g.scalar.activation(ap(v), ap(V("j16", 0, v[2] - v[1])), AF.Identity, bias=z, scale=0.0), [V("j16")], [v])
+    for v in [V("tp1", 328, 352), V("dr1", 328, 352)] + [V("wf", b * WD + C, (b + 1) * WD) for b in range(4)]:
+        act(v, V("j16", 0, v[2] - v[1]), 0.0)
+    onat, mu = lst(20), [lst(20) for k in range(4)]
+    copy(onat, V("oi"))
+    copy(mu[0], V("mi"))
+
+    acti(V("orow"), V("iota"), onat)
+    acti(V("mrow"), V("iota"), mu[0])
+    run("v", lambda: g.vector.tensor_copy(ind(V("prow"), onat), ap(V("iota"))), [V("iota"), onat], [V("prow")], "scat")
+    ot = look20(V("orow"), ku0)
+    ou = lst(20)
+    ts(ou, ot, float(B), OP.add)
+    ts(V("cur0", 0, 20), ot, float(B), OP.add)
+    for b in range(4):
+        quant(cols("eq", b), cols("ep", b), V("ect", 3 - b, 515 - b))
+    quant(V("xq"), V("xp"), V("x0"))
+    xt0 = look20(V("mrow"), ou)
+    xu = lst(20)
+    ts(xu, xt0, float(B), OP.add)
+    quant(V("uq"), V("up"), V("ut"))
+    copy(V("ulu"), V("uli"))
+    run("s", lambda: g.scalar.activation(T.up16[:], T.up[:].indirect(T.ulu[:]), AF.Copy), [V("up"), V("ulu")], [V("up16")], "ind")
+    run("v", lambda: g.vector.tensor_copy(T.uq16[:].bitcast(dt.uint32), T.uq[:].bitcast(dt.uint32).indirect(T.ulu[:])), [V("uq"), V("ulu")], [V("uq16")], "ind")
+    Mt0 = look20(V("prow"), xu)
+    M0, x1 = tmp(20), tmp(20)
+    ts(M0, Mt0, float(B), OP.add)
+
+    def sides(y, M, o, k):
+        d, b2 = tmp(20), tmp(20)
+        tt(d, M, (K[0], K2)[k], OP.is_gt)
+        ts(b2, o, float(B), OP.is_lt, 2.0, OP.mult)
+        tt(y, d, b2, OP.add)
+
+    def static(t, M):
+        k = t % 2
+        cur = V("cur%d" % t)
+        o = sub(cur, 0, 20)
+        oA, oB = sub(cur, 0, 20, 2), sub(cur, 1, 20, 2)
+        y = sub(cur, 40, 60)
+        if M is None: M = sub(cur, 60, 80)
+        else: sides(y, M, o, 0)
+        MA, MB = sub(M, 0, 20, 2), sub(M, 1, 20, 2)
+        eq, gt, S, do, bi, biu = tmp(10), tmp(10), tmp(10), tmp(10), tmp(20), lst(20)
+        ix, ixu = sub(bi, 10, 20), sub(biu, 10, 20)
+        if k:
+            bl = tmp(10)
+            tt(bl, MA, sub(K[k], 1, 20, 2), OP.is_equal)
+            tt(sub(bi, 0, 10), bl, first, OP.max)
+        else:
+            tt(sub(bi, 0, 10), MA, sub(K[k], 1, 20, 2), OP.is_equal)
+        tt(eq, sub(y, 0, 20, 2), sub(y, 1, 20, 2), OP.is_equal)
+        tt(gt, MA, MB, OP.is_gt)
+        tt(S, eq, gt, OP.mult)
+        tt(do, oB, oA, OP.subtract)
+        tt(ix, do, S, OP.mult)
+        ts(biu, bi, float(B), OP.add)
+        acti(V("bd%d" % t), V("bw"), sub(biu, 0, 10))
+        acti(first_of("dr%d" % t, k), V("cw"), ixu)
+        acti(second_of("dr%d" % t, k), V("cw"), ixu)
+        return dict(t=t, do=do, S=S, M=M, oA=oA, oB=oB)
+
+    def static2(r):
+        copy(V("dl%d" % r["t"], 6, 26), r["M"])
+        r["oAu"], r["oBu"] = lst(10), lst(10)
+        copy(r["oBu"], r["oB"])
+        copy(r["oAu"], r["oA"])
+        r["D"] = look20(win0("dr%d" % r["t"]), V("dl%d" % r["t"], 6, 26))
+
+    def products(t):
+        mm(V("ps4", 0, C), V("uq16"), V("up16"), V("xq"), V("xp"))
+        for b in range(4):
+            mm(V("ps%d" % b, 0, C), cols("eq", b), cols("ep", b), V("xq"), V("xp"))
+        act(V("sc"), V("ps4", 0, C))
+        for b in range(4):
+            act(wfF(b), V("ps%d" % b, 0, C), 0.5)
+
+    fill(V("cw", B, B + 1), 1.0)
+    r = static(0, M0)
+    ts(x1, xt0, 1024.0, OP.mult, 1024.0 * B, OP.add)
+    tt(V("cur0", 20, 40), x1, M0, OP.add)
+    products(0)
+    static2(r)
+    P = None
+    for t in range(3):
+        k = t % 2
+        nl = 5 + k
+        nu = 10 - nl
+        dl, tp, er = "dl%d" % t, "tp%d" % t, "er%d" % t
+        cur, st = V("cur%d" % t), V("st%d" % t)
+        val = sub(cur, 20, 40)
+        D, S, do = r["D"], r["S"], r["do"]
+        tti(V("sb"), V("sc"), r["oBu"], V("bd%d" % t), OP.max)
+        tti(first_of(tp, k), V("sc"), r["oAu"], V("sb"), OP.is_gt)
+        ts(second_of(tp, k), first_of(tp, k), -1.0, OP.mult)
+        fg, fs = "fg%d" % t, "fs%d" % t
+        eu = lst(20)
+
+        def renew(tc, tM, c0, c1):
+            n = c1 - c0
+            d1, alt, rr, dd, d2 = tmp(2 * n), tmp(2 * n), tmp(n), tmp(n), tmp(n)
+            tt(d1, tM, sub(D, 2 * c0, 2 * c1), OP.mult)
+            tt(rr, tc, sub(S, c0, c1), OP.is_gt)
+            tt(alt, d1, sub(val, 2 * c0, 2 * c1), OP.add)
+            aA, aB = sub(alt, 0, 2 * n, 2), sub(alt, 1, 2 * n, 2)
+            tt(dd, aB, aA, OP.subtract)
+            tt(d2, dd, rr, OP.mult)
+            eA, eB = sub(st, 20 + 2 * c0, 20 + 2 * c1, 2), sub(st, 21 + 2 * c0, 20 + 2 * c1, 2)
+            tt(eA, aA, d2, OP.add)
+            tt(eB, aB, d2, OP.subtract)
+            ts(sub(eu, c0, c1), eA, 1.0 / 1024, OP.mult)
+            ts(sub(eu, 10 + c0, 10 + c1), eB, 1.0 / 1024, OP.mult)
+
+        wl = 16 * (6 + 2 * nl)
+        fl = V(fs, 0, wl)
+        lookup(V(fg, 0, wl), fl, win0(tp), V(dl, 0, 6 + 2 * nl))
+        renew(tab(fl, 0, nl), tab(fl, 6, 6 + 2 * nl), 0, nl)
+        for b in range(4):
+            acti(V("et", b, 128 * nl - 7 + b, 8), wfF(b), sub(eu, 0, nl), 2.0)
+            tsi(V("et", 4 + b, 128 * nl - 3 + b, 8), wfF(b), sub(eu, 10, 10 + nl), 2.0, OP.mult)
+        ne = NE[t]
+        qe, pe, lq, lp = [V(s + str(t), 0, ne) for s in ("qe", "pe", "lq", "lp")]
+        quant(qe, pe, V("et", 0, 4 * ne))
+        dst = T.cores[rank ^ STEP[t]]
+        rid, pid = topo.addr(dst)[:2]
+        arr, loc, full = "arr%d" % t, "loc%d" % t, 2 * len(topo.engines(core, dst))
+
+        def send(qe=qe, pe=pe, lq=lq, lp=lp, pid=pid, rid=rid, arr=arr, loc=loc, full=full, mask=topo.mask(core, dst)):
+            order("g", [qe, pe], [])
+            g.remote_dma(by(lq), by(qe), T.sem[arr], T.sem[loc], pid, rid, mask)
+            g.remote_dma(ap(lp), ap(pe), T.sem[arr], T.sem[loc], pid, rid, mask)
+            count[arr] = count[loc] = full
+            note("g", loc, full, [qe, pe], [])
+            log[lq[0]] = [(lq, arr, full, True, "r")]
+            log[lp[0]] = [(lp, arr, full, True, "r")]
+
+        put("g", send, [qe, pe], [lq, lp], 1.0, 2.2)
+        for b in range(4):
+            acti(cols("ah", b, C), wfF(b), mu[t])
+        if t == 0:
+            tt(V("ra8"), V("prow"), V("mask", 0, C), OP.mult)
+            scan(V("rs8"), V("ra8"))
+            p0 = tab(V("rs8"), 0, 20)
+            ts(V("dl0", 36, 56), p0, float(B), OP.add)
+            P = tmp(20)
+            ts(P, p0, float(B - PB), OP.add)
+        wu, lu = 16 * (2 * nu + 10), 6 + 2 * nl
+        fv = V(fs, LW - C, LW - C + wu)
+        lookup(V(fg, LW - C, LW - C + wu), fv, win0(tp), V(dl, lu, lu + 2 * nu + 10))
+        tc = tab(fv, 2 * nu, 2 * nu + 10)
+        renew(sub(tc, nl, 10), tab(fv, 0, 2 * nu), nl, 10)
+        fu = V(fs, LW, LW + C)
+        lookup(V(fg, LW, LW + C), fu, win0(tp), V(dl, 36, 56))
+        acti(first_of(er, k), V("iota"), sub(eu, 0, 10))
+        acti(second_of(er, k), V("iota"), sub(eu, 10, 20))
+        if k: act(V(er, 16 + C - 1, 16 + C), V(er, 15, 16))
+        pn, pf, pz, pu = tmp(20), tmp(20), tmp(20), lst(20) if t == 2 else V("dl%d" % (t + 1), 36, 56)
+        tt(pn, P, tab(fu, 0, 20), OP.add)
+        P = pn
+        ts(pu, pn, float(PB), OP.add)
+        t1 = tmp(10)
+        tt(t1, tc, do, OP.mult)
+        tt(sub(st, 0, 20, 2), sub(cur, 0, 20, 2), t1, OP.add)
+        tt(sub(st, 1, 20, 2), sub(cur, 1, 20, 2), t1, OP.subtract)
+        ts(pf, pn, float(B - PB), OP.is_lt, 1000.0, OP.mult)
+        tt(pz, pf, pn, OP.add)
+        if t == 2:
+            ofu = lst(20)
+            copy(sub(ofu, 0, 10), sub(st, 0, 20, 2))
+            copy(sub(ofu, 10, 20), sub(st, 1, 20, 2))
+        mn = look20(win0(er), pu)
+        vm, vl = tmp(20), lst(20)
+        tt(vm, pz, mn, OP.max)
+        ts(vl, vm, float(B), OP.add)
+        if t < 2:
+            ts(sub(st, 60, 80), sub(st, 20, 40), 1023, OP.bitwise_and)
+            sides(sub(st, 40, 60), sub(st, 60, 80), sub(st, 0, 20), k)
+            s, h = T["st%d" % t], T["sh%d" % t]
+            pairs = []
+            if t == 0:
+                for q in range(0, 128, 16):
+                    pairs.append((h[q + 1:q + 16, :], s[q:q + 15, :]))
+                for z in (0, 20, 40, 60):
+                    pairs.append((h[0:128:16, z + 2:z + 20], s[15:128:16, z:z + 18]))
+                    pairs.append((h[0:128:16, z:z + 2], s[15:128:16, z + 18:z + 20]))
+            else:
+                for q in range(0, 128, 16):
+                    pairs.append((h[q:q + 15, :], s[q + 1:q + 16, :]))
+                for z in (0, 20, 40, 60):
+                    pairs.append((h[15:128:16, z:z + 18], s[0:128:16, z + 2:z + 20]))
+                    pairs.append((h[15:128:16, z + 18:z + 20], s[0:128:16, z:z + 2]))
+            dma("y", pairs, [st], [V("sh%d" % t)])
+        for b in range(4):
+            mm(V("ps%d" % b, 0, ne), cols("eq", b), cols("ep", b), lq, lp)
+            act(V("wf", b * WD + C + 1 - k, b * WD + C + 1 - k + ne), V("ps%d" % b, 0, ne), 0.5)
+        for b in range(4):
+            tti(V("zt", *el(b)), wf(b), vl, cols("ah", b, C), OP.add)
+        act(V("af"), V("ah"), 2.0)
+        quant(V("zq"), V("zp"), V("zt"))
+        ts(mu[t + 1], mn, float(B), OP.add)
+        if t == 2:
+            actb(V("romo", 0, C - 1, 2), V("iota"), sub(ofu, 0, 10), float(B))
+            actb(V("romo", 1, C, 2), V("iota"), sub(ofu, 10, 20), float(B))
+        for b in range(4):
+            mm(V("ps%d" % (4 + b), 0, C), cols("wq", b), cols("wp", b), V("zq"), V("zp"))
+            act(cols("gs", b, C), V("ps%d" % (4 + b), 0, C), 0.0078125)
+        if t < 2:
+            n, h = "cur%d" % (t + 1), "sh%d" % t
+            if t == 0:
+                copy(V(n, 0, 79, 2), V(h, 1, 80, 2))
+                copy(V(n, 1, 80, 2), V("st0", 0, 79, 2))
+            else:
+                copy(V(n, 0, 79, 2), V("st1", 1, 80, 2))
+                copy(V(n, 1, 80, 2), V(h, 0, 79, 2))
+            r = static(t + 1, None)
+        else:
+            quant(V("vq"), V("vp"), V("vt"))
+        for b in range(4):
+            tti(V("xt", *el(b)), cols("gs", b, C), mu[t + 1], cols("af", b, C), OP.add)
+        quant(V("xq"), V("xp"), V("xt"))
+        if t < 2:
+            products(t + 1)
+            static2(r)
+    for z in range(2):
+        mm(V("ps%d" % (4 + z), 0, B), V("vq"), V("vp"), V("xq", B * z, B * z + B), V("xp", B * z, B * z + B))
+    dma("y", [(T.oc[:], by(V("xq")))] + [(T.osc[4 * q:4 * q + 4, :], T.xp[32 * q:32 * q + 4, :]) for q in range(4)], [V("xq"), V("xp")], [])
+    act(V("ysb", 0, B), V("ps4", 0, B))
+    copy(V("ysb", B, C), V("ps5", 0, B))
+    dma("s", [(T.y[:, 0:B], T.ysb[:, 0:B])], [V("ysb", 0, B)], [])
+    dma("s", [(T.y[:, B:C], T.ysb[:, B:C])], [V("ysb", B, C)], [])
+    actb(V("romm"), V("iota"), mu[3], float(B))
+    dma("y", [(T.om[:, 0:C], T.romo[0:128:16, :]), (T.om[:, C:2 * C], T.romm[0:128:16, :])], [V("romo"), V("romm")], [])
+    if "plan" not in PLAN:
+        seen, before = {}, []
+        for i, (q, issue, reads, writes, cost, late) in enumerate(calls):
+            p = set()
+            for vs, isw in ((reads, False), (writes, True)):
+                for v in vs:
+                    psum = v[0][:2] == "ps"
+                    for w, j, oldw in seen.get(v[0], ()):
+                        if (isw or oldw or (psum and calls[j][0] != q)) and (psum or clash(v, w)): p.add(j)
+            for vs, isw in ((reads, False), (writes, True)):
+                for v in vs: seen.setdefault(v[0], []).append((v, i, isw))
+            before.append(sorted(p))
+        PLAN["plan"] = plan([(c[0], c[4], c[5]) for c in calls], before)
+    for i in PLAN["plan"]:
+        calls[i][1]()
+    for sem, n in count.items():
+        know("g", sem, n)
+
+
+PLAN = {}
+MACHINES = [(1.0, 0.06, 0.0, 0.0), (1.1, 0.1, 0.06, 0.5), (1.2, 0.15, 0.1, 1.0), (0.9, 0.08, 0.05, 2.0)]
+TRIES = 170000
+
+
+def walk(ops, before, seqs, m):
+    fac, wake, own, more = m
+    end, at, free = {}, {q: 0 for q in seqs}, {q: 0.0 for q in seqs}
+    begun = {}
+    left = len(ops)
+    while left:
+        moved = False
+        for q, seq in seqs.items():
+            while at[q] < len(seq):
+                i = seq[at[q]]
+                t, late = free[q], False
+                ok = True
+                for j in before[i]:
+                    if j not in end:
+                        ok = False
+                        break
+                if not ok: break
+                for j in before[i]:
+                    e = end[j] + (own if ops[j][0] == q and end[j] >= free[q] - 1e-9 else wake if ops[j][0] != q and end[j] > free[q] else 0.0)
+                    if e > t: t = e
+                begun[i] = t
+                free[q] = t + ops[i][1] * (fac if q in "vs" else 1.0)
+                end[i] = free[q] + (ops[i][2] + more if ops[i][2] else 0.0)
+                at[q] += 1
+                left -= 1
+                moved = True
+        if not moved: return 1e9, begun
+    return max(end.values()), begun
+
+
+def plan(ops, before):
+    n = len(ops)
+    known, need = [0] * n, []
+    for i in range(n):
+        keep, a = [], 0
+        for j in sorted(before[i], reverse=True):
+            if not (a >> j) & 1:
+                keep.append(j)
+                a |= known[j] | (1 << j)
+        known[i] = a
+        need.append(keep)
+    seqs = {q: [i for i in range(n) if ops[i][0] == q] for q in "vstgy"}
+    base = [walk(ops, need, seqs, m)[0] for m in MACHINES]
+    now, rng = 1.0, np.random.RandomState(4)
+    best = (now, seqs)
+    for turn in range(TRIES):
+        q = "vvvs"[rng.randint(4)]
+        row = list(seqs[q])
+        a, k = int(rng.randint(len(row))), 1 if rng.rand() < 0.6 else int(rng.randint(1, 8))
+        b = a + int(rng.randint(1, 40)) * (1 if rng.rand() < 0.5 else -1)
+        lim = now - 0.0006 * max(0.0, 1.0 - 1.2 * turn / TRIES) * math.log(rng.rand() + 1e-12)
+        run = row[a:a + k]
+        del row[a:a + k]
+        b = max(0, min(len(row), b))
+        mid = row[min(a, b):max(a, b)]
+        if b > a and any([j in run for i in mid for j in need[i]]): continue
+        if b < a and any([j in mid for i in run for j in need[i]]): continue
+        row[b:b] = run
+        new = dict(seqs)
+        new[q] = row
+        total = 0.0
+        for m, w in zip(MACHINES, base):
+            r = walk(ops, need, new, m)[0] / w
+            total += r / len(MACHINES)
+            if r > lim + 0.03: total += 9.0
+            if total > lim: break
+        if total <= lim:
+            now, seqs = total, new
+            if now < best[0]: best = (now, seqs)
+    begun = walk(ops, need, best[1], MACHINES[1])[1]
+    return [i for t, i in sorted([(begun[i], i) for i in range(n)])]

@@ -9,8 +9,8 @@ WD = C + EW
 NE = [160, 162, 160]
 F8, BF, F32, U16, U8, I32 = "float8_e4m3fn_x4", "bfloat16", "float32", "uint16", "uint8", "int32"
 CYCLE = 0.00104
-LW = 640
 PB = 839
+BIG = 2.0 ** 64
 
 SCRATCH = {
     "oi": ("sbuf", [128, 20], I32), "mi": ("sbuf", [128, 20], I32),
@@ -21,12 +21,13 @@ SCRATCH = {
     "vq": ("sbuf", [128, 128], F8), "vp": ("sbuf", [128, 128], U8),
     "ect": ("sbuf", [128, 516], BF), "ones": ("sbuf", [128, 516], BF),
     "eq": ("sbuf", [128, 512], F8), "ep": ("sbuf", [128, 512], U8),
-    "iota": ("sbuf", [128, C], BF), "cw": ("sbuf", [128, C], BF), "bw": ("sbuf", [128, B + 8], F32),
-    "j16": ("sbuf", [128, C], BF), "mask": ("sbuf", [128, LW], BF), "hold": ("sbuf", [128, LW], BF),
+    "iota": ("sbuf", [128, C], BF), "cw": ("sbuf", [128, C], BF),
+    "j16": ("sbuf", [128, 16], F32), "k16": ("sbuf", [128, 16], BF), "kk": ("sbuf", [128, C], BF),
     "pcol": ("sbuf", [128, 8], I32), "pcol2": ("sbuf", [128, 8], I32), "uli": ("sbuf", [128, 8], I32), "ulu": ("sbuf", [128, 8], U16),
     "kpat": ("sbuf", [128, 20], F32),
     "tb": ("sbuf", [128, 3000], F32), "ub": ("sbuf", [128, 1000], U16),
     "mrow": ("sbuf", [128, C], BF), "orow": ("sbuf", [128, C], BF), "prow": ("sbuf", [128, C], BF),
+    "pmrow": ("sbuf", [128, C], BF), "xrow": ("sbuf", [128, C], BF), "Mrow": ("sbuf", [128, C], BF),
     "wf": ("sbuf", [128, 4 * WD], BF),
     "ah": ("sbuf", [128, 4 * C], BF), "af": ("sbuf", [128, 4 * C], BF),
     "et": ("sbuf", [128, 4 * 192], BF), "zt": ("sbuf", [128, 4 * C], BF), "xt": ("sbuf", [128, 4 * C], BF),
@@ -38,15 +39,14 @@ SCRATCH = {
 for _t in range(3):
     for _n, _d in (("qe", F8), ("pe", U8), ("lq", F8), ("lp", U8)):
         SCRATCH[_n + str(_t)] = ("sbuf", [128, EW], _d)
-    for _n, _w, _d in (("dl", 56, U16), ("tp", 352, BF), ("dr", 352, BF), ("er", 352, BF), ("bd", B, F32),
-                       ("st", 80, I32), ("sh", 80, I32), ("cur", 80, I32), ("fg", 2 * LW, BF), ("fs", 2 * LW, BF)):
+    for _n, _w, _d in (("tp", 352, BF), ("dr", 352, BF), ("er", 352, BF), ("dm", C, BF), ("cur", 80, I32), ("go", 24, I32)):
         SCRATCH[_n + str(_t)] = ("sbuf", [128, _w], _d)
-for _k in range(10):
-    SCRATCH["ra%d" % _k] = ("sbuf", [128, C], BF)
-    SCRATCH["rs%d" % _k] = ("sbuf", [128, C], BF)
+for _k in range(26):
+    SCRATCH["r%d" % _k] = ("sbuf", [128, C], BF)
 for _k in range(8):
     SCRATCH["ps%d" % _k] = ("psum", [128, 512], F32)
-SEMAPHORES = ["vs", "ss", "ts", "gs"] + ["d%d" % k for k in range(16)] + ["arr%d" % k for k in range(3)] + ["loc%d" % k for k in range(3)]
+SEMAPHORES = ["vs", "ss", "ts", "gs"] + ["d%d" % k for k in range(24)] + ["arr%d" % k for k in range(3)] + ["loc%d" % k for k in range(3)]
+ON = {"sb": "v", "p": "s", "mn": "s", "dm": "s", "af0": "v", "af1": "v", "pm0": "v", "pm1": "s", "M0": "v", "M1": "s", "dr1": "s"}
 
 
 def rank_program(g, core, T, topo):
@@ -120,16 +120,16 @@ def rank_program(g, core, T, topo):
         n = (o[2] - o[1] + o[3] - 1) // o[3]
         narrow = all(SCRATCH[v[0]][2] in (BF, U16) for v in reads + writes)
         psum = any(v[0][:2] == "ps" for v in reads)
-        if kind == "ind": c = 0.055 + 1.56 * CYCLE * n
-        elif kind == "scat": c = 3.5 * CYCLE * n
+        if kind == "ind": c = 0.06 + 1.56 * CYCLE * n
+        elif kind == "scat": c = 3.8 * CYCLE * n
         elif kind == "q": c = 0.015 + 4 * 0.00028 * n
-        elif q == "t": c = (n + 16) * CYCLE * 1.2
-        elif q == "g": c = 0.17 + 2 * CYCLE * n
-        elif q == "s": c = CYCLE * max(n, 64) + 0.1
+        elif q == "t": c = (n + 16) * CYCLE
+        elif q == "g": c = 0.2 + 2 * CYCLE * n
+        elif q == "s": c = CYCLE * max(n, 64) + 0.08
         else: c = CYCLE * max(64, n * (2 if kind == "tt" and not psum else 0.5 if narrow else 1))
         put(q, issue, reads, writes, c)
 
-    def dma(q, pairs, reads, writes):
+    def dma(q, pairs, reads, writes, late=2.2):
         def issue():
             order(q, reads, writes)
             s = "d%d" % ndma[0]
@@ -138,8 +138,7 @@ def rank_program(g, core, T, topo):
                 queue[q].dma_start(o, i).then_inc(T.sem[s], 16)
             count[s] = 16 * len(pairs)
             note(q, s, count[s], reads, writes)
-        big = writes and SCRATCH[writes[0][0]][1][1] > 500
-        put(q, issue, reads, writes, 0.07 * len(pairs), 4.0 if big else 2.2)
+        put(q, issue, reads, writes, 0.07 * len(pairs), late)
 
     def copy(out, a):
         run("v", lambda: g.vector.tensor_copy(ap(out), ap(a)), [a], [out])
@@ -148,28 +147,31 @@ def rank_program(g, core, T, topo):
         run("v", lambda: g.vector.tensor_tensor(ap(out), ap(a), ap(b), op), [a, b], [out], "tt")
 
     def ts(out, a, s1, op0, s2=None, op1=None):
+        more = [s for s in (s1, s2) if isinstance(s, tuple)]
+        s1, s2 = [ap(s) if isinstance(s, tuple) else s for s in (s1, s2)]
         if op1 is None:
-            run("v", lambda: g.vector.tensor_scalar(ap(out), ap(a), s1, None, op0), [a], [out])
+            run("v", lambda: g.vector.tensor_scalar(ap(out), ap(a), s1, None, op0), [a] + more, [out])
         else:
-            run("v", lambda: g.vector.tensor_scalar(ap(out), ap(a), s1, s2, op0, op1), [a], [out])
-
-    def tsp(out, a, col, op):
-        run("v", lambda: g.vector.tensor_scalar(ap(out), ap(a), ap(col), None, op), [a, col], [out])
+            run("v", lambda: g.vector.tensor_scalar(ap(out), ap(a), s1, s2, op0, op1), [a] + more, [out])
 
     def tti(out, win, off, b, op):
         run("v", lambda: g.vector.tensor_tensor(ap(out), ind(win, off), ap(b), op), [win, off, b], [out], "ind")
 
-    def tsi(out, win, off, s1, op0):
-        run("v", lambda: g.vector.tensor_scalar(ap(out), ind(win, off), s1, None, op0), [win, off], [out], "ind")
-
     def fill(out, c):
         run("v", lambda: g.vector.memset(ap(out), c), [], [out])
 
-    def act(out, a, scale=1.0):
-        run("s", lambda: g.scalar.activation(ap(out), ap(a), AF.Copy, scale=scale), [a], [out])
+    def act(out, a, scale=1.0, bias=None):
+        if bias is None: run("s", lambda: g.scalar.activation(ap(out), ap(a), AF.Copy, scale=scale), [a], [out])
+        else: run("s", lambda: g.scalar.activation(ap(out), ap(a), AF.Identity, bias=bias, scale=scale), [a], [out])
 
-    def acti(out, win, off, scale=1.0):
-        run("s", lambda: g.scalar.activation(ap(out), ind(win, off), AF.Copy, scale=scale), [win, off], [out], "ind")
+    def scaled(q, out, a, scale):
+        if q == "s": act(out, a, scale)
+        else: ts(out, a, scale, OP.mult)
+
+    def pick(q, out, win, off, scale=1.0):
+        if q == "s": run("s", lambda: g.scalar.activation(ap(out), ind(win, off), AF.Copy, scale=scale), [win, off], [out], "ind")
+        elif scale == 1.0: run("v", lambda: g.vector.tensor_copy(ap(out), ind(win, off)), [win, off], [out], "ind")
+        else: run("v", lambda: g.vector.tensor_scalar(ap(out), ind(win, off), scale, None, OP.mult), [win, off], [out], "ind")
 
     def actb(out, win, off, bias):
         run("s", lambda: g.scalar.activation(ap(out), ind(win, off), AF.Identity, bias=bias), [win, off], [out], "ind")
@@ -193,204 +195,209 @@ def rank_program(g, core, T, topo):
         nub[0] += n + n % 2
         return V("ub", nub[0] - n - n % 2, nub[0] - n % 2)
 
+    def row(n=C):
+        nrow[0] += 1
+        return V("r%d" % (nrow[0] - 1), 0, n)
+
     def sub(v, lo, hi, step=1):
         if v[3] == 1: return (v[0], v[1] + lo, v[1] + hi, step)
         return (v[0], v[1] + lo * v[3], min(v[2], v[1] + (hi - 1) * v[3] + 1), v[3] * step)
 
-    def tab(v, lo, hi):
-        return (v[0], v[1] + 16 * lo + 15, v[1] + 16 * hi, 16)
+    def tab(v):
+        return (v[0], v[1] + 15, v[2], 16)
 
     def scan(out, data):
-        h = V("hold", 0, data[2] - data[1])
+        h = V("kk", 0, out[2] - out[1])
         run("v", lambda: g.vector.tensor_tensor_scan(ap(out), ap(h), ap(data), 0.0, OP.mult, OP.add), [h, data], [out])
 
-    def lookup(raw, out, win, off):
-        tti(raw, win, off, V("mask", 0, raw[2] - raw[1]), OP.mult)
-        scan(out, raw)
-
-    def look20(win, off):
-        k = nrow[0]
-        nrow[0] += 1
-        lookup(V("ra%d" % k), V("rs%d" % k), win, off)
-        return tab(V("rs%d" % k), 0, 20)
+    def table(data, n=C):
+        out = row(n)
+        scan(out, data)
+        return tab(out)
 
     def win0(name):
         return V(name, 16, 16 + C)
 
-    def first_of(name, k):
-        return V(name, 16 - k, 16 - k + C - 1, 2)
-
-    def second_of(name, k):
-        return V(name, 17 - k, 17 - k + C - 1, 2)
+    def place(name, k, e):
+        return V(name, 16 + e - k, 16 + e - k + C - 1, 2)
 
     def wf(b):
         return V("wf", b * WD, (b + 1) * WD)
 
-    def wfF(b):
-        return V("wf", b * WD, b * WD + C)
+    def wfF(b, h=None):
+        return V("wf", b * WD, b * WD + C) if h is None else V("wf", b * WD + B * h, b * WD + B * h + B)
 
-    def el(b):
-        return (b, 4 * C - 3 + b, 4)
+    def el(name, b, h):
+        return V(name, 4 * B * h + b, 4 * B * (h + 1) - 3 + b, 4)
+
+    def half(name, h, b=0, w=1):
+        return V(name, (b * C + B * h) * w, (b * C + B * h + B) * w)
 
     def cols(name, b, n=128):
         return V(name, n * b, n * b + n)
 
+    def bank(k, n=B):
+        return V("ps%d" % k, 0, n)
+
     dma("y", [(T.oi[:], T.o[:]), (T.mi[:], T.m[:])], [], [V("oi"), V("mi")])
-    dma("s", [(T.x0[:], T.x[:])], [], [V("x0")])
-    dma("y", [(T.ut[:], T.u[:])], [], [V("ut")])
-    dma("y", [(by(V("wq")), T.wc[:]), (T.wp[:], T.ws[:])], [], [V("wq"), V("wp")])
-    dma("y", [(T.vt[:], T.v[:])], [], [V("vt")])
+    dma("s", [(T.x0[:, 0:4 * B], T.x[:, 0:4 * B])], [], [half("x0", 0, 0, 4)], 2.8)
+    dma("y", [(T.ut[:], T.u[:])], [], [V("ut")], 2.8)
+    dma("s", [(T.x0[:, 4 * B:4 * C], T.x[:, 4 * B:4 * C])], [], [half("x0", 1, 0, 4)], 3.2)
+    dma("y", [(by(V("wq")), T.wc[:]), (T.wp[:], T.ws[:])], [], [V("wq"), V("wp")], 4.5)
+    dma("y", [(T.vt[:], T.v[:])], [], [V("vt")], 5.0)
 
     iota(V("pcol"), [[0, 8]], 0, 1)
-    iota(V("kpat"), [[32, 10], [1, 2]], 0, 0)
-    iota(V("j16"), [[0, C // 16], [1, 16]], 0, 0)
     iota(V("iota"), [[1, C]], -B, 0)
+    iota(V("j16"), [[1, 16]], 0, 0)
+    iota(V("kpat"), [[32, 10], [0, 2]], 1, 0)
     iota(V("uli"), [[16, 8]], 0, 0)
     fill(V("ones"), 1.0)
     run("g", lambda: g.affine_select(T.ect[:], T.ones[:], [[1, 516]], OP.is_equal, 0.0, -3, -4), [V("ones")], [V("ect")])
-    iota(V("cw"), [[1024, C]], -1024 * B, 0)
-    pm, pm2 = tmp(1), tmp(1)
+    pm, pm1, pm2 = tmp(1), tmp(1), tmp(1)
     ts(V("pcol2"), V("pcol"), 15, OP.bitwise_and)
     copy(pm, V("pcol2", 0, 1))
-    ts(pm2, pm, 2.0, OP.mult)
-    K = [tmp(20), tmp(20)]
-    tsp(K[0], V("kpat"), pm2, OP.add)
-    ts(K[1], K[0], -1.0, OP.add)
-    ku0, first = lst(20), tmp(10)
-    copy(ku0, K[0])
-    ts(first, sub(K[1], 0, 20, 2), 0.0, OP.is_lt)
-    last, K2 = tmp(20), tmp(20)
-    ts(last, K[1], 0.0, OP.is_lt, float(C), OP.mult)
-    tt(K2, K[1], last, OP.add)
-    for t in range(3):
-        kA = sub(K[t % 2], 0, 20, 2)
-        ts(V("dl%d" % t, 0, 6), sub(kA, 0, 6), 0.0, OP.max)
-        ts(V("dl%d" % t, 26, 36), kA, 0.0, OP.max)
-    tsp(V("mask", 0, C), V("j16"), pm, OP.is_equal)
-    run("s", lambda: g.scalar.activation(ap(V("hold", 0, C)), T.j16[:], AF.Sign), [V("j16")], [V("hold", 0, C)])
-    act(V("mask", C, LW), V("mask", 0, C))
-    act(V("hold", C, LW), V("hold", 0, C))
-    for v, z in ((V("bw", 0, B + 1), -1e29), (V("bw", B + 1, B + 8), 1e29)):
-        run("s", lambda v=v, z=z: g.scalar.activation(ap(v), ap(V("j16", 0, v[2] - v[1])), AF.Identity, bias=z, scale=0.0), [V("j16")], [v])
+    ts(pm1, V("pcol2", 0, 1), 1.0, OP.add)
+    ts(pm2, V("pcol2", 0, 1), 2.0, OP.mult)
+    k1, k2, lanes = tmp(16), tmp(16), lst(20)
+    ts(k1, V("j16"), pm, OP.not_equal)
+    ts(k2, V("j16"), pm1, OP.is_equal, BIG, OP.mult)
+    tt(V("k16"), k1, k2, OP.add)
+    ts(lanes, V("kpat"), 0.0, OP.mult, pm, OP.add)
+    pick("s", V("kk"), V("k16"), lanes)
+    w, iw, iw2, iw1k, wv, wp0, wlo, w1k, no0 = [tmp(1) for k in range(9)]
+    ts(w, pm, 15.0, OP.is_lt, BIG, OP.mult)
+    ts(w, w, 1.0, OP.max)
+    ts(iw, pm, 15.0, OP.is_equal, 1.0 / BIG, OP.max)
+    ts(iw2, iw, 2.0, OP.mult)
+    ts(iw1k, iw, 1.0 / 1024, OP.mult)
+    ts(wv, w, 1025.0 * B, OP.mult)
+    ts(wp0, w, float(B - PB), OP.mult)
+    ts(wlo, w, float(B - PB), OP.mult)
+    ts(w1k, w, 1000.0, OP.mult)
+    ts(no0, pm, 0.0, OP.is_gt)
+    KB = [tmp(20), tmp(20)]
+    ts(sub(KB[0], 0, 10), V("kpat", 0, 19, 2), pm2, OP.add)
+    ts(sub(KB[0], 10, 20), V("kpat", 0, 19, 2), pm2, OP.add)
+    ts(KB[1], KB[0], -1.0, OP.add)
+    act(V("cw"), V("iota"), 1024.0)
+    act(V("cw", B, B + 1), V("iota", B, B + 1), 0.0, 1.0)
     for v in [V("tp1", 328, 352), V("dr1", 328, 352)] + [V("wf", b * WD + C, (b + 1) * WD) for b in range(4)]:
-        act(v, V("j16", 0, v[2] - v[1]), 0.0)
-    onat, mu = lst(20), [lst(20) for k in range(4)]
-    copy(onat, V("oi"))
-    copy(mu[0], V("mi"))
-
-    acti(V("orow"), V("iota"), onat)
-    acti(V("mrow"), V("iota"), mu[0])
-    run("v", lambda: g.vector.tensor_copy(ind(V("prow"), onat), ap(V("iota"))), [V("iota"), onat], [V("prow")], "scat")
-    ot = look20(V("orow"), ku0)
-    ou = lst(20)
-    ts(ou, ot, float(B), OP.add)
-    ts(V("cur0", 0, 20), ot, float(B), OP.add)
+        act(v, V("iota", 0, v[2] - v[1]), 0.0)
     for b in range(4):
         quant(cols("eq", b), cols("ep", b), V("ect", 3 - b, 515 - b))
-    quant(V("xq"), V("xp"), V("x0"))
-    xt0 = look20(V("mrow"), ou)
-    xu = lst(20)
-    ts(xu, xt0, float(B), OP.add)
-    quant(V("uq"), V("up"), V("ut"))
     copy(V("ulu"), V("uli"))
+
+    onat, mnat, mu = lst(20), lst(20), [lst(20) for k in range(4)]
+    copy(onat, V("oi"))
+    run("v", lambda: g.vector.tensor_copy(ind(V("prow"), onat), ap(V("iota"))), [V("iota"), onat], [V("prow")], "scat")
+    copy(mnat, V("mi"))
+    ts(sub(mu[0], 0, 10), V("mi", 0, 10), -float(B), OP.add)
+    copy(sub(mu[0], 10, 20), V("mi", 10, 20))
+    pick("s", V("orow"), V("iota"), onat)
+    pick("s", V("mrow"), V("iota"), mnat)
+    pick("s", V("xrow"), V("mrow"), onat)
+    for h in range(2):
+        pick(ON["pm%d" % h], half("pmrow", h), V("prow"), sub(mnat, 10 * h, 10 * h + 10))
+    for h in range(2):
+        pick(ON["M%d" % h], half("Mrow", h), V("pmrow"), sub(onat, 10 * h, 10 * h + 10))
+
+    def couples(name, first):
+        out = row()
+        for e in range(2):
+            scan(sub(out, B * e, B * e + B), V(name, e if first else 1 - e, C - 1 + (e if first else 1 - e), 2))
+        return tab(out)
+
+    ts(V("cur0", 20, 40), couples("orow", True), iw2, OP.mult, 1.0, OP.add)
+    M0 = couples("Mrow", False)
+    ts(V("cur0", 60, 80), M0, iw, OP.mult, float(B), OP.add)
+    x0, val0 = tmp(20), tmp(20)
+    ts(x0, couples("xrow", False), 1024.0, OP.mult, wv, OP.add)
+    tt(val0, x0, M0, OP.add)
+    p0 = table(V("prow"))
+    P, pu = tmp(20), lst(20)
+    ts(P, p0, wp0, OP.add)
+    ts(pu, p0, iw, OP.mult, float(B), OP.add)
+
+    quant(V("uq"), V("up"), V("ut"))
     run("s", lambda: g.scalar.activation(T.up16[:], T.up[:].indirect(T.ulu[:]), AF.Copy), [V("up"), V("ulu")], [V("up16")], "ind")
     run("v", lambda: g.vector.tensor_copy(T.uq16[:].bitcast(dt.uint32), T.uq[:].bitcast(dt.uint32).indirect(T.ulu[:])), [V("uq"), V("ulu")], [V("uq16")], "ind")
-    Mt0 = look20(V("prow"), xu)
-    M0, x1 = tmp(20), tmp(20)
-    ts(M0, Mt0, float(B), OP.add)
 
-    def sides(y, M, o, k):
-        d, b2 = tmp(20), tmp(20)
-        tt(d, M, (K[0], K2)[k], OP.is_gt)
-        ts(b2, o, float(B), OP.is_lt, 2.0, OP.mult)
-        tt(y, d, b2, OP.add)
-
-    def static(t, M):
+    def static(t, val):
         k = t % 2
         cur = V("cur%d" % t)
-        o = sub(cur, 0, 20)
-        oA, oB = sub(cur, 0, 20, 2), sub(cur, 1, 20, 2)
-        y = sub(cur, 40, 60)
-        if M is None: M = sub(cur, 60, 80)
-        else: sides(y, M, o, 0)
-        MA, MB = sub(M, 0, 20, 2), sub(M, 1, 20, 2)
-        eq, gt, S, do, bi, biu = tmp(10), tmp(10), tmp(10), tmp(10), tmp(20), lst(20)
-        ix, ixu = sub(bi, 10, 20), sub(biu, 10, 20)
-        if k:
-            bl = tmp(10)
-            tt(bl, MA, sub(K[k], 1, 20, 2), OP.is_equal)
-            tt(sub(bi, 0, 10), bl, first, OP.max)
-        else:
-            tt(sub(bi, 0, 10), MA, sub(K[k], 1, 20, 2), OP.is_equal)
-        tt(eq, sub(y, 0, 20, 2), sub(y, 1, 20, 2), OP.is_equal)
-        tt(gt, MA, MB, OP.is_gt)
-        tt(S, eq, gt, OP.mult)
-        tt(do, oB, oA, OP.subtract)
+        a = 1 if t < 2 else 0
+        oA, oB = sub(cur, 30 - 10 * a, 40 - 10 * a), sub(cur, 20 + 10 * a, 30 + 10 * a)
+        M, uM = sub(cur, 60, 80), sub(cur, 40, 60)
+        if val is None:
+            ts(M, sub(cur, 0, 20), 1023, OP.bitwise_and)
+        tt(uM, M, KB[k], OP.subtract)
+        d, pr, nb, dob, oA2, mn, mn2, S, ix = tmp(30), tmp(30), tmp(10), tmp(10), tmp(10), tmp(10), tmp(10), tmp(10), tmp(10)
+        oAu, oBu, ixu, Mu = lst(10), lst(10), lst(10), lst(20)
+        lo, hi = sub(cur, 20, 50), sub(cur, 30, 60)
+        if a: tt(d, hi, lo, OP.subtract)
+        else: tt(d, lo, hi, OP.subtract)
+        do = sub(d, 0, 10)
+        ts(nb, sub(uM, 10 * a, 10 * a + 10), 0.0, OP.not_equal)
+        if k: ts(sub(nb, 0, 1), sub(nb, 0, 1), no0, OP.mult)
+        tt(pr, lo, hi, OP.mult)
+        tt(dob, do, nb, OP.mult)
+        tt(mn, sub(pr, 0, 10), sub(pr, 20, 30), OP.min)
+        tt(oA2, oB, dob, OP.subtract)
+        tt(mn2, mn, sub(d, 20, 30), OP.min)
+        ts(oBu, oB, 0.5, OP.mult, 159.5, OP.add)
+        ts(S, mn2, 0.0, OP.is_gt)
+        ts(oAu, oA2, 0.5, OP.mult, 159.5, OP.add)
         tt(ix, do, S, OP.mult)
-        ts(biu, bi, float(B), OP.add)
-        acti(V("bd%d" % t), V("bw"), sub(biu, 0, 10))
-        acti(first_of("dr%d" % t, k), V("cw"), ixu)
-        acti(second_of("dr%d" % t, k), V("cw"), ixu)
-        return dict(t=t, do=do, S=S, M=M, oA=oA, oB=oB)
+        copy(Mu, M)
+        ts(ixu, ix, 0.5, OP.mult, float(B), OP.add)
+        if val is None:
+            val = tmp(20)
+            ts(val, sub(cur, 0, 20), w, OP.mult)
+        dr = "dr%d" % t
+        pick("s", place(dr, k, 0), V("cw"), ixu)
+        pick(ON["dr1"], place(dr, k, 1), V("cw"), ixu)
+        pick(ON["dm"], V("dm%d" % t), win0(dr), Mu)
+        return dict(a=a, dob=dob, S=S, oA=oA, oB=oB, oAu=oAu, oBu=oBu, Mu=Mu, val=val)
 
-    def static2(r):
-        copy(V("dl%d" % r["t"], 6, 26), r["M"])
-        r["oAu"], r["oBu"] = lst(10), lst(10)
-        copy(r["oBu"], r["oB"])
-        copy(r["oAu"], r["oA"])
-        r["D"] = look20(win0("dr%d" % r["t"]), V("dl%d" % r["t"], 6, 26))
+    FB = [[0, 1, 2, 3], [5, 6, 7, 0]]
 
-    def products(t):
-        mm(V("ps4", 0, C), V("uq16"), V("up16"), V("xq"), V("xp"))
+    def products(src, h):
+        q, p = half("xq", h), half("xp", h)
+        quant(q, p, half(src, h, 0, 4))
+        mm(bank(4), V("uq16"), V("up16"), q, p)
+        act(half("sc", h), bank(4))
         for b in range(4):
-            mm(V("ps%d" % b, 0, C), cols("eq", b), cols("ep", b), V("xq"), V("xp"))
-        act(V("sc"), V("ps4", 0, C))
-        for b in range(4):
-            act(wfF(b), V("ps%d" % b, 0, C), 0.5)
+            mm(bank(FB[h][b]), cols("eq", b), cols("ep", b), q, p)
+            act(wfF(b, h), bank(FB[h][b]), 0.5)
 
-    fill(V("cw", B, B + 1), 1.0)
-    r = static(0, M0)
-    ts(x1, xt0, 1024.0, OP.mult, 1024.0 * B, OP.add)
-    tt(V("cur0", 20, 40), x1, M0, OP.add)
-    products(0)
-    static2(r)
-    P = None
+    r = static(0, val0)
+    products("x0", 0)
+    products("x0", 1)
     for t in range(3):
         k = t % 2
         nl = 5 + k
-        nu = 10 - nl
-        dl, tp, er = "dl%d" % t, "tp%d" % t, "er%d" % t
-        cur, st = V("cur%d" % t), V("st%d" % t)
-        val = sub(cur, 20, 40)
-        D, S, do = r["D"], r["S"], r["do"]
-        tti(V("sb"), V("sc"), r["oBu"], V("bd%d" % t), OP.max)
-        tti(first_of(tp, k), V("sc"), r["oAu"], V("sb"), OP.is_gt)
-        ts(second_of(tp, k), first_of(tp, k), -1.0, OP.mult)
-        fg, fs = "fg%d" % t, "fs%d" % t
-        eu = lst(20)
-
-        def renew(tc, tM, c0, c1):
-            n = c1 - c0
-            d1, alt, rr, dd, d2 = tmp(2 * n), tmp(2 * n), tmp(n), tmp(n), tmp(n)
-            tt(d1, tM, sub(D, 2 * c0, 2 * c1), OP.mult)
-            tt(rr, tc, sub(S, c0, c1), OP.is_gt)
-            tt(alt, d1, sub(val, 2 * c0, 2 * c1), OP.add)
-            aA, aB = sub(alt, 0, 2 * n, 2), sub(alt, 1, 2 * n, 2)
-            tt(dd, aB, aA, OP.subtract)
-            tt(d2, dd, rr, OP.mult)
-            eA, eB = sub(st, 20 + 2 * c0, 20 + 2 * c1, 2), sub(st, 21 + 2 * c0, 20 + 2 * c1, 2)
-            tt(eA, aA, d2, OP.add)
-            tt(eB, aB, d2, OP.subtract)
-            ts(sub(eu, c0, c1), eA, 1.0 / 1024, OP.mult)
-            ts(sub(eu, 10 + c0, 10 + c1), eB, 1.0 / 1024, OP.mult)
-
-        wl = 16 * (6 + 2 * nl)
-        fl = V(fs, 0, wl)
-        lookup(V(fg, 0, wl), fl, win0(tp), V(dl, 0, 6 + 2 * nl))
-        renew(tab(fl, 0, nl), tab(fl, 6, 6 + 2 * nl), 0, nl)
+        a = r["a"]
+        tp, er = "tp%d" % t, "er%d" % t
+        pick(ON["sb"], V("sb"), V("sc"), r["oBu"])
+        tti(place(tp, k, 0), V("sc"), r["oAu"], V("sb"), OP.is_gt)
+        ts(place(tp, k, 1), place(tp, k, 0), -1.0, OP.mult)
+        ur, tc, rr, alt, dd, d2, e, eu = row(), tmp(10), tmp(10), tmp(20), tmp(10), tmp(10), tmp(20), lst(20)
+        tcw = table(place(tp, k, 0), B)
+        tti(ur, win0(tp), r["Mu"], V("dm%d" % t), OP.mult)
+        ts(tc, tcw, iw, OP.mult, 0.5, OP.is_gt)
+        u = table(ur)
+        tt(rr, tc, r["S"], OP.is_gt)
+        tt(alt, r["val"], u, OP.add)
+        A, Bv = (10 * a, 10 * a + 10), (10 - 10 * a, 20 - 10 * a)
+        tt(dd, sub(alt, *Bv), sub(alt, *A), OP.subtract)
+        tt(d2, dd, rr, OP.mult)
+        tt(sub(e, *A), sub(alt, *A), d2, OP.add)
+        tt(sub(e, *Bv), sub(alt, *Bv), d2, OP.subtract)
+        ts(eu, e, iw1k, OP.mult)
+        euA, euB = sub(eu, *A), sub(eu, *Bv)
         for b in range(4):
-            acti(V("et", b, 128 * nl - 7 + b, 8), wfF(b), sub(eu, 0, nl), 2.0)
-            tsi(V("et", 4 + b, 128 * nl - 3 + b, 8), wfF(b), sub(eu, 10, 10 + nl), 2.0, OP.mult)
+            pick("s", V("et", b, 128 * nl - 7 + b, 8), wfF(b), sub(euA, 0, nl), 2.0)
+            pick("v", V("et", 4 + b, 128 * nl - 3 + b, 8), wfF(b), sub(euB, 0, nl), 2.0)
         ne = NE[t]
         qe, pe, lq, lp = [V(s + str(t), 0, ne) for s in ("qe", "pe", "lq", "lp")]
         quant(qe, pe, V("et", 0, 4 * ne))
@@ -408,101 +415,88 @@ def rank_program(g, core, T, topo):
             log[lp[0]] = [(lp, arr, full, True, "r")]
 
         put("g", send, [qe, pe], [lq, lp], 1.0, 2.2)
-        for b in range(4):
-            acti(cols("ah", b, C), wfF(b), mu[t])
-        if t == 0:
-            tt(V("ra8"), V("prow"), V("mask", 0, C), OP.mult)
-            scan(V("rs8"), V("ra8"))
-            p0 = tab(V("rs8"), 0, 20)
-            ts(V("dl0", 36, 56), p0, float(B), OP.add)
-            P = tmp(20)
-            ts(P, p0, float(B - PB), OP.add)
-        wu, lu = 16 * (2 * nu + 10), 6 + 2 * nl
-        fv = V(fs, LW - C, LW - C + wu)
-        lookup(V(fg, LW - C, LW - C + wu), fv, win0(tp), V(dl, lu, lu + 2 * nu + 10))
-        tc = tab(fv, 2 * nu, 2 * nu + 10)
-        renew(sub(tc, nl, 10), tab(fv, 0, 2 * nu), nl, 10)
-        fu = V(fs, LW, LW + C)
-        lookup(V(fg, LW, LW + C), fu, win0(tp), V(dl, 36, 56))
-        acti(first_of(er, k), V("iota"), sub(eu, 0, 10))
-        acti(second_of(er, k), V("iota"), sub(eu, 10, 20))
-        if k: act(V(er, 16 + C - 1, 16 + C), V(er, 15, 16))
-        pn, pf, pz, pu = tmp(20), tmp(20), tmp(20), lst(20) if t == 2 else V("dl%d" % (t + 1), 36, 56)
-        tt(pn, P, tab(fu, 0, 20), OP.add)
-        P = pn
-        ts(pu, pn, float(PB), OP.add)
         t1 = tmp(10)
-        tt(t1, tc, do, OP.mult)
-        tt(sub(st, 0, 20, 2), sub(cur, 0, 20, 2), t1, OP.add)
-        tt(sub(st, 1, 20, 2), sub(cur, 1, 20, 2), t1, OP.subtract)
-        ts(pf, pn, float(B - PB), OP.is_lt, 1000.0, OP.mult)
+        tt(t1, tc, r["dob"], OP.mult)
+        if t < 2:
+            nx, go = V("cur%d" % (t + 1)), V("go%d" % t, 0, 20)
+            stay, move = (A, Bv) if t == 0 else (Bv, A)
+            ts(sub(go, 0, 10), sub(e, *move), iw, OP.mult)
+            ts(sub(nx, 0, 10), sub(e, *stay), iw, OP.mult)
+            tt(sub(nx, 30, 40) if t == 0 else sub(go, 10, 20), r["oA"], t1, OP.add)
+            tt(sub(go, 10, 20) if t == 0 else sub(nx, 30, 40), r["oB"], t1, OP.subtract)
+            s, h = T[go[0]], T[nx[0]]
+            pairs = []
+            for q in range(0, 128, 16):
+                pairs.append((h[q + 1:q + 16, 10:30], s[q:q + 15, 0:20]) if t == 0 else (h[q:q + 15, 10:30], s[q + 1:q + 16, 0:20]))
+            for z in (0, 10):
+                if t == 0:
+                    pairs.append((h[0:128:16, z + 11:z + 20], s[15:128:16, z:z + 9]))
+                    pairs.append((h[0:128:16, z + 10:z + 11], s[15:128:16, z + 9:z + 10]))
+                else:
+                    pairs.append((h[15:128:16, z + 10:z + 19], s[0:128:16, z + 1:z + 10]))
+                    pairs.append((h[15:128:16, z + 19:z + 20], s[0:128:16, z:z + 1]))
+            dma("y", pairs, [go], [sub(nx, 0, 40)])
+        else:
+            of, ofu = tmp(20), lst(20)
+            tt(sub(of, 0, 10), r["oA"], t1, OP.add)
+            tt(sub(of, 10, 20), r["oB"], t1, OP.subtract)
+            ts(ofu, of, 0.5, OP.mult, 159.5, OP.add)
+        fr, mr = row(), row()
+        pick(ON["p"], fr, win0(tp), pu)
+        pick("s", place(er, k, 0), V("iota"), euA)
+        pick("s", place(er, k, 1), V("iota"), euB)
+        if k: act(V(er, 16 + C - 1, 16 + C), V(er, 15, 16))
+        pn, pf, pz, pu = tmp(20), tmp(20), tmp(20), lst(20)
+        tt(pn, P, table(fr), OP.add)
+        P = pn
+        ts(pu, pn, iw, OP.mult, float(PB), OP.add)
+        ts(pf, pn, wlo, OP.is_lt, w1k, OP.mult)
         tt(pz, pf, pn, OP.add)
-        if t == 2:
-            ofu = lst(20)
-            copy(sub(ofu, 0, 10), sub(st, 0, 20, 2))
-            copy(sub(ofu, 10, 20), sub(st, 1, 20, 2))
-        mn = look20(win0(er), pu)
+        pick(ON["mn"], mr, win0(er), pu)
+        mn = table(mr)
         vm, vl = tmp(20), lst(20)
         tt(vm, pz, mn, OP.max)
-        ts(vl, vm, float(B), OP.add)
+        ts(vl, vm, iw, OP.mult, float(B), OP.add)
+        ts(sub(mu[t + 1], 0, 10), sub(mn, 0, 10), iw, OP.mult)
+        ts(sub(mu[t + 1], 10, 20), sub(mn, 10, 20), iw, OP.mult, float(B), OP.add)
+        for h in (1, 0):
+            for b in range(4):
+                pick("s", half("ah", h, b), wfF(b, 1 - h), sub(mu[t], 10 * h, 10 * h + 10))
+        for b in range(4):
+            mm(bank(b, ne), cols("eq", b), cols("ep", b), lq, lp)
+            act(V("wf", b * WD + C + 1 - k, b * WD + C + 1 - k + ne), bank(b, ne), 0.5)
+        for z in range(2):
+            scaled(ON["af%d" % z], V("af", 2 * C * z, 2 * C * z + 2 * C), V("ah", 2 * C * z, 2 * C * z + 2 * C), 2.0)
+        for h in (1, 0):
+            for b in range(4):
+                tti(el("zt", b, h), wf(b), sub(vl, 10 * h, 10 * h + 10), half("ah", h, b), OP.add)
+            quant(half("zq", h), half("zp", h), half("zt", h, 0, 4))
+            for b in range(4):
+                n = 4 * (1 - h) + b
+                mm(bank(n), cols("wq", b), cols("wp", b), half("zq", h), half("zp", h))
+                act(half("gs", h, b), bank(n), 0.0078125)
         if t < 2:
-            ts(sub(st, 60, 80), sub(st, 20, 40), 1023, OP.bitwise_and)
-            sides(sub(st, 40, 60), sub(st, 60, 80), sub(st, 0, 20), k)
-            s, h = T["st%d" % t], T["sh%d" % t]
-            pairs = []
-            if t == 0:
-                for q in range(0, 128, 16):
-                    pairs.append((h[q + 1:q + 16, :], s[q:q + 15, :]))
-                for z in (0, 20, 40, 60):
-                    pairs.append((h[0:128:16, z + 2:z + 20], s[15:128:16, z:z + 18]))
-                    pairs.append((h[0:128:16, z:z + 2], s[15:128:16, z + 18:z + 20]))
-            else:
-                for q in range(0, 128, 16):
-                    pairs.append((h[q:q + 15, :], s[q + 1:q + 16, :]))
-                for z in (0, 20, 40, 60):
-                    pairs.append((h[15:128:16, z:z + 18], s[0:128:16, z + 2:z + 20]))
-                    pairs.append((h[15:128:16, z + 18:z + 20], s[0:128:16, z:z + 2]))
-            dma("y", pairs, [st], [V("sh%d" % t)])
-        for b in range(4):
-            mm(V("ps%d" % b, 0, ne), cols("eq", b), cols("ep", b), lq, lp)
-            act(V("wf", b * WD + C + 1 - k, b * WD + C + 1 - k + ne), V("ps%d" % b, 0, ne), 0.5)
-        for b in range(4):
-            tti(V("zt", *el(b)), wf(b), vl, cols("ah", b, C), OP.add)
-        act(V("af"), V("ah"), 2.0)
-        quant(V("zq"), V("zp"), V("zt"))
-        ts(mu[t + 1], mn, float(B), OP.add)
-        if t == 2:
-            actb(V("romo", 0, C - 1, 2), V("iota"), sub(ofu, 0, 10), float(B))
-            actb(V("romo", 1, C, 2), V("iota"), sub(ofu, 10, 20), float(B))
-        for b in range(4):
-            mm(V("ps%d" % (4 + b), 0, C), cols("wq", b), cols("wp", b), V("zq"), V("zp"))
-            act(cols("gs", b, C), V("ps%d" % (4 + b), 0, C), 0.0078125)
-        if t < 2:
-            n, h = "cur%d" % (t + 1), "sh%d" % t
-            if t == 0:
-                copy(V(n, 0, 79, 2), V(h, 1, 80, 2))
-                copy(V(n, 1, 80, 2), V("st0", 0, 79, 2))
-            else:
-                copy(V(n, 0, 79, 2), V("st1", 1, 80, 2))
-                copy(V(n, 1, 80, 2), V(h, 0, 79, 2))
             r = static(t + 1, None)
         else:
             quant(V("vq"), V("vp"), V("vt"))
-        for b in range(4):
-            tti(V("xt", *el(b)), cols("gs", b, C), mu[t + 1], cols("af", b, C), OP.add)
-        quant(V("xq"), V("xp"), V("xt"))
-        if t < 2:
-            products(t + 1)
-            static2(r)
-    for z in range(2):
-        mm(V("ps%d" % (4 + z), 0, B), V("vq"), V("vp"), V("xq", B * z, B * z + B), V("xp", B * z, B * z + B))
-    dma("y", [(T.oc[:], by(V("xq")))] + [(T.osc[4 * q:4 * q + 4, :], T.xp[32 * q:32 * q + 4, :]) for q in range(4)], [V("xq"), V("xp")], [])
-    act(V("ysb", 0, B), V("ps4", 0, B))
-    copy(V("ysb", B, C), V("ps5", 0, B))
-    dma("s", [(T.y[:, 0:B], T.ysb[:, 0:B])], [V("ysb", 0, B)], [])
-    dma("s", [(T.y[:, B:C], T.ysb[:, B:C])], [V("ysb", B, C)], [])
-    actb(V("romm"), V("iota"), mu[3], float(B))
-    dma("y", [(T.om[:, 0:C], T.romo[0:128:16, :]), (T.om[:, C:2 * C], T.romm[0:128:16, :])], [V("romo"), V("romm")], [])
+            actb(V("romo", 0, C - 1, 2), V("iota"), sub(ofu, 0, 10), float(B))
+            actb(V("romo", 1, C, 2), V("iota"), sub(ofu, 10, 20), float(B))
+            for h in range(2):
+                actb(half("romm", h), V("iota"), sub(mu[3], 10 * h, 10 * h + 10), float(C - B * h))
+            dma("y", [(T.om[:, 0:C], T.romo[0:128:16, :]), (T.om[:, C:2 * C], T.romm[0:128:16, :])], [V("romo"), V("romm")], [])
+        for h in range(2):
+            for b in range(4):
+                tti(el("xt", b, h), half("gs", 1 - h, b), sub(mu[t + 1], 10 * h, 10 * h + 10), half("af", h, b), OP.add)
+            if t < 2:
+                products("xt", h)
+            else:
+                q, p = half("xq", h), half("xp", h)
+                quant(q, p, half("xt", h, 0, 4))
+                mm(bank(h), V("vq"), V("vp"), q, p)
+                dma("y", [(T.oc[:, 4 * B * h:4 * B * h + 4 * B], by(q))]
+                    + [(T.osc[4 * z:4 * z + 4, B * h:B * h + B], T.xp[32 * z:32 * z + 4, B * h:B * h + B]) for z in range(4)], [q, p], [], 2.5)
+                act(half("ysb", h), bank(h))
+                dma("s", [(T.y[:, B * h:B * h + B], ap(half("ysb", h)))], [half("ysb", h)], [], 2.5)
     if "plan" not in PLAN:
         seen, before = {}, []
         for i, (q, issue, reads, writes, cost, late) in enumerate(calls):
@@ -510,8 +504,8 @@ def rank_program(g, core, T, topo):
             for vs, isw in ((reads, False), (writes, True)):
                 for v in vs:
                     psum = v[0][:2] == "ps"
-                    for w, j, oldw in seen.get(v[0], ()):
-                        if (isw or oldw or (psum and calls[j][0] != q)) and (psum or clash(v, w)): p.add(j)
+                    for wv_, j, oldw in seen.get(v[0], ()):
+                        if (isw or oldw or (psum and calls[j][0] != q)) and (psum or clash(v, wv_)): p.add(j)
             for vs, isw in ((reads, False), (writes, True)):
                 for v in vs: seen.setdefault(v[0], []).append((v, i, isw))
             before.append(sorted(p))
@@ -523,78 +517,38 @@ def rank_program(g, core, T, topo):
 
 
 PLAN = {}
-MACHINES = [(1.0, 0.06, 0.0, 0.0), (1.1, 0.1, 0.06, 0.5), (1.2, 0.15, 0.1, 1.0), (0.9, 0.08, 0.05, 2.0)]
-TRIES = 170000
-
-
-def walk(ops, before, seqs, m):
-    fac, wake, own, more = m
-    end, at, free = {}, {q: 0 for q in seqs}, {q: 0.0 for q in seqs}
-    begun = {}
-    left = len(ops)
-    while left:
-        moved = False
-        for q, seq in seqs.items():
-            while at[q] < len(seq):
-                i = seq[at[q]]
-                t, late = free[q], False
-                ok = True
-                for j in before[i]:
-                    if j not in end:
-                        ok = False
-                        break
-                if not ok: break
-                for j in before[i]:
-                    e = end[j] + (own if ops[j][0] == q and end[j] >= free[q] - 1e-9 else wake if ops[j][0] != q and end[j] > free[q] else 0.0)
-                    if e > t: t = e
-                begun[i] = t
-                free[q] = t + ops[i][1] * (fac if q in "vs" else 1.0)
-                end[i] = free[q] + (ops[i][2] + more if ops[i][2] else 0.0)
-                at[q] += 1
-                left -= 1
-                moved = True
-        if not moved: return 1e9, begun
-    return max(end.values()), begun
+WAKE, OWN = 0.08, 0.06
+AHEAD = 0.12
 
 
 def plan(ops, before):
     n = len(ops)
-    known, need = [0] * n, []
+    after = [[] for i in range(n)]
     for i in range(n):
-        keep, a = [], 0
-        for j in sorted(before[i], reverse=True):
-            if not (a >> j) & 1:
-                keep.append(j)
-                a |= known[j] | (1 << j)
-        known[i] = a
-        need.append(keep)
-    seqs = {q: [i for i in range(n) if ops[i][0] == q] for q in "vstgy"}
-    base = [walk(ops, need, seqs, m)[0] for m in MACHINES]
-    now, rng = 1.0, np.random.RandomState(4)
-    best = (now, seqs)
-    for turn in range(TRIES):
-        q = "vvvs"[rng.randint(4)]
-        row = list(seqs[q])
-        a, k = int(rng.randint(len(row))), 1 if rng.rand() < 0.6 else int(rng.randint(1, 8))
-        b = a + int(rng.randint(1, 40)) * (1 if rng.rand() < 0.5 else -1)
-        lim = now - 0.0006 * max(0.0, 1.0 - 1.2 * turn / TRIES) * math.log(rng.rand() + 1e-12)
-        run = row[a:a + k]
-        del row[a:a + k]
-        b = max(0, min(len(row), b))
-        mid = row[min(a, b):max(a, b)]
-        if b > a and any([j in run for i in mid for j in need[i]]): continue
-        if b < a and any([j in mid for i in run for j in need[i]]): continue
-        row[b:b] = run
-        new = dict(seqs)
-        new[q] = row
-        total = 0.0
-        for m, w in zip(MACHINES, base):
-            r = walk(ops, need, new, m)[0] / w
-            total += r / len(MACHINES)
-            if r > lim + 0.03: total += 9.0
-            if total > lim: break
-        if total <= lim:
-            now, seqs = total, new
-            if now < best[0]: best = (now, seqs)
-    begun = walk(ops, need, best[1], MACHINES[1])[1]
-    return [i for t, i in sorted([(begun[i], i) for i in range(n)])]
+        for j in before[i]: after[j].append(i)
+    urge = [0.0] * n
+    for i in range(n - 1, -1, -1):
+        urge[i] = ops[i][1] + ops[i][2] + max([urge[j] + WAKE for j in after[i]] + [0.0])
+    left = [len(b) for b in before]
+    ready = [i for i in range(n) if not left[i]]
+    end, free, last, out = {}, {q: 0.0 for q in "vstgy"}, {q: -1 for q in "vstgy"}, []
+
+    def start(i):
+        q = ops[i][0]
+        return max([free[q]] + [end[j] + ((OWN if j == last[q] else 0.0) if ops[j][0] == q and not ops[j][2] else WAKE) for j in before[i]])
+
+    while ready:
+        at = {i: start(i) for i in ready}
+        first = min(ready, key=lambda i: (at[i], -urge[i]))
+        q = ops[first][0]
+        i = max([j for j in ready if ops[j][0] == q and at[j] <= at[first] + AHEAD], key=lambda j: (urge[j] - at[j], -j))
+        ready.remove(i)
+        out.append(i)
+        free[q] = at[i] + ops[i][1]
+        end[i] = free[q] + ops[i][2]
+        last[q] = i
+        for j in after[i]:
+            left[j] -= 1
+            if not left[j]: ready.append(j)
+    PLAN["end"] = max(end.values())
+    return out

@@ -8,7 +8,7 @@ EW = 176
 WD = C + EW
 NE = [160, 162, 160]
 F8, BF, F32, U16, U8, I32 = "float8_e4m3fn_x4", "bfloat16", "float32", "uint16", "uint8", "int32"
-CYCLE = 0.00104
+CYCLE = 0.00093
 PB = 839
 BIG = 2.0 ** 64
 
@@ -22,11 +22,11 @@ SCRATCH = {
     "ect": ("sbuf", [128, 516], BF), "ones": ("sbuf", [128, 516], BF),
     "eq": ("sbuf", [128, 512], F8), "ep": ("sbuf", [128, 512], U8),
     "iota": ("sbuf", [128, C], BF), "cw": ("sbuf", [128, C], BF),
-    "j16": ("sbuf", [128, 16], F32), "k16": ("sbuf", [128, 16], BF), "kk": ("sbuf", [128, C], BF),
-    "pcol": ("sbuf", [128, 8], I32), "pcol2": ("sbuf", [128, 8], I32), "uli": ("sbuf", [128, 8], I32), "ulu": ("sbuf", [128, 8], U16),
-    "kpat": ("sbuf", [128, 20], F32),
+    "six": ("sbuf", [128, 128], BF), "d0": ("sbuf", [128, 128], F32), "d1": ("sbuf", [128, 128], F32),
+    "k16": ("sbuf", [128, 16], BF), "kk": ("sbuf", [128, C], BF),
+    "pcol": ("sbuf", [128, 8], I32), "pcol2": ("sbuf", [128, 8], I32), "ulu": ("sbuf", [128, 8], U16),
     "tb": ("sbuf", [128, 3000], F32), "ub": ("sbuf", [128, 1000], U16),
-    "mrow": ("sbuf", [128, C], BF), "orow": ("sbuf", [128, C], BF), "prow": ("sbuf", [128, C], BF),
+    "orow": ("sbuf", [128, C], BF), "prow": ("sbuf", [128, C], BF),
     "pmrow": ("sbuf", [128, C], BF), "xrow": ("sbuf", [128, C], BF), "Mrow": ("sbuf", [128, C], BF),
     "wf": ("sbuf", [128, 4 * WD], BF),
     "ah": ("sbuf", [128, 4 * C], BF), "af": ("sbuf", [128, 4 * C], BF),
@@ -39,14 +39,20 @@ SCRATCH = {
 for _t in range(3):
     for _n, _d in (("qe", F8), ("pe", U8), ("lq", F8), ("lp", U8)):
         SCRATCH[_n + str(_t)] = ("sbuf", [128, EW], _d)
-    for _n, _w, _d in (("tp", 352, BF), ("dr", 352, BF), ("er", 352, BF), ("dm", C, BF), ("cur", 80, I32), ("go", 24, I32)):
+    for _n, _w, _d in (("tp", 352, BF), ("dr", 352, BF), ("er", 352, BF), ("dm", C, BF), ("cur", 72, F32),
+                       ("uv", C + 20, F32), ("ne", 128, F32), ("vi", 60, I32), ("tq", B + 16, BF)):
         SCRATCH[_n + str(_t)] = ("sbuf", [128, _w], _d)
-for _k in range(26):
+for _t in range(2):
+    for _n, _w, _d in (("go", 40, F32), ("tw", 64, F32), ("tn", 32, F32)):
+        SCRATCH[_n + str(_t)] = ("sbuf", [128, _w], _d)
+for _k in range(24):
     SCRATCH["r%d" % _k] = ("sbuf", [128, C], BF)
 for _k in range(8):
     SCRATCH["ps%d" % _k] = ("psum", [128, 512], F32)
 SEMAPHORES = ["vs", "ss", "ts", "gs"] + ["d%d" % k for k in range(24)] + ["arr%d" % k for k in range(3)] + ["loc%d" % k for k in range(3)]
-ON = {"sb": "v", "p": "s", "mn": "s", "dm": "s", "af0": "v", "af1": "v", "pm0": "v", "pm1": "s", "M0": "v", "M1": "s", "dr1": "s"}
+ON = {"sb": "s", "p": "s", "mn": "s", "dm": "s", "af0": "s", "af1": "v", "pm0": "v", "pm1": "s", "M0": "v", "M1": "s", "dr1": "s",
+      "x0": "s", "sc0": "s", "sc1": "v", "tp": "v", "shift": "d"}
+ALT = True
 
 
 def rank_program(g, core, T, topo):
@@ -107,7 +113,7 @@ def rank_program(g, core, T, topo):
     calls = []
 
     def put(q, issue, reads, writes, cost, late=0.0):
-        calls.append((q, issue, reads, writes, cost, late))
+        calls.append((q, issue, reads, writes, cost, late, None))
 
     def run(q, fn, reads, writes, kind=""):
         def issue():
@@ -120,25 +126,25 @@ def rank_program(g, core, T, topo):
         n = (o[2] - o[1] + o[3] - 1) // o[3]
         narrow = all(SCRATCH[v[0]][2] in (BF, U16) for v in reads + writes)
         psum = any(v[0][:2] == "ps" for v in reads)
-        if kind == "ind": c = 0.06 + 1.56 * CYCLE * n
+        if kind == "ind": c = 0.06 + 1.25 * CYCLE * n
         elif kind == "scat": c = 3.8 * CYCLE * n
-        elif kind == "q": c = 0.015 + 4 * 0.00028 * n
+        elif kind == "q": c = 0.015 + 4 * 0.00025 * n
         elif q == "t": c = (n + 16) * CYCLE
-        elif q == "g": c = 0.2 + 2 * CYCLE * n
-        elif q == "s": c = CYCLE * max(n, 64) + 0.08
-        else: c = CYCLE * max(64, n * (2 if kind == "tt" and not psum else 0.5 if narrow else 1))
+        elif q == "g": c = 0.18 + 2 * CYCLE * n
+        elif q == "s": c = CYCLE * max(n, 64) + 0.1
+        else: c = 0.01 + CYCLE * max(64, n * (2 if kind == "tt" and not psum else 0.5 if narrow else 1))
         put(q, issue, reads, writes, c)
 
-    def dma(q, pairs, reads, writes, late=2.2):
+    def dma(q, pairs, reads, writes, late=2.2, add=False):
         def issue():
             order(q, reads, writes)
             s = "d%d" % ndma[0]
             ndma[0] += 1
             for o, i in pairs:
-                queue[q].dma_start(o, i).then_inc(T.sem[s], 16)
+                (g.dma_start(o, i, accum_op=OP.add) if add else queue[q].dma_start(o, i)).then_inc(T.sem[s], 16)
             count[s] = 16 * len(pairs)
             note(q, s, count[s], reads, writes)
-        put(q, issue, reads, writes, 0.07 * len(pairs), late)
+        put(q, issue, reads, writes, (1.0 if add else 0.07) * len(pairs), late)
 
     def copy(out, a):
         run("v", lambda: g.vector.tensor_copy(ap(out), ap(a)), [a], [out])
@@ -164,17 +170,25 @@ def rank_program(g, core, T, topo):
         if bias is None: run("s", lambda: g.scalar.activation(ap(out), ap(a), AF.Copy, scale=scale), [a], [out])
         else: run("s", lambda: g.scalar.activation(ap(out), ap(a), AF.Identity, bias=bias, scale=scale), [a], [out])
 
+    def either(q):
+        v, s = calls.pop(), calls.pop()
+        calls.append((s if q == "s" else v)[:6] + ((v if q == "s" else s),))
+
     def scaled(q, out, a, scale):
-        if q == "s": act(out, a, scale)
-        else: ts(out, a, scale, OP.mult)
+        act(out, a, scale)
+        ts(out, a, scale, OP.mult)
+        either(q)
 
     def pick(q, out, win, off, scale=1.0):
-        if q == "s": run("s", lambda: g.scalar.activation(ap(out), ind(win, off), AF.Copy, scale=scale), [win, off], [out], "ind")
-        elif scale == 1.0: run("v", lambda: g.vector.tensor_copy(ap(out), ind(win, off)), [win, off], [out], "ind")
+        run("s", lambda: g.scalar.activation(ap(out), ind(win, off), AF.Copy, scale=scale), [win, off], [out], "ind")
+        if scale == 1.0: run("v", lambda: g.vector.tensor_copy(ap(out), ind(win, off)), [win, off], [out], "ind")
         else: run("v", lambda: g.vector.tensor_scalar(ap(out), ind(win, off), scale, None, OP.mult), [win, off], [out], "ind")
+        either(q)
 
     def actb(out, win, off, bias):
         run("s", lambda: g.scalar.activation(ap(out), ind(win, off), AF.Identity, bias=bias), [win, off], [out], "ind")
+        run("v", lambda: g.vector.tensor_scalar(ap(out), ind(win, off), bias, None, OP.add), [win, off], [out], "ind")
+        either("s")
 
     def quant(q, p, a):
         run("v", lambda: g.vector.quantize_mx(ap(q), ap(p), ap(a)), [a], [q, p], "q")
@@ -215,11 +229,11 @@ def rank_program(g, core, T, topo):
         scan(out, data)
         return tab(out)
 
-    def win0(name):
-        return V(name, 16, 16 + C)
+    def win0(name, k):
+        return V(name, 16, 16 + C + k)
 
-    def place(name, k, e):
-        return V(name, 16 + e - k, 16 + e - k + C - 1, 2)
+    def place(name, e, s=0):
+        return V(name, 16 + e + s, 16 + e + s + C - 1, 2)
 
     def wf(b):
         return V("wf", b * WD, (b + 1) * WD)
@@ -247,45 +261,61 @@ def rank_program(g, core, T, topo):
     dma("y", [(T.vt[:], T.v[:])], [], [V("vt")], 5.0)
 
     iota(V("pcol"), [[0, 8]], 0, 1)
-    iota(V("iota"), [[1, C]], -B, 0)
-    iota(V("j16"), [[1, 16]], 0, 0)
-    iota(V("kpat"), [[32, 10], [0, 2]], 1, 0)
-    iota(V("uli"), [[16, 8]], 0, 0)
     fill(V("ones"), 1.0)
     run("g", lambda: g.affine_select(T.ect[:], T.ones[:], [[1, 516]], OP.is_equal, 0.0, -3, -4), [V("ones")], [V("ect")])
-    pm, pm1, pm2 = tmp(1), tmp(1), tmp(1)
+    one = V("ones", 0, C)
+    run("v", lambda: g.vector.tensor_tensor_scan(T.iota[:], ap(one), ap(one), -1.0 - B, OP.mult, OP.add), [one], [V("iota")])
+    pm, pm0, pm1, pm2 = tmp(1), tmp(1), tmp(1), tmp(1)
     ts(V("pcol2"), V("pcol"), 15, OP.bitwise_and)
     copy(pm, V("pcol2", 0, 1))
-    ts(pm1, V("pcol2", 0, 1), 1.0, OP.add)
-    ts(pm2, V("pcol2", 0, 1), 2.0, OP.mult)
+    ts(pm0, V("pcol2", 0, 1), -float(B), OP.add)
+    ts(pm1, V("pcol2", 0, 1), 1.0 - B, OP.add)
+    ts(pm2, V("pcol2", 0, 1), 2.0, OP.mult, float(B), OP.add)
     k1, k2, lanes = tmp(16), tmp(16), lst(20)
-    ts(k1, V("j16"), pm, OP.not_equal)
-    ts(k2, V("j16"), pm1, OP.is_equal, BIG, OP.mult)
+    ts(k1, V("iota", 0, 16), pm0, OP.not_equal)
+    ts(k2, V("iota", 0, 16), pm1, OP.is_equal, BIG, OP.mult)
     tt(V("k16"), k1, k2, OP.add)
-    ts(lanes, V("kpat"), 0.0, OP.mult, pm, OP.add)
+    ts(lanes, V("iota", 0, 20), 0.0, OP.mult, pm, OP.add)
     pick("s", V("kk"), V("k16"), lanes)
-    w, iw, iw2, iw1k, wv, wp0, wlo, w1k, no0 = [tmp(1) for k in range(9)]
+    shift = [lst(2), lst(2)]
+    for t, (edge, far, near) in enumerate(((0.0, 48.0, -1.0), (15.0, 16.0, 1.0))):
+        fill(V("go%d" % t), 0.0)
+        if ON["shift"] != "v": continue
+        c1, c2 = tmp(1), tmp(1)
+        ts(c1, pm, edge, OP.is_equal, far, OP.mult)
+        ts(c2, c1, pm, OP.add, B + near, OP.add)
+        ts(shift[t], V("iota", 0, 32, 16), c2, OP.add)
+    w, iw, iw2, iw1k, wv, wlo, w1k, no0 = [tmp(1) for k in range(8)]
     ts(w, pm, 15.0, OP.is_lt, BIG, OP.mult)
     ts(w, w, 1.0, OP.max)
     ts(iw, pm, 15.0, OP.is_equal, 1.0 / BIG, OP.max)
     ts(iw2, iw, 2.0, OP.mult)
     ts(iw1k, iw, 1.0 / 1024, OP.mult)
     ts(wv, w, 1025.0 * B, OP.mult)
-    ts(wp0, w, float(B - PB), OP.mult)
     ts(wlo, w, float(B - PB), OP.mult)
     ts(w1k, w, 1000.0, OP.mult)
     ts(no0, pm, 0.0, OP.is_gt)
-    KB = [tmp(20), tmp(20)]
-    ts(sub(KB[0], 0, 10), V("kpat", 0, 19, 2), pm2, OP.add)
-    ts(sub(KB[0], 10, 20), V("kpat", 0, 19, 2), pm2, OP.add)
-    ts(KB[1], KB[0], -1.0, OP.add)
+    KB = tmp(20)
+    ts(sub(KB, 0, 10), V("iota", 1, C, 32), pm2, OP.add)
+    ts(sub(KB, 10, 20), V("iota", 1, C, 32), pm2, OP.add)
+    fill(V("d0"), 1.0)
+    fill(V("d0", 0, 120, 6), 0.0)
+    fill(V("d0", 2, 120, 6), -1.0)
+    six = lst(8)
+    iota(V("six", 120, 128), [[0, 8]], B, 0)
+    for j in range(6):
+        far = 10 * (j // 2 % 2)
+        for e in range(2):
+            at = (10 * e + far) % 20
+            iota(V("six", 60 * e + j, 60 * e + 60, 6), [[16 if j % 2 else 1, 10]], 16 * at + 15 - B if j % 2 else B + at, 0)
+    ts(six, table(V("six", 0, 128), 128), iw, OP.mult, float(B), OP.add)
     act(V("cw"), V("iota"), 1024.0)
     act(V("cw", B, B + 1), V("iota", B, B + 1), 0.0, 1.0)
-    for v in [V("tp1", 328, 352), V("dr1", 328, 352)] + [V("wf", b * WD + C, (b + 1) * WD) for b in range(4)]:
+    for v in [V("tp1", 328, 352), V("dr1", 328, 352), V("er0", 0, 24), V("tq1", B, B + 16)] + [V("wf", b * WD + C, (b + 1) * WD) for b in range(4)]:
         act(v, V("iota", 0, v[2] - v[1]), 0.0)
     for b in range(4):
         quant(cols("eq", b), cols("ep", b), V("ect", 3 - b, 515 - b))
-    copy(V("ulu"), V("uli"))
+    ts(V("ulu"), V("iota", 0, 128, 16), float(B), OP.add)
 
     onat, mnat, mu = lst(20), lst(20), [lst(20) for k in range(4)]
     copy(onat, V("oi"))
@@ -294,8 +324,6 @@ def rank_program(g, core, T, topo):
     ts(sub(mu[0], 0, 10), V("mi", 0, 10), -float(B), OP.add)
     copy(sub(mu[0], 10, 20), V("mi", 10, 20))
     pick("s", V("orow"), V("iota"), onat)
-    pick("s", V("mrow"), V("iota"), mnat)
-    pick("s", V("xrow"), V("mrow"), onat)
     for h in range(2):
         pick(ON["pm%d" % h], half("pmrow", h), V("prow"), sub(mnat, 10 * h, 10 * h + 10))
     for h in range(2):
@@ -307,33 +335,34 @@ def rank_program(g, core, T, topo):
             scan(sub(out, B * e, B * e + B), V(name, e if first else 1 - e, C - 1 + (e if first else 1 - e), 2))
         return tab(out)
 
-    ts(V("cur0", 20, 40), couples("orow", True), iw2, OP.mult, 1.0, OP.add)
-    M0 = couples("Mrow", False)
-    ts(V("cur0", 60, 80), M0, iw, OP.mult, float(B), OP.add)
-    x0, val0 = tmp(20), tmp(20)
-    ts(x0, couples("xrow", False), 1024.0, OP.mult, wv, OP.add)
-    tt(val0, x0, M0, OP.add)
+    ts(V("cur0", 32, 52), couples("orow", True), iw2, OP.mult, 1.0, OP.add)
+    M0w = couples("Mrow", False)
+    ts(V("vi0", 20, 40), M0w, iw, OP.mult, float(B), OP.add)
     p0 = table(V("prow"))
     P, pu = tmp(20), lst(20)
-    ts(P, p0, wp0, OP.add)
+    ts(P, p0, wlo, OP.add)
     ts(pu, p0, iw, OP.mult, float(B), OP.add)
 
     quant(V("uq"), V("up"), V("ut"))
     run("s", lambda: g.scalar.activation(T.up16[:], T.up[:].indirect(T.ulu[:]), AF.Copy), [V("up"), V("ulu")], [V("up16")], "ind")
     run("v", lambda: g.vector.tensor_copy(T.uq16[:].bitcast(dt.uint32), T.uq[:].bitcast(dt.uint32).indirect(T.ulu[:])), [V("uq"), V("ulu")], [V("uq16")], "ind")
 
-    def static(t, val):
+    def static(t):
         k = t % 2
         cur = V("cur%d" % t)
         a = 1 if t < 2 else 0
-        oA, oB = sub(cur, 30 - 10 * a, 40 - 10 * a), sub(cur, 20 + 10 * a, 30 + 10 * a)
-        M, uM = sub(cur, 60, 80), sub(cur, 40, 60)
-        if val is None:
-            ts(M, sub(cur, 0, 20), 1023, OP.bitwise_and)
-        tt(uM, M, KB[k], OP.subtract)
+        oA, oB = sub(cur, 42 - 10 * a, 52 - 10 * a), sub(cur, 32 + 10 * a, 42 + 10 * a)
+        vi = V("vi%d" % t)
+        M, uM = sub(vi, 20, 40), sub(cur, 52, 72)
+        if t:
+            copy(sub(vi, 0, 20), sub(cur, 0, 20))
+            ts(M, sub(vi, 0, 20), 1023, OP.bitwise_and)
+        ts(sub(vi, 40, 60), sub(vi, 0, 20) if t else M, 1023, OP.bitwise_and, 1, OP.logical_shift_right)
+        tt(uM, M, KB, OP.subtract)
         d, pr, nb, dob, oA2, mn, mn2, S, ix = tmp(30), tmp(30), tmp(10), tmp(10), tmp(10), tmp(10), tmp(10), tmp(10), tmp(10)
-        oAu, oBu, ixu, Mu = lst(10), lst(10), lst(10), lst(20)
-        lo, hi = sub(cur, 20, 50), sub(cur, 30, 60)
+        oAu, oBu, ixu, Mu2 = lst(10), lst(10), lst(10), lst(40)
+        Mu = sub(Mu2, 0, 20)
+        lo, hi = sub(cur, 32, 62), sub(cur, 42, 72)
         if a: tt(d, hi, lo, OP.subtract)
         else: tt(d, lo, hi, OP.subtract)
         do = sub(d, 0, 10)
@@ -348,52 +377,62 @@ def rank_program(g, core, T, topo):
         ts(S, mn2, 0.0, OP.is_gt)
         ts(oAu, oA2, 0.5, OP.mult, 159.5, OP.add)
         tt(ix, do, S, OP.mult)
-        copy(Mu, M)
+        copy(Mu2, sub(vi, 20, 60))
         ts(ixu, ix, 0.5, OP.mult, float(B), OP.add)
-        if val is None:
-            val = tmp(20)
+        val = V("uv%d" % t, C, C + 20)
+        if t:
             ts(val, sub(cur, 0, 20), w, OP.mult)
+        else:
+            x0 = tmp(20)
+            pick(ON["x0"], V("xrow"), V("orow"), Mu)
+            ts(x0, table(V("xrow")), 1024.0, OP.mult, wv, OP.add)
+            tt(val, x0, M0w, OP.add)
         dr = "dr%d" % t
-        pick("s", place(dr, k, 0), V("cw"), ixu)
-        pick(ON["dr1"], place(dr, k, 1), V("cw"), ixu)
-        pick(ON["dm"], V("dm%d" % t), win0(dr), Mu)
-        return dict(a=a, dob=dob, S=S, oA=oA, oB=oB, oAu=oAu, oBu=oBu, Mu=Mu, val=val)
+        pick("s", place(dr, 0), V("cw"), ixu)
+        pick(ON["dr1"], place(dr, 1), V("cw"), ixu, -1.0)
+        pick(ON["dm"], V("dm%d" % t), win0(dr, k), Mu)
+        return dict(a=a, dob=dob, S=S, oA=oA, oB=oB, oAu=oAu, oBu=oBu, Mf=sub(Mu2, 20, 40))
 
     FB = [[0, 1, 2, 3], [5, 6, 7, 0]]
 
-    def products(src, h):
+    def products(src, h, z):
         q, p = half("xq", h), half("xp", h)
         quant(q, p, half(src, h, 0, 4))
         mm(bank(4), V("uq16"), V("up16"), q, p)
-        act(half("sc", h), bank(4))
+        scaled(ON["sc%d" % z], half("sc", h), bank(4), 1.0)
         for b in range(4):
-            mm(bank(FB[h][b]), cols("eq", b), cols("ep", b), q, p)
-            act(wfF(b, h), bank(FB[h][b]), 0.5)
+            mm(bank(FB[z][b]), cols("eq", b), cols("ep", b), q, p)
+            scaled("s", wfF(b, h), bank(FB[z][b]), 0.5)
 
-    r = static(0, val0)
-    products("x0", 0)
-    products("x0", 1)
+    def turned(out, a):
+        run("v", lambda: g.vector.transpose(ap(out), ap(a)), [a], [out])
+
+    def part(name, h, b):
+        return V(name, (4 * h + b) * B, (4 * h + b + 1) * B)
+
+    r = static(0)
+    products("x0", 0, 0)
+    products("x0", 1, 1)
     for t in range(3):
         k = t % 2
         nl = 5 + k
         a = r["a"]
         tp, er = "tp%d" % t, "er%d" % t
         pick(ON["sb"], V("sb"), V("sc"), r["oBu"])
-        tti(place(tp, k, 0), V("sc"), r["oAu"], V("sb"), OP.is_gt)
-        ts(place(tp, k, 1), place(tp, k, 0), -1.0, OP.mult)
-        ur, tc, rr, alt, dd, d2, e, eu = row(), tmp(10), tmp(10), tmp(20), tmp(10), tmp(10), tmp(20), lst(20)
-        tcw = table(place(tp, k, 0), B)
-        tti(ur, win0(tp), r["Mu"], V("dm%d" % t), OP.mult)
-        ts(tc, tcw, iw, OP.mult, 0.5, OP.is_gt)
-        u = table(ur)
-        tt(rr, tc, r["S"], OP.is_gt)
-        tt(alt, r["val"], u, OP.add)
+        tq = "tq%d" % t
+        tti(V(tq, 0, B), V("sc"), r["oAu"], V("sb"), OP.is_gt)
+        ur, tc, eu, uv, e = row(), tmp(10), lst(20), "uv%d" % t, V("ne%d" % t, 5, 120, 6)
+        tti(ur, V(tq, 0, B + k), r["Mf"], V("dm%d" % t), OP.mult)
+        ts(tc, table(V(tq, 0, B), B), iw, OP.mult, 0.5, OP.is_gt)
+        scan(V(uv, 0, C), ur)
+        for z in range(2):
+            tt(V("d0", 60 * z + 4, 60 * z + 60, 6), tc, r["S"], OP.is_gt)
+        pick("v", V("d1"), V(uv), six)
+        run("v", lambda t=t: g.vector.tensor_tensor_scan(T["ne%d" % t][:], T.d0[:], T.d1[:], 0.0, OP.mult, OP.add), [V("d0"), V("d1")], [V("ne%d" % t)])
         A, Bv = (10 * a, 10 * a + 10), (10 - 10 * a, 20 - 10 * a)
-        tt(dd, sub(alt, *Bv), sub(alt, *A), OP.subtract)
-        tt(d2, dd, rr, OP.mult)
-        tt(sub(e, *A), sub(alt, *A), d2, OP.add)
-        tt(sub(e, *Bv), sub(alt, *Bv), d2, OP.subtract)
         ts(eu, e, iw1k, OP.mult)
+        for z in range(2):
+            scaled(ON["tp"], place(tp, z), V(tq, 0, B), 1.0 - 2.0 * z)
         euA, euB = sub(eu, *A), sub(eu, *Bv)
         for b in range(4):
             pick("s", V("et", b, 128 * nl - 7 + b, 8), wfF(b), sub(euA, 0, nl), 2.0)
@@ -414,69 +453,84 @@ def rank_program(g, core, T, topo):
             log[lq[0]] = [(lq, arr, full, True, "r")]
             log[lp[0]] = [(lp, arr, full, True, "r")]
 
-        put("g", send, [qe, pe], [lq, lp], 1.0, 2.2)
+        put("g", send, [qe, pe], [lq, lp], 0.6 + 0.8 * (t == 0), 1.7)
         t1 = tmp(10)
         tt(t1, tc, r["dob"], OP.mult)
         if t < 2:
-            nx, go = V("cur%d" % (t + 1)), V("go%d" % t, 0, 20)
+            nx, go, tw, tn = V("cur%d" % (t + 1)), V("go%d" % t), V("tw%d" % t), V("tn%d" % t)
             stay, move = (A, Bv) if t == 0 else (Bv, A)
-            ts(sub(go, 0, 10), sub(e, *move), iw, OP.mult)
-            ts(sub(nx, 0, 10), sub(e, *stay), iw, OP.mult)
-            tt(sub(nx, 30, 40) if t == 0 else sub(go, 10, 20), r["oA"], t1, OP.add)
-            tt(sub(go, 10, 20) if t == 0 else sub(nx, 30, 40), r["oB"], t1, OP.subtract)
-            s, h = T[go[0]], T[nx[0]]
-            pairs = []
-            for q in range(0, 128, 16):
-                pairs.append((h[q + 1:q + 16, 10:30], s[q:q + 15, 0:20]) if t == 0 else (h[q:q + 15, 10:30], s[q + 1:q + 16, 0:20]))
-            for z in (0, 10):
-                if t == 0:
-                    pairs.append((h[0:128:16, z + 11:z + 20], s[15:128:16, z:z + 9]))
-                    pairs.append((h[0:128:16, z + 10:z + 11], s[15:128:16, z + 9:z + 10]))
-                else:
-                    pairs.append((h[15:128:16, z + 10:z + 19], s[0:128:16, z + 1:z + 10]))
-                    pairs.append((h[15:128:16, z + 19:z + 20], s[0:128:16, z:z + 1]))
-            dma("y", pairs, [go], [sub(nx, 0, 40)])
+            z = 1 - t
+            ts(sub(go, z, z + 10), sub(e, *move), iw, OP.mult, 1.0 - 2.0 * t, OP.add)
+            ts(sub(nx, 0, 10), sub(e, *stay), iw, OP.mult, 1.0 - 2.0 * t, OP.add)
+            tt(sub(nx, 42, 52) if t == 0 else sub(go, 22, 32), r["oA"], t1, OP.add)
+            tt(sub(go, 23, 33) if t == 0 else sub(nx, 42, 52), r["oB"], t1, OP.subtract)
+            if ON["shift"] == "v":
+                copy(sub(go, 10 * t, 10 * t + 23, 22), sub(go, 10 * z, 10 * z + 23, 22))
+                turned(sub(tw, 0, 32), sub(go, z, z + 32))
+                turned(sub(tw, 32, 64), sub(go, t, t + 32))
+                pick("v", tn, tw, shift[t])
+                turned(sub(nx, 10, 42), tn)
+            else:
+                sv, hv, pairs = T[go[0]], T[nx[0]], []
+                for q in range(0, 128, 16):
+                    pairs.append((hv[q + 1:q + 16, 10:42], sv[q:q + 15, 1:33]) if t == 0 else (hv[q:q + 15, 10:42], sv[q + 1:q + 16, 0:32]))
+                for y in (0, 22):
+                    if t == 0:
+                        pairs.append((hv[0:128:16, y + 11:y + 20], sv[15:128:16, y + 1:y + 10]))
+                        pairs.append((hv[0:128:16, y + 10:y + 11], sv[15:128:16, y + 10:y + 11]))
+                    else:
+                        pairs.append((hv[15:128:16, y + 10:y + 19], sv[0:128:16, y + 1:y + 10]))
+                        pairs.append((hv[15:128:16, y + 19:y + 20], sv[0:128:16, y:y + 1]))
+                dma("y", pairs, [go], [sub(nx, 0, 52)])
         else:
             of, ofu = tmp(20), lst(20)
             tt(sub(of, 0, 10), r["oA"], t1, OP.add)
             tt(sub(of, 10, 20), r["oB"], t1, OP.subtract)
             ts(ofu, of, 0.5, OP.mult, 159.5, OP.add)
         fr, mr = row(), row()
-        pick(ON["p"], fr, win0(tp), pu)
-        pick("s", place(er, k, 0), V("iota"), euA)
-        pick("s", place(er, k, 1), V("iota"), euB)
-        if k: act(V(er, 16 + C - 1, 16 + C), V(er, 15, 16))
+        kn = (t + 1) % 2 if t < 2 else 0
+        pick(ON["p"], fr, win0(tp, k), pu)
+        pick("s", place(er, 0, kn - k), V("iota"), euA)
+        pick("s", place(er, 1, kn - k), V("iota"), euB)
+        if k: scaled("v", V(er, 16 + C - 1, 16 + C), V(er, 15, 16), 1.0)
         pn, pf, pz, pu = tmp(20), tmp(20), tmp(20), lst(20)
         tt(pn, P, table(fr), OP.add)
         P = pn
-        ts(pu, pn, iw, OP.mult, float(PB), OP.add)
+        ts(pu, pn, iw, OP.mult, float(PB + kn), OP.add)
         ts(pf, pn, wlo, OP.is_lt, w1k, OP.mult)
         tt(pz, pf, pn, OP.add)
-        pick(ON["mn"], mr, win0(er), pu)
+        pick(ON["mn"], mr, win0(er, kn), pu)
         mn = table(mr)
         vm, vl = tmp(20), lst(20)
         tt(vm, pz, mn, OP.max)
         ts(vl, vm, iw, OP.mult, float(B), OP.add)
         ts(sub(mu[t + 1], 0, 10), sub(mn, 0, 10), iw, OP.mult)
         ts(sub(mu[t + 1], 10, 20), sub(mn, 10, 20), iw, OP.mult, float(B), OP.add)
-        for h in (1, 0):
+        early = 1 - k if ALT else 1
+        for h in (early, 1 - early):
             for b in range(4):
-                pick("s", half("ah", h, b), wfF(b, 1 - h), sub(mu[t], 10 * h, 10 * h + 10))
+                pick("s", part("ah", h, b), wfF(b, 1 - h), sub(mu[t], 10 * h, 10 * h + 10))
+            ah, af = half("ah", h, 0, 4), half("af", h, 0, 4)
+            q = ON["af%d" % (h != early)]
+            if q == "d":
+                dma("y", [(ap(af), ap(ah))], [ah], [af])
+                dma("g", [(ap(af), ap(ah))], [ah, af], [af], 2.5, True)
+            else:
+                scaled(q, af, ah, 2.0)
+        zs = (1 - early, early) if ALT else (1, 0)
         for b in range(4):
             mm(bank(b, ne), cols("eq", b), cols("ep", b), lq, lp)
-            act(V("wf", b * WD + C + 1 - k, b * WD + C + 1 - k + ne), bank(b, ne), 0.5)
-        for z in range(2):
-            scaled(ON["af%d" % z], V("af", 2 * C * z, 2 * C * z + 2 * C), V("ah", 2 * C * z, 2 * C * z + 2 * C), 2.0)
-        for h in (1, 0):
+            scaled("s", V("wf", b * WD + C + 1 - k, b * WD + C + 1 - k + ne), bank(b, ne), 0.5)
+        for z, h in enumerate(zs):
             for b in range(4):
-                tti(el("zt", b, h), wf(b), sub(vl, 10 * h, 10 * h + 10), half("ah", h, b), OP.add)
+                tti(el("zt", b, h), wf(b), sub(vl, 10 * h, 10 * h + 10), part("ah", h, b), OP.add)
             quant(half("zq", h), half("zp", h), half("zt", h, 0, 4))
             for b in range(4):
-                n = 4 * (1 - h) + b
+                n = 4 * z + b
                 mm(bank(n), cols("wq", b), cols("wp", b), half("zq", h), half("zp", h))
-                act(half("gs", h, b), bank(n), 0.0078125)
+                scaled("s", half("gs", h, b), bank(n), 0.0078125)
         if t < 2:
-            r = static(t + 1, None)
+            r = static(t + 1)
         else:
             quant(V("vq"), V("vp"), V("vt"))
             actb(V("romo", 0, C - 1, 2), V("iota"), sub(ofu, 0, 10), float(B))
@@ -484,44 +538,60 @@ def rank_program(g, core, T, topo):
             for h in range(2):
                 actb(half("romm", h), V("iota"), sub(mu[3], 10 * h, 10 * h + 10), float(C - B * h))
             dma("y", [(T.om[:, 0:C], T.romo[0:128:16, :]), (T.om[:, C:2 * C], T.romm[0:128:16, :])], [V("romo"), V("romm")], [])
-        for h in range(2):
+        for z, h in enumerate(zs[::-1]):
             for b in range(4):
-                tti(el("xt", b, h), half("gs", 1 - h, b), sub(mu[t + 1], 10 * h, 10 * h + 10), half("af", h, b), OP.add)
+                tti(el("xt", b, h), half("gs", 1 - h, b), sub(mu[t + 1], 10 * h, 10 * h + 10), part("af", h, b), OP.add)
             if t < 2:
-                products("xt", h)
+                products("xt", h, z)
             else:
                 q, p = half("xq", h), half("xp", h)
                 quant(q, p, half("xt", h, 0, 4))
                 mm(bank(h), V("vq"), V("vp"), q, p)
                 dma("y", [(T.oc[:, 4 * B * h:4 * B * h + 4 * B], by(q))]
                     + [(T.osc[4 * z:4 * z + 4, B * h:B * h + B], T.xp[32 * z:32 * z + 4, B * h:B * h + B]) for z in range(4)], [q, p], [], 2.5)
-                act(half("ysb", h), bank(h))
+                scaled("s", half("ysb", h), bank(h), 1.0)
                 dma("s", [(T.y[:, B * h:B * h + B], ap(half("ysb", h)))], [half("ysb", h)], [], 2.5)
     if "plan" not in PLAN:
         seen, before = {}, []
-        for i, (q, issue, reads, writes, cost, late) in enumerate(calls):
+        for i, (q, issue, reads, writes, cost, late, other) in enumerate(calls):
             p = set()
             for vs, isw in ((reads, False), (writes, True)):
                 for v in vs:
-                    psum = v[0][:2] == "ps"
-                    for wv_, j, oldw in seen.get(v[0], ()):
-                        if (isw or oldw or (psum and calls[j][0] != q)) and (psum or clash(v, wv_)): p.add(j)
+                    for old, j, oldw in seen.get(v[0], ()):
+                        if v[0][:2] == "ps" or ((isw or oldw) and clash(v, old)): p.add(j)
             for vs, isw in ((reads, False), (writes, True)):
                 for v in vs: seen.setdefault(v[0], []).append((v, i, isw))
             before.append(sorted(p))
-        PLAN["plan"] = plan([(c[0], c[4], c[5]) for c in calls], before)
-    for i in PLAN["plan"]:
-        calls[i][1]()
+        PLAN["plan"] = plan([(c[0], c[4], c[5]) for c in calls], before, [c[6] and (c[6][0], c[6][4]) for c in calls])
+    for i, q in PLAN["plan"]:
+        (calls[i] if calls[i][0] == q else calls[i][6])[1]()
     for sem, n in count.items():
         know("g", sem, n)
 
 
 PLAN = {}
-WAKE, OWN = 0.08, 0.06
-AHEAD = 0.12
+WAKE, OWN = 0.22, 0.17
+PASSES = 6
 
 
-def plan(ops, before):
+def lay(ops, before, rank, back):
+    at, busy = [0.0] * len(ops), {q: [] for q in "vstgy"}
+    for i in rank:
+        q, cost, late = ops[i]
+        t = late if back and not before[i] else 0.0
+        for j in before[i]:
+            p = i if back else j
+            t = max(t, at[j] + ops[j][1] + ops[p][2] + (OWN if ops[j][0] == q and not ops[p][2] else WAKE))
+        k, row = 0, busy[q]
+        for k in range(len(row) + 1):
+            if k == len(row) or t + cost <= row[k][0] + 1e-9: break
+            t = max(t, row[k][1])
+        row.insert(k, (t, t + cost))
+        at[i] = t
+    return at
+
+
+def plan(ops, before, other):
     n = len(ops)
     after = [[] for i in range(n)]
     for i in range(n):
@@ -529,26 +599,93 @@ def plan(ops, before):
     urge = [0.0] * n
     for i in range(n - 1, -1, -1):
         urge[i] = ops[i][1] + ops[i][2] + max([urge[j] + WAKE for j in after[i]] + [0.0])
-    left = [len(b) for b in before]
-    ready = [i for i in range(n) if not left[i]]
-    end, free, last, out = {}, {q: 0.0 for q in "vstgy"}, {q: -1 for q in "vstgy"}, []
+    rank, best = sorted(range(n), key=lambda i: (-urge[i], i)), None
+    for turn in range(PASSES):
+        at = lay(ops, before, rank, False)
+        end = max(at[i] + ops[i][1] + ops[i][2] for i in range(n))
+        if best is None or end < best[0]: best = (end, at)
+        late = lay(ops, after, sorted(range(n), key=lambda i: (-at[i] - ops[i][1], -i)), True)
+        rank = sorted(range(n), key=lambda i: (-late[i] - ops[i][1], i))
+    PLAN["end"] = best[0]
+    return polish(ops, before, after, other, sorted(range(n), key=lambda i: (best[1][i], i)))
 
-    def start(i):
-        q = ops[i][0]
-        return max([free[q]] + [end[j] + ((OWN if j == last[q] else 0.0) if ops[j][0] == q and not ops[j][2] else WAKE) for j in before[i]])
 
-    while ready:
-        at = {i: start(i) for i in ready}
-        first = min(ready, key=lambda i: (at[i], -urge[i]))
-        q = ops[first][0]
-        i = max([j for j in ready if ops[j][0] == q and at[j] <= at[first] + AHEAD], key=lambda j: (urge[j] - at[j], -j))
-        ready.remove(i)
-        out.append(i)
-        free[q] = at[i] + ops[i][1]
-        end[i] = free[q] + ops[i][2]
-        last[q] = i
-        for j in after[i]:
-            left[j] -= 1
-            if not left[j]: ready.append(j)
-    PLAN["end"] = max(end.values())
-    return out
+MACHINES = [(1.0, 0.0, 0.17, 0.2, True), (1.0, -0.3, 0.17, 0.23, False), (1.35, 1.3, 0.15, 0.2, False)]
+TRIES = 200000
+
+
+def polish(ops, before, after, other, seq):
+    n = len(ops)
+    qn = ["vstgy".index(o[0]) for o in ops]
+    known, need = [0] * n, []
+    for i in range(n):
+        keep, a = [], 0
+        for j in sorted(before[i], reverse=True):
+            if not (a >> j) & 1:
+                keep.append(j)
+                a |= known[j] | (1 << j)
+        known[i] = a
+        need.append(keep)
+    sets = []
+    for fac, more, own, wake, hide in MACHINES:
+        cost = [{qn[i]: ops[i][1] * (fac if ops[i][0] in "vst" else 1.0)} for i in range(n)]
+        for i in range(n):
+            if other[i]: cost[i]["vs".index(other[i][0])] = other[i][1] * fac
+        sets.append((cost, [o[2] + more if o[2] else 0.0 for o in ops], own, wake, hide))
+
+    def walk(seq, lo, end, m):
+        cost, late, own, wake, hide = m
+        free, k, left = [0.0] * 5, lo - 1, set(range(5))
+        while left and k >= 0:
+            i = seq[k]
+            if qn[i] in left:
+                left.discard(qn[i])
+                free[qn[i]] = end[i] - late[i]
+            k -= 1
+        end = list(end)
+        for i in seq[lo:]:
+            q = qn[i]
+            t = f = free[q]
+            for j in need[i]:
+                e = end[j]
+                if e + wake > t and (e >= f - 1e-9 or not hide):
+                    e += own if qn[j] == q else wake
+                    if e > t: t = e
+            t += cost[i][q]
+            free[q] = t
+            end[i] = t + late[i]
+        return end
+
+    ends = [walk(seq, 0, [0.0] * n, m) for m in sets]
+    base = [max(e) for e in ends]
+    now, rng = 1.0, np.random.RandomState(4)
+    best = (now, seq, list(qn))
+    pos = [0] * n
+    for k, i in enumerate(seq): pos[i] = k
+    for turn in range(TRIES):
+        a = int(rng.randint(n))
+        i = seq[a]
+        lo = max([pos[j] for j in before[i]] + [-1]) + 1
+        hi = min([pos[j] for j in after[i]] + [n]) - 1
+        b = a + int(rng.randint(1, 30)) * (1 if rng.rand() < 0.5 else -1)
+        b = max(lo, min(hi, b))
+        lim = now - 0.0005 * max(0.0, 1.0 - 1.2 * turn / TRIES) * math.log(rng.rand() + 1e-12)
+        flip = other[i] and rng.rand() < 0.3
+        if flip: qn[i] = 1 - qn[i]
+        elif b == a or not [j for j in seq[min(a, b):max(a, b) + 1] if j != i and qn[j] == qn[i]]: continue
+        new = seq[:a] + seq[a + 1:]
+        new.insert(b, i)
+        total, got = 0.0, []
+        for m, e, w in zip(sets, ends, base):
+            got.append(walk(new, min(a, b), e, m))
+            r = max(got[-1]) / w
+            total += r / len(sets)
+            if r > lim + 0.03: total += 9.0
+            if total > lim: break
+        if total <= lim:
+            now, seq, ends = total, new, got
+            for k in range(min(a, b), max(a, b) + 1): pos[seq[k]] = k
+            if now < best[0]: best = (now, seq, list(qn))
+        elif flip: qn[i] = 1 - qn[i]
+    PLAN["gain"] = best[0]
+    return [(i, "vstgy"[best[2][i]]) for i in best[1]]

@@ -4,7 +4,7 @@ from concourse.mybir import dt, AluOpType as OP, ActivationFunctionType as AF
 
 C, B = 320, 160
 STEP = [1, 2, 4]
-EW = 176
+EW = 208
 WD = C + EW
 NE = [160, 162, 160]
 F8, BF, F32, U16, U8, I32 = "float8_e4m3fn_x4", "bfloat16", "float32", "uint16", "uint8", "int32"
@@ -22,13 +22,13 @@ SCRATCH = {
     "ect": ("sbuf", [128, 516], BF), "ones": ("sbuf", [128, 516], BF),
     "eq": ("sbuf", [128, 512], F8), "ep": ("sbuf", [128, 512], U8),
     "iota": ("sbuf", [128, C], BF), "cw": ("sbuf", [128, C], BF),
-    "six": ("sbuf", [128, 128], BF), "d0": ("sbuf", [128, 128], F32), "d1": ("sbuf", [128, 128], F32),
+    "six": ("sbuf", [128, 128], BF), "d0": ("sbuf", [128, 128], F32),
     "k16": ("sbuf", [128, 16], BF), "kk": ("sbuf", [128, C], BF),
     "pcol": ("sbuf", [128, 8], I32), "pcol2": ("sbuf", [128, 8], I32), "ulu": ("sbuf", [128, 8], U16),
     "tb": ("sbuf", [128, 3000], F32), "ub": ("sbuf", [128, 1000], U16),
     "orow": ("sbuf", [128, C], BF), "prow": ("sbuf", [128, C], BF),
     "pmrow": ("sbuf", [128, C], BF), "xrow": ("sbuf", [128, C], BF), "Mrow": ("sbuf", [128, C], BF),
-    "wf": ("sbuf", [128, 4 * WD], BF),
+    "wf": ("sbuf", [128, 4 * WD], BF), "w2": ("sbuf", [128, 4 * C], BF), "ft": ("sbuf", [128, 4 * C], BF),
     "ah": ("sbuf", [128, 4 * C], BF), "af": ("sbuf", [128, 4 * C], BF),
     "et": ("sbuf", [128, 4 * 192], BF), "zt": ("sbuf", [128, 4 * C], BF), "xt": ("sbuf", [128, 4 * C], BF),
     "zq": ("sbuf", [128, C], F8), "zp": ("sbuf", [128, C], U8),
@@ -38,20 +38,20 @@ SCRATCH = {
 }
 for _t in range(3):
     for _n, _d in (("qe", F8), ("pe", U8), ("lq", F8), ("lp", U8)):
-        SCRATCH[_n + str(_t)] = ("sbuf", [128, EW], _d)
+        SCRATCH[_n + str(_t)] = ("sbuf", [128, C], _d)
+    SCRATCH["le%d" % _t] = ("sbuf", [128, 20], U16)
     for _n, _w, _d in (("tp", 352, BF), ("dr", 352, BF), ("er", 352, BF), ("dm", C, BF), ("cur", 72, F32),
-                       ("uv", C + 20, F32), ("ne", 128, F32), ("vi", 60, I32), ("tq", B + 16, BF)):
+                       ("d1", 128, F32), ("ne", 128, F32), ("vi", 60, I32), ("tq", B + 16, BF)):
         SCRATCH[_n + str(_t)] = ("sbuf", [128, _w], _d)
 for _t in range(2):
     for _n, _w, _d in (("go", 40, F32), ("tw", 64, F32), ("tn", 32, F32)):
         SCRATCH[_n + str(_t)] = ("sbuf", [128, _w], _d)
-for _k in range(24):
-    SCRATCH["r%d" % _k] = ("sbuf", [128, C], BF)
+SCRATCH["rows"] = ("sbuf", [128, 28 * C], BF)
 for _k in range(8):
     SCRATCH["ps%d" % _k] = ("psum", [128, 512], F32)
-SEMAPHORES = ["vs", "ss", "ts", "gs"] + ["d%d" % k for k in range(24)] + ["arr%d" % k for k in range(3)] + ["loc%d" % k for k in range(3)]
+SEMAPHORES = ["vs", "ss", "ts", "gs"] + ["d%d" % k for k in range(32)] + [s + "%d%d" % (t, k) for s in ("arr", "loc") for t in range(3) for k in range(3)]
 ON = {"sb": "s", "p": "s", "mn": "s", "dm": "s", "af0": "s", "af1": "v", "pm0": "v", "pm1": "s", "M0": "v", "M1": "s", "dr1": "s",
-      "x0": "s", "sc0": "s", "sc1": "v", "tp": "v", "shift": "d"}
+      "x0": "s", "sc0": "s", "sc1": "v", "tp": "v", "shift": "d", "F": "halves", "E": "F"}
 ALT = True
 
 
@@ -174,10 +174,14 @@ def rank_program(g, core, T, topo):
         v, s = calls.pop(), calls.pop()
         calls.append((s if q == "s" else v)[:6] + ((v if q == "s" else s),))
 
-    def scaled(q, out, a, scale):
-        act(out, a, scale)
-        ts(out, a, scale, OP.mult)
+    def scaled(q, out, a, scale, bias=None):
+        act(out, a, scale, bias)
+        if bias is None: ts(out, a, scale, OP.mult)
+        else: ts(out, a, scale, OP.mult, bias, OP.add)
         either(q)
+
+    def const(out, c):
+        scaled("s", out, V("ones", 0, (out[2] - out[1] + out[3] - 1) // out[3]), c)
 
     def pick(q, out, win, off, scale=1.0):
         run("s", lambda: g.scalar.activation(ap(out), ind(win, off), AF.Copy, scale=scale), [win, off], [out], "ind")
@@ -211,7 +215,7 @@ def rank_program(g, core, T, topo):
 
     def row(n=C):
         nrow[0] += 1
-        return V("r%d" % (nrow[0] - 1), 0, n)
+        return V("rows", C * (nrow[0] - 1), C * (nrow[0] - 1) + n)
 
     def sub(v, lo, hi, step=1):
         if v[3] == 1: return (v[0], v[1] + lo, v[1] + hi, step)
@@ -236,7 +240,7 @@ def rank_program(g, core, T, topo):
         return V(name, 16 + e + s, 16 + e + s + C - 1, 2)
 
     def wf(b):
-        return V("wf", b * WD, (b + 1) * WD)
+        return V("wf", b * WD, b * WD + C + 1 + B)
 
     def wfF(b, h=None):
         return V("wf", b * WD, b * WD + C) if h is None else V("wf", b * WD + B * h, b * WD + B * h + B)
@@ -253,10 +257,10 @@ def rank_program(g, core, T, topo):
     def bank(k, n=B):
         return V("ps%d" % k, 0, n)
 
-    dma("y", [(T.oi[:], T.o[:]), (T.mi[:], T.m[:])], [], [V("oi"), V("mi")])
-    dma("s", [(T.x0[:, 0:4 * B], T.x[:, 0:4 * B])], [], [half("x0", 0, 0, 4)], 2.8)
-    dma("y", [(T.ut[:], T.u[:])], [], [V("ut")], 2.8)
-    dma("s", [(T.x0[:, 4 * B:4 * C], T.x[:, 4 * B:4 * C])], [], [half("x0", 1, 0, 4)], 3.2)
+    dma("y", [(T.oi[:], T.o[:]), (T.mi[:], T.m[:])], [], [V("oi"), V("mi")], 1.9)
+    dma("s", [(T.x0[:, 0:4 * B], T.x[:, 0:4 * B])], [], [half("x0", 0, 0, 4)], 2.5)
+    dma("y", [(T.ut[:], T.u[:])], [], [V("ut")], 2.5)
+    dma("s", [(T.x0[:, 4 * B:4 * C], T.x[:, 4 * B:4 * C])], [], [half("x0", 1, 0, 4)], 2.9)
     dma("y", [(by(V("wq")), T.wc[:]), (T.wp[:], T.ws[:])], [], [V("wq"), V("wp")], 4.5)
     dma("y", [(T.vt[:], T.v[:])], [], [V("vt")], 5.0)
 
@@ -268,9 +272,9 @@ def rank_program(g, core, T, topo):
     pm, pm0, pm1, pm2 = tmp(1), tmp(1), tmp(1), tmp(1)
     ts(V("pcol2"), V("pcol"), 15, OP.bitwise_and)
     copy(pm, V("pcol2", 0, 1))
-    ts(pm0, V("pcol2", 0, 1), -float(B), OP.add)
-    ts(pm1, V("pcol2", 0, 1), 1.0 - B, OP.add)
-    ts(pm2, V("pcol2", 0, 1), 2.0, OP.mult, float(B), OP.add)
+    scaled("s", pm0, pm, 1.0, -float(B))
+    scaled("s", pm1, pm, 1.0, 1.0 - B)
+    scaled("s", pm2, pm, 2.0, float(B))
     k1, k2, lanes = tmp(16), tmp(16), lst(20)
     ts(k1, V("iota", 0, 16), pm0, OP.not_equal)
     ts(k2, V("iota", 0, 16), pm1, OP.is_equal, BIG, OP.mult)
@@ -279,40 +283,38 @@ def rank_program(g, core, T, topo):
     pick("s", V("kk"), V("k16"), lanes)
     shift = [lst(2), lst(2)]
     for t, (edge, far, near) in enumerate(((0.0, 48.0, -1.0), (15.0, 16.0, 1.0))):
-        fill(V("go%d" % t), 0.0)
+        const(V("go%d" % t, 8, 24), 0.0)
         if ON["shift"] != "v": continue
         c1, c2 = tmp(1), tmp(1)
         ts(c1, pm, edge, OP.is_equal, far, OP.mult)
         ts(c2, c1, pm, OP.add, B + near, OP.add)
         ts(shift[t], V("iota", 0, 32, 16), c2, OP.add)
     w, iw, iw2, iw1k, wv, wlo, w1k, no0 = [tmp(1) for k in range(8)]
-    ts(w, pm, 15.0, OP.is_lt, BIG, OP.mult)
-    ts(w, w, 1.0, OP.max)
+    ts(no0, pm, 15.0, OP.is_lt)
+    scaled("s", w, no0, BIG, 1.0)
     ts(iw, pm, 15.0, OP.is_equal, 1.0 / BIG, OP.max)
-    ts(iw2, iw, 2.0, OP.mult)
-    ts(iw1k, iw, 1.0 / 1024, OP.mult)
-    ts(wv, w, 1025.0 * B, OP.mult)
-    ts(wlo, w, float(B - PB), OP.mult)
-    ts(w1k, w, 1000.0, OP.mult)
+    scaled("s", iw2, iw, 2.0)
+    scaled("s", iw1k, iw, 1.0 / 1024)
+    scaled("s", wv, w, 1025.0 * B)
+    scaled("s", wlo, w, float(B - PB))
+    scaled("s", w1k, w, 1000.0)
     ts(no0, pm, 0.0, OP.is_gt)
     KB = tmp(20)
     ts(sub(KB, 0, 10), V("iota", 1, C, 32), pm2, OP.add)
     ts(sub(KB, 10, 20), V("iota", 1, C, 32), pm2, OP.add)
-    fill(V("d0"), 1.0)
-    fill(V("d0", 0, 120, 6), 0.0)
-    fill(V("d0", 2, 120, 6), -1.0)
+    const(V("d0", 1, 120, 2), 1.0)
+    const(V("d0", 0, 120, 6), 0.0)
+    const(V("d0", 2, 120, 6), -1.0)
     six = lst(8)
-    iota(V("six", 120, 128), [[0, 8]], B, 0)
-    for j in range(6):
-        far = 10 * (j // 2 % 2)
-        for e in range(2):
-            at = (10 * e + far) % 20
-            iota(V("six", 60 * e + j, 60 * e + 60, 6), [[16 if j % 2 else 1, 10]], 16 * at + 15 - B if j % 2 else B + at, 0)
+    iota(V("six", 60, 128), [[0, 68]], -B, 0)
+    for z, (step, first) in enumerate(((1, 0), (16, 15))):
+        for j in range(3):
+            iota(V("six", 64 * z + j, 64 * z + 60, 3), [[step * (10 - 20 * (j % 2)), 2], [step, 10]], first + 10 * step * (j % 2) - B, 0)
     ts(six, table(V("six", 0, 128), 128), iw, OP.mult, float(B), OP.add)
-    act(V("cw"), V("iota"), 1024.0)
-    act(V("cw", B, B + 1), V("iota", B, B + 1), 0.0, 1.0)
-    for v in [V("tp1", 328, 352), V("dr1", 328, 352), V("er0", 0, 24), V("tq1", B, B + 16)] + [V("wf", b * WD + C, (b + 1) * WD) for b in range(4)]:
-        act(v, V("iota", 0, v[2] - v[1]), 0.0)
+    scaled("s", V("cw"), V("iota"), 1024.0)
+    const(V("cw", B, B + 1), 1.0)
+    for v in [V("tp1", 336, 337), V("dr1", 336, 337), V("er0", 16, 17), V("tq1", B, B + 1), V("wf", C, 4 * WD, WD)]:
+        const(v, 0.0)
     for b in range(4):
         quant(cols("eq", b), cols("ep", b), V("ect", 3 - b, 515 - b))
     ts(V("ulu"), V("iota", 0, 128, 16), float(B), OP.add)
@@ -379,30 +381,60 @@ def rank_program(g, core, T, topo):
         tt(ix, do, S, OP.mult)
         copy(Mu2, sub(vi, 20, 60))
         ts(ixu, ix, 0.5, OP.mult, float(B), OP.add)
-        val = V("uv%d" % t, C, C + 20)
+        val, d1, sv = sub(cur, 0, 20), V("d1%d" % t, 0, 128, 2), sub(six, 0, 4)
         if t:
-            ts(val, sub(cur, 0, 20), w, OP.mult)
+            run("v", lambda: g.vector.tensor_scalar(ap(d1), ind(val, sv), ap(w), None, OP.mult), [val, sv, w], [d1], "ind")
         else:
             x0 = tmp(20)
             pick(ON["x0"], V("xrow"), V("orow"), Mu)
             ts(x0, table(V("xrow")), 1024.0, OP.mult, wv, OP.add)
             tt(val, x0, M0w, OP.add)
+            pick("v", d1, val, sv)
         dr = "dr%d" % t
         pick("s", place(dr, 0), V("cw"), ixu)
-        pick(ON["dr1"], place(dr, 1), V("cw"), ixu, -1.0)
-        pick(ON["dm"], V("dm%d" % t), win0(dr, k), Mu)
+        if t: scaled("v", place(dr, 1), place(dr, 0), -1.0)
+        else: pick("v", place(dr, 1), V("cw"), ixu, -1.0)
+        if t: pick("s", V("dm%d" % t), win0(dr, k), Mu)
+        for h in range(0 if t else 2):
+            pick("sv"[h], half("dm0", h), win0(dr, k), sub(Mu, 10 * h, 10 * h + 10))
         return dict(a=a, dob=dob, S=S, oA=oA, oB=oB, oAu=oAu, oBu=oBu, Mf=sub(Mu2, 20, 40))
 
     FB = [[0, 1, 2, 3], [5, 6, 7, 0]]
 
-    def products(src, h, z):
+    def products(src, h, z, t):
         q, p = half("xq", h), half("xp", h)
         quant(q, p, half(src, h, 0, 4))
         mm(bank(4), V("uq16"), V("up16"), q, p)
         scaled(ON["sc%d" % z], half("sc", h), bank(4), 1.0)
         for b in range(4):
-            mm(bank(FB[z][b]), cols("eq", b), cols("ep", b), q, p)
-            scaled("s", wfF(b, h), bank(FB[z][b]), 0.5)
+            if ON["F"] == "halves":
+                mm(bank(FB[z][b]), cols("eq", b), cols("ep", b), q, p)
+                scaled("s", wfF(b, h), bank(FB[z][b]), 0.5)
+            elif z:
+                mm(bank(b, C), cols("eq", b), cols("ep", b), V("xq"), V("xp"))
+                scaled("s", wfF(b), bank(b, C), 0.5)
+        if ON["E"] == "F":
+            for b in range(4):
+                scaled("v", el("ft", b, h), wfF(b, h), 2.0)
+            qe, pe, lq, lp = [half(s + str(t), h) for s in ("qe", "pe", "lq", "lp")]
+            quant(qe, pe, half("ft", h, 0, 4))
+            send(t, "%d%d" % (t, z), [(lq, qe, True), (lp, pe, False)], 0.6 + 0.8 * (t + z == 0), 1.7)
+
+    def send(t, tag, pairs, cost, late):
+        dst = T.cores[rank ^ STEP[t]]
+        rid, pid = topo.addr(dst)[:2]
+        arr, loc, full = "arr" + tag, "loc" + tag, len(pairs) * len(topo.engines(core, dst))
+
+        def issue():
+            order("g", [p[1] for p in pairs], [])
+            for land, src, codes in pairs:
+                g.remote_dma(by(land) if codes else ap(land), by(src) if codes else ap(src), T.sem[arr], T.sem[loc], pid, rid, topo.mask(core, dst))
+            count[arr] = count[loc] = full
+            note("g", loc, full, [p[1] for p in pairs], [])
+            for land, src, codes in pairs:
+                log.setdefault(land[0], []).append((land, arr, full, True, "r"))
+
+        put("g", issue, [p[1] for p in pairs], [p[0] for p in pairs], cost, late)
 
     def turned(out, a):
         run("v", lambda: g.vector.transpose(ap(out), ap(a)), [a], [out])
@@ -411,8 +443,8 @@ def rank_program(g, core, T, topo):
         return V(name, (4 * h + b) * B, (4 * h + b + 1) * B)
 
     r = static(0)
-    products("x0", 0, 0)
-    products("x0", 1, 1)
+    products("x0", 0, 0, 0)
+    products("x0", 1, 1, 0)
     for t in range(3):
         k = t % 2
         nl = 5 + k
@@ -421,39 +453,31 @@ def rank_program(g, core, T, topo):
         pick(ON["sb"], V("sb"), V("sc"), r["oBu"])
         tq = "tq%d" % t
         tti(V(tq, 0, B), V("sc"), r["oAu"], V("sb"), OP.is_gt)
-        ur, tc, eu, uv, e = row(), tmp(10), lst(20), "uv%d" % t, V("ne%d" % t, 5, 120, 6)
+        ur, us, tc, eu, d1, e = row(), row(), tmp(10), lst(20), V("d1%d" % t), V("ne%d" % t, 5, 120, 6)
         tti(ur, V(tq, 0, B + k), r["Mf"], V("dm%d" % t), OP.mult)
         ts(tc, table(V(tq, 0, B), B), iw, OP.mult, 0.5, OP.is_gt)
-        scan(V(uv, 0, C), ur)
+        scan(us, ur)
         for z in range(2):
             tt(V("d0", 60 * z + 4, 60 * z + 60, 6), tc, r["S"], OP.is_gt)
-        pick("v", V("d1"), V(uv), six)
-        run("v", lambda t=t: g.vector.tensor_tensor_scan(T["ne%d" % t][:], T.d0[:], T.d1[:], 0.0, OP.mult, OP.add), [V("d0"), V("d1")], [V("ne%d" % t)])
+        pick("v", sub(d1, 1, 128, 2), us, sub(six, 4, 8))
+        n6 = [V(z, 0, 120) for z in ("ne%d" % t, "d0", d1[0])]
+        run("v", lambda n6=n6: g.vector.tensor_tensor_scan(ap(n6[0]), ap(n6[1]), ap(n6[2]), 0.0, OP.mult, OP.add), n6[1:], n6[:1])
         A, Bv = (10 * a, 10 * a + 10), (10 - 10 * a, 20 - 10 * a)
         ts(eu, e, iw1k, OP.mult)
         for z in range(2):
             scaled(ON["tp"], place(tp, z), V(tq, 0, B), 1.0 - 2.0 * z)
         euA, euB = sub(eu, *A), sub(eu, *Bv)
-        for b in range(4):
-            pick("s", V("et", b, 128 * nl - 7 + b, 8), wfF(b), sub(euA, 0, nl), 2.0)
-            pick("v", V("et", 4 + b, 128 * nl - 3 + b, 8), wfF(b), sub(euB, 0, nl), 2.0)
         ne = NE[t]
-        qe, pe, lq, lp = [V(s + str(t), 0, ne) for s in ("qe", "pe", "lq", "lp")]
-        quant(qe, pe, V("et", 0, 4 * ne))
-        dst = T.cores[rank ^ STEP[t]]
-        rid, pid = topo.addr(dst)[:2]
-        arr, loc, full = "arr%d" % t, "loc%d" % t, 2 * len(topo.engines(core, dst))
-
-        def send(qe=qe, pe=pe, lq=lq, lp=lp, pid=pid, rid=rid, arr=arr, loc=loc, full=full, mask=topo.mask(core, dst)):
-            order("g", [qe, pe], [])
-            g.remote_dma(by(lq), by(qe), T.sem[arr], T.sem[loc], pid, rid, mask)
-            g.remote_dma(ap(lp), ap(pe), T.sem[arr], T.sem[loc], pid, rid, mask)
-            count[arr] = count[loc] = full
-            note("g", loc, full, [qe, pe], [])
-            log[lq[0]] = [(lq, arr, full, True, "r")]
-            log[lp[0]] = [(lp, arr, full, True, "r")]
-
-        put("g", send, [qe, pe], [lq, lp], 0.6 + 0.8 * (t == 0), 1.7)
+        if ON["E"] == "F":
+            le = V("le%d" % t)
+            send(t, "%d2" % t, [(le, eu, False)], 0.3, 1.5)
+        else:
+            for b in range(4):
+                pick("s", V("et", b, 128 * nl - 7 + b, 8), wfF(b), sub(euA, 0, nl), 2.0)
+                pick("v", V("et", 4 + b, 128 * nl - 3 + b, 8), wfF(b), sub(euB, 0, nl), 2.0)
+            qe, pe, lq, lp = [V(s + str(t), 0, ne) for s in ("qe", "pe", "lq", "lp")]
+            quant(qe, pe, V("et", 0, 4 * ne))
+            send(t, "%d0" % t, [(lq, qe, True), (lp, pe, False)], 0.6 + 0.8 * (t == 0), 1.7)
         t1 = tmp(10)
         tt(t1, tc, r["dob"], OP.mult)
         if t < 2:
@@ -518,9 +542,19 @@ def rank_program(g, core, T, topo):
             else:
                 scaled(q, af, ah, 2.0)
         zs = (1 - early, early) if ALT else (1, 0)
-        for b in range(4):
+        for b in range(4 if ON["E"] != "F" else 0):
             mm(bank(b, ne), cols("eq", b), cols("ep", b), lq, lp)
             scaled("s", V("wf", b * WD + C + 1 - k, b * WD + C + 1 - k + ne), bank(b, ne), 0.5)
+        if ON["E"] == "F":
+            for z, h in enumerate((1 - early, early) if ALT else (0, 1)):
+                for b in range(4):
+                    n = FB[1][b] if z == 0 else b + 1
+                    mm(bank(n), cols("eq", b), cols("ep", b), half("lq%d" % t, h), half("lp%d" % t, h))
+                    scaled("s", half("w2", h, b), bank(n), 0.5)
+            for b in range(4):
+                for z, blk in enumerate((A, Bv)):
+                    at = b * WD + C + 1 - k + z
+                    pick("sv"[z], V("wf", at, at + 32 * nl - 1, 2), V("w2", b * C, b * C + C), sub(le, blk[0], blk[0] + nl))
         for z, h in enumerate(zs):
             for b in range(4):
                 tti(el("zt", b, h), wf(b), sub(vl, 10 * h, 10 * h + 10), part("ah", h, b), OP.add)
@@ -535,14 +569,15 @@ def rank_program(g, core, T, topo):
             quant(V("vq"), V("vp"), V("vt"))
             actb(V("romo", 0, C - 1, 2), V("iota"), sub(ofu, 0, 10), float(B))
             actb(V("romo", 1, C, 2), V("iota"), sub(ofu, 10, 20), float(B))
-            for h in range(2):
-                actb(half("romm", h), V("iota"), sub(mu[3], 10 * h, 10 * h + 10), float(C - B * h))
+            act(V("romm"), mr, 1.0, float(B))
+            ts(V("romm"), mr, float(B), OP.add)
+            either("s")
             dma("y", [(T.om[:, 0:C], T.romo[0:128:16, :]), (T.om[:, C:2 * C], T.romm[0:128:16, :])], [V("romo"), V("romm")], [])
         for z, h in enumerate(zs[::-1]):
             for b in range(4):
                 tti(el("xt", b, h), half("gs", 1 - h, b), sub(mu[t + 1], 10 * h, 10 * h + 10), part("af", h, b), OP.add)
             if t < 2:
-                products("xt", h, z)
+                products("xt", h, z, t + 1)
             else:
                 q, p = half("xq", h), half("xp", h)
                 quant(q, p, half("xt", h, 0, 4))
@@ -611,7 +646,7 @@ def plan(ops, before, other):
 
 
 MACHINES = [(1.0, 0.0, 0.17, 0.2, True), (1.0, -0.3, 0.17, 0.23, False), (1.35, 1.3, 0.15, 0.2, False)]
-TRIES = 200000
+TRIES, SOON, HEAT, REACH, AIM = 240000, 0.2, 0.0002, 30, 0.5
 
 
 def polish(ops, before, after, other, seq):
@@ -656,20 +691,37 @@ def polish(ops, before, after, other, seq):
             end[i] = t + late[i]
         return end
 
+    def worth(end):
+        return max(end) + SOON * sum(end) / n
+
     ends = [walk(seq, 0, [0.0] * n, m) for m in sets]
-    base = [max(e) for e in ends]
+    base = [worth(e) for e in ends]
     now, rng = 1.0, np.random.RandomState(4)
     best = (now, seq, list(qn))
     pos = [0] * n
     for k, i in enumerate(seq): pos[i] = k
     for turn in range(TRIES):
-        a = int(rng.randint(n))
-        i = seq[a]
+        if turn % 100 == 0:
+            m = turn // 100 % len(sets)
+            end, cost, late, last, prev, block = ends[m], sets[m][0], sets[m][1], {}, {}, []
+            for j in seq:
+                prev[j] = last.get(qn[j], -1)
+                last[qn[j]] = j
+            i = end.index(max(end))
+            while i >= 0:
+                p, t = prev[i], end[i] - late[i] - cost[i][qn[i]]
+                if p >= 0 and end[p] - late[p] > t - 1e-6:
+                    if p not in need[i]: block += [(p, 1), (i, -1)]
+                    i = p
+                else:
+                    i = max(need[i], key=lambda j: end[j]) if need[i] else -1
+        i, way = block[int(rng.randint(len(block)))] if block and rng.rand() < AIM else (int(rng.randint(n)), 1 if rng.rand() < 0.5 else -1)
+        a = pos[i]
         lo = max([pos[j] for j in before[i]] + [-1]) + 1
         hi = min([pos[j] for j in after[i]] + [n]) - 1
-        b = a + int(rng.randint(1, 30)) * (1 if rng.rand() < 0.5 else -1)
+        b = a + int(rng.randint(1, REACH)) * way
         b = max(lo, min(hi, b))
-        lim = now - 0.0005 * max(0.0, 1.0 - 1.2 * turn / TRIES) * math.log(rng.rand() + 1e-12)
+        lim = now - HEAT * max(0.0, 1.0 - 1.2 * turn / TRIES) * math.log(rng.rand() + 1e-12)
         flip = other[i] and rng.rand() < 0.3
         if flip: qn[i] = 1 - qn[i]
         elif b == a or not [j for j in seq[min(a, b):max(a, b) + 1] if j != i and qn[j] == qn[i]]: continue
@@ -678,7 +730,7 @@ def polish(ops, before, after, other, seq):
         total, got = 0.0, []
         for m, e, w in zip(sets, ends, base):
             got.append(walk(new, min(a, b), e, m))
-            r = max(got[-1]) / w
+            r = worth(got[-1]) / w
             total += r / len(sets)
             if r > lim + 0.03: total += 9.0
             if total > lim: break

@@ -4,13 +4,19 @@ from concourse.mybir import dt, AluOpType as OP, ActivationFunctionType as AF
 
 C, B = 320, 160
 STEP = [1, 2, 4]
-EW = 208
-WD = C + EW
-NE = [160, 162, 160]
 F8, BF, F32, U16, U8, I32 = "float8_e4m3fn_x4", "bfloat16", "float32", "uint16", "uint8", "int32"
 CYCLE = 0.00093
-PB = 839
-BIG = 2.0 ** 64
+BIG = 2.0 ** 40
+HUGE = 2.0 ** 90
+WD = C + 208
+MID = 81
+ON = {"sb": "2", "p": "s", "mn": "s", "af0": "s", "af1": "v", "pm0": "v", "pm1": "s", "M0": "v", "M1": "s",
+      "x0": "s", "sc0": "s", "sc1": "v", "tp": "v", "X": "n", "Z": "n", "F2": 2, "late": 1, "ft": 1, "E": "e", "PH": 2, "TD": 2, "G": 1, "bank": 1, "G2": "s", "G3": "g", "swap": (0, 1, 2)}
+TD = (0, 1, 2)
+RAW = [(1, 1), (2, 1)]
+XW, ZW, EP = ON["X"] == "w", ON["Z"] == "w", ON["E"] == "p"
+WD = 2 * C + 16 if EP else WD
+PB = B if ZW else 839
 
 SCRATCH = {
     "oi": ("sbuf", [128, 20], I32), "mi": ("sbuf", [128, 20], I32),
@@ -23,36 +29,36 @@ SCRATCH = {
     "eq": ("sbuf", [128, 512], F8), "ep": ("sbuf", [128, 512], U8),
     "iota": ("sbuf", [128, C], BF), "cw": ("sbuf", [128, C], BF),
     "six": ("sbuf", [128, 128], BF), "d0": ("sbuf", [128, 128], F32),
-    "k16": ("sbuf", [128, 16], BF), "kk": ("sbuf", [128, C], BF),
+    "k16": ("sbuf", [128, 16], BF), "kk": ("sbuf", [128, C], BF), "k4": ("sbuf", [128, 16], BF), "kw": ("sbuf", [128, C], BF),
     "pcol": ("sbuf", [128, 8], I32), "pcol2": ("sbuf", [128, 8], I32), "ulu": ("sbuf", [128, 8], U16),
-    "tb": ("sbuf", [128, 3000], F32), "ub": ("sbuf", [128, 1000], U16),
+    "tb": ("sbuf", [128, 3000], F32), "ub": ("sbuf", [128, 1400], U16),
     "orow": ("sbuf", [128, C], BF), "prow": ("sbuf", [128, C], BF),
     "pmrow": ("sbuf", [128, C], BF), "xrow": ("sbuf", [128, C], BF), "Mrow": ("sbuf", [128, C], BF),
     "wf": ("sbuf", [128, 4 * WD], BF), "w2": ("sbuf", [128, 4 * C], BF), "ft": ("sbuf", [128, 4 * C], BF),
     "ah": ("sbuf", [128, 4 * C], BF), "af": ("sbuf", [128, 4 * C], BF),
-    "et": ("sbuf", [128, 4 * 192], BF), "zt": ("sbuf", [128, 4 * C], BF), "xt": ("sbuf", [128, 4 * C], BF),
+    "zt": ("sbuf", [128, 4 * C], BF), "xt": ("sbuf", [128, 4 * C], BF),
     "zq": ("sbuf", [128, C], F8), "zp": ("sbuf", [128, C], U8),
     "xq": ("sbuf", [128, C], F8), "xp": ("sbuf", [128, C], U8),
-    "gs": ("sbuf", [128, 4 * C], F32), "sc": ("sbuf", [128, C], F32), "sb": ("sbuf", [128, B], F32),
+    "gs": ("sbuf", [128, 4 * C], F32), "sc": ("sbuf", [128, 2 * C], F32), "sb": ("sbuf", [128, B], F32),
     "ysb": ("sbuf", [128, C], F32), "romo": ("sbuf", [128, C], F32), "romm": ("sbuf", [128, C], F32),
+    "vr": ("sbuf", [128, C], BF), "vt4": ("sbuf", [128, C], BF), "tp": ("sbuf", [128, 352], BF),
+    "td": ("sbuf", [128, 496], BF), "tda": ("sbuf", [128, 480], BF), "tdb": ("sbuf", [128, 480], BF),
 }
 for _t in range(3):
     for _n, _d in (("qe", F8), ("pe", U8), ("lq", F8), ("lp", U8)):
         SCRATCH[_n + str(_t)] = ("sbuf", [128, C], _d)
     SCRATCH["le%d" % _t] = ("sbuf", [128, 20], U16)
-    for _n, _w, _d in (("tp", 352, BF), ("dr", 352, BF), ("er", 352, BF), ("dm", C, BF), ("cur", 72, F32),
-                       ("d1", 128, F32), ("ne", 128, F32), ("vi", 60, I32), ("tq", B + 16, BF)):
+    SCRATCH["vl%d" % _t] = ("sbuf", [128, 80], U16)
+    for _n, _w, _d in (("dr", 352, BF), ("er", 560, BF), ("dm", C, BF), ("cur", 80, F32),
+                       ("d1", 128, F32), ("ne", 128, F32), ("vi", 60, I32)):
         SCRATCH[_n + str(_t)] = ("sbuf", [128, _w], _d)
 for _t in range(2):
-    for _n, _w, _d in (("go", 40, F32), ("tw", 64, F32), ("tn", 32, F32)):
-        SCRATCH[_n + str(_t)] = ("sbuf", [128, _w], _d)
-SCRATCH["rows"] = ("sbuf", [128, 28 * C], BF)
+    SCRATCH["go%d" % _t] = ("sbuf", [128, 48], F32)
+    SCRATCH["vw%d" % _t] = ("sbuf", [128, 352], BF)
+SCRATCH["rows"] = ("sbuf", [128, 33 * C], BF)
 for _k in range(8):
     SCRATCH["ps%d" % _k] = ("psum", [128, 512], F32)
 SEMAPHORES = ["vs", "ss", "ts", "gs"] + ["d%d" % k for k in range(32)] + [s + "%d%d" % (t, k) for s in ("arr", "loc") for t in range(3) for k in range(3)]
-ON = {"sb": "s", "p": "s", "mn": "s", "dm": "s", "af0": "s", "af1": "v", "pm0": "v", "pm1": "s", "M0": "v", "M1": "s", "dr1": "s",
-      "x0": "s", "sc0": "s", "sc1": "v", "tp": "v", "shift": "d", "F": "halves", "E": "F"}
-ALT = True
 
 
 def rank_program(g, core, T, topo):
@@ -71,6 +77,7 @@ def rank_program(g, core, T, topo):
         return (name, lo, SCRATCH[name][1][1] if hi is None else hi, step)
 
     def ap(v):
+        if not isinstance(v, tuple): return v
         return T[v[0]][:, v[1]:v[2]:v[3]] if v[3] != 1 else T[v[0]][:, v[1]:v[2]]
 
     def by(v):
@@ -78,6 +85,9 @@ def rank_program(g, core, T, topo):
 
     def ind(win, off):
         return ap(win).indirect(ap(off))
+
+    def views(*a):
+        return [v for v in a if isinstance(v, tuple)]
 
     def clash(a, b):
         if a[1] >= b[2] or b[1] >= a[2]: return False
@@ -124,16 +134,19 @@ def rank_program(g, core, T, topo):
             note(q, s, count[s], reads, writes)
         o = writes[0]
         n = (o[2] - o[1] + o[3] - 1) // o[3]
-        narrow = all(SCRATCH[v[0]][2] in (BF, U16) for v in reads + writes)
+        narrow = all(SCRATCH[v[0]][2] in (BF, U16) for v in reads + writes if v[2] - v[1] > 1)
         psum = any(v[0][:2] == "ps" for v in reads)
-        if kind == "ind": c = 0.06 + 1.25 * CYCLE * n
-        elif kind == "scat": c = 3.8 * CYCLE * n
-        elif kind == "q": c = 0.015 + 4 * 0.00025 * n
-        elif q == "t": c = (n + 16) * CYCLE
-        elif q == "g": c = 0.18 + 2 * CYCLE * n
-        elif q == "s": c = CYCLE * max(n, 64) + 0.1
-        else: c = 0.01 + CYCLE * max(64, n * (2 if kind == "tt" and not psum else 0.5 if narrow else 1))
-        put(q, issue, reads, writes, c)
+        cs = []
+        for m in MACHINES:
+            if kind == "ind": c = 0.06 + m["gather"] * CYCLE * n
+            elif kind == "scat": c = 3.0 * m["gather"] * CYCLE * n
+            elif kind == "q": c = 0.015 + 4 * 0.00025 * n
+            elif q == "t": c = (n + 16) * CYCLE * m["product"]
+            elif q == "g": c = 0.18 + 2 * CYCLE * n
+            elif q == "s": c = CYCLE * max(n, 64) + m["act"]
+            else: c = 0.01 + CYCLE * max(64, n * (2 if kind == "tt" and not psum else 0.5 if narrow else 1))
+            cs.append(c * m["compute"])
+        put(q, issue, reads, writes, cs)
 
     def dma(q, pairs, reads, writes, late=2.2, add=False):
         def issue():
@@ -144,7 +157,7 @@ def rank_program(g, core, T, topo):
                 (g.dma_start(o, i, accum_op=OP.add) if add else queue[q].dma_start(o, i)).then_inc(T.sem[s], 16)
             count[s] = 16 * len(pairs)
             note(q, s, count[s], reads, writes)
-        put(q, issue, reads, writes, (1.0 if add else 0.07) * len(pairs), late)
+        put(q, issue, reads, writes, [(1.0 if add else 0.07) * len(pairs) for m in MACHINES], late)
 
     def copy(out, a):
         run("v", lambda: g.vector.tensor_copy(ap(out), ap(a)), [a], [out])
@@ -153,12 +166,10 @@ def rank_program(g, core, T, topo):
         run("v", lambda: g.vector.tensor_tensor(ap(out), ap(a), ap(b), op), [a, b], [out], "tt")
 
     def ts(out, a, s1, op0, s2=None, op1=None):
-        more = [s for s in (s1, s2) if isinstance(s, tuple)]
-        s1, s2 = [ap(s) if isinstance(s, tuple) else s for s in (s1, s2)]
         if op1 is None:
-            run("v", lambda: g.vector.tensor_scalar(ap(out), ap(a), s1, None, op0), [a] + more, [out])
+            run("v", lambda: g.vector.tensor_scalar(ap(out), ap(a), ap(s1), None, op0), [a] + views(s1), [out])
         else:
-            run("v", lambda: g.vector.tensor_scalar(ap(out), ap(a), s1, s2, op0, op1), [a] + more, [out])
+            run("v", lambda: g.vector.tensor_scalar(ap(out), ap(a), ap(s1), ap(s2), op0, op1), [a] + views(s1, s2), [out])
 
     def tti(out, win, off, b, op):
         run("v", lambda: g.vector.tensor_tensor(ap(out), ind(win, off), ap(b), op), [win, off, b], [out], "ind")
@@ -166,9 +177,9 @@ def rank_program(g, core, T, topo):
     def fill(out, c):
         run("v", lambda: g.vector.memset(ap(out), c), [], [out])
 
-    def act(out, a, scale=1.0, bias=None):
-        if bias is None: run("s", lambda: g.scalar.activation(ap(out), ap(a), AF.Copy, scale=scale), [a], [out])
-        else: run("s", lambda: g.scalar.activation(ap(out), ap(a), AF.Identity, bias=bias, scale=scale), [a], [out])
+    def act(out, a, scale=1.0, bias=None, fn=None):
+        if bias is None and not views(scale) and not fn: run("s", lambda: g.scalar.activation(ap(out), ap(a), AF.Copy, scale=scale), [a], [out])
+        else: run("s", lambda: g.scalar.activation(ap(out), ap(a), fn or AF.Identity, bias=ap(bias or 0.0), scale=ap(scale)), [a] + views(scale, bias), [out])
 
     def either(q):
         v, s = calls.pop(), calls.pop()
@@ -180,19 +191,20 @@ def rank_program(g, core, T, topo):
         else: ts(out, a, scale, OP.mult, bias, OP.add)
         either(q)
 
-    def const(out, c):
+    def const(out, c, q="s"):
+        if q == "g" and ON["G"]: return iota(out, [[0, (out[2] - out[1] + out[3] - 1) // out[3]]], int(c), 0)
         scaled("s", out, V("ones", 0, (out[2] - out[1] + out[3] - 1) // out[3]), c)
 
-    def pick(q, out, win, off, scale=1.0):
-        run("s", lambda: g.scalar.activation(ap(out), ind(win, off), AF.Copy, scale=scale), [win, off], [out], "ind")
-        if scale == 1.0: run("v", lambda: g.vector.tensor_copy(ap(out), ind(win, off)), [win, off], [out], "ind")
-        else: run("v", lambda: g.vector.tensor_scalar(ap(out), ind(win, off), scale, None, OP.mult), [win, off], [out], "ind")
+    def pick(q, out, win, off, scale=1.0, bias=None):
+        r = [win, off] + views(scale)
+        if bias is not None:
+            run("s", lambda: g.scalar.activation(ap(out), ind(win, off), AF.Identity, bias=bias), r, [out], "ind")
+            run("v", lambda: g.vector.tensor_scalar(ap(out), ind(win, off), bias, None, OP.add), r, [out], "ind")
+        else:
+            run("s", lambda: g.scalar.activation(ap(out), ind(win, off), AF.Identity if views(scale) else AF.Copy, scale=ap(scale)), r, [out], "ind")
+            if scale == 1.0: run("v", lambda: g.vector.tensor_copy(ap(out), ind(win, off)), r, [out], "ind")
+            else: run("v", lambda: g.vector.tensor_scalar(ap(out), ind(win, off), ap(scale), None, OP.mult), r, [out], "ind")
         either(q)
-
-    def actb(out, win, off, bias):
-        run("s", lambda: g.scalar.activation(ap(out), ind(win, off), AF.Identity, bias=bias), [win, off], [out], "ind")
-        run("v", lambda: g.vector.tensor_scalar(ap(out), ind(win, off), bias, None, OP.add), [win, off], [out], "ind")
-        either("s")
 
     def quant(q, p, a):
         run("v", lambda: g.vector.quantize_mx(ap(q), ap(p), ap(a)), [a], [q, p], "q")
@@ -221,11 +233,11 @@ def rank_program(g, core, T, topo):
         if v[3] == 1: return (v[0], v[1] + lo, v[1] + hi, step)
         return (v[0], v[1] + lo * v[3], min(v[2], v[1] + (hi - 1) * v[3] + 1), v[3] * step)
 
-    def tab(v):
-        return (v[0], v[1] + 15, v[2], 16)
+    def tab(v, n=16):
+        return (v[0], v[1] + n - 1, v[2], n)
 
-    def scan(out, data):
-        h = V("kk", 0, out[2] - out[1])
+    def scan(out, data, n=16):
+        h = V("kk" if n == 16 else "kw", 0, out[2] - out[1])
         run("v", lambda: g.vector.tensor_tensor_scan(ap(out), ap(h), ap(data), 0.0, OP.mult, OP.add), [h, data], [out])
 
     def table(data, n=C):
@@ -236,20 +248,23 @@ def rank_program(g, core, T, topo):
     def win0(name, k):
         return V(name, 16, 16 + C + k)
 
-    def place(name, e, s=0):
-        return V(name, 16 + e + s, 16 + e + s + C - 1, 2)
+    def place(name, e, s=0, n=B):
+        return V(name, 16 + e + s, 16 + e + s + 2 * n - 1, 2)
 
-    def wf(b):
-        return V("wf", b * WD, b * WD + C + 1 + B)
-
-    def wfF(b, h=None):
-        return V("wf", b * WD, b * WD + C) if h is None else V("wf", b * WD + B * h, b * WD + B * h + B)
-
-    def el(name, b, h):
-        return V(name, 4 * B * h + b, 4 * B * (h + 1) - 3 + b, 4)
+    def el(name, b, h, n=1):
+        return V(name, 4 * B * h + b, 4 * B * (h + n) - 3 + b, 4)
 
     def half(name, h, b=0, w=1):
         return V(name, (b * C + B * h) * w, (b * C + B * h + B) * w)
+
+    def htile(name, h):
+        return half(name, h, 0, 4)
+
+    def part(name, h, b):
+        return el(name, b, h) if XW else V(name, (4 * h + b) * B, (4 * h + b + 1) * B)
+
+    def wfF(b, h):
+        return el("wf", b, h) if ZW else V("wf", b * WD + B * h, b * WD + B * h + B)
 
     def cols(name, b, n=128):
         return V(name, n * b, n * b + n)
@@ -257,79 +272,116 @@ def rank_program(g, core, T, topo):
     def bank(k, n=B):
         return V("ps%d" % k, 0, n)
 
-    dma("y", [(T.oi[:], T.o[:]), (T.mi[:], T.m[:])], [], [V("oi"), V("mi")], 1.9)
-    dma("s", [(T.x0[:, 0:4 * B], T.x[:, 0:4 * B])], [], [half("x0", 0, 0, 4)], 2.5)
-    dma("y", [(T.ut[:], T.u[:])], [], [V("ut")], 2.5)
-    dma("s", [(T.x0[:, 4 * B:4 * C], T.x[:, 4 * B:4 * C])], [], [half("x0", 1, 0, 4)], 2.9)
-    dma("y", [(by(V("wq")), T.wc[:]), (T.wp[:], T.ws[:])], [], [V("wq"), V("wp")], 4.5)
-    dma("y", [(T.vt[:], T.v[:])], [], [V("vt")], 5.0)
+    dma("y", [(T.oi[:], T.o[:])], [], [V("oi")], 1.9)
+    dma("s", [(T.mi[:], T.m[:])], [], [V("mi")], 1.9)
+    dma("y", [(T.ut[:], T.u[:])], [], [V("ut")], 2.6)
+    dma("s", [(T.x0[:, 0:4 * B], T.x[:, 0:4 * B])], [], [htile("x0", 0)], 3.0)
+    dma("y", [(T.x0[:, 4 * B:4 * C], T.x[:, 4 * B:4 * C])], [], [htile("x0", 1)], 3.6)
+    first = len(calls)
+    behind = [V("x0")] if ON["late"] else []
+    dma("y", [(by(V("wq")), T.wc[:]), (T.wp[:], T.ws[:]), (T.vt[:], T.v[:])], behind, [V("wq"), V("wp"), V("vt")], 4.0)
 
     iota(V("pcol"), [[0, 8]], 0, 1)
     fill(V("ones"), 1.0)
     run("g", lambda: g.affine_select(T.ect[:], T.ones[:], [[1, 516]], OP.is_equal, 0.0, -3, -4), [V("ones")], [V("ect")])
     one = V("ones", 0, C)
     run("v", lambda: g.vector.tensor_tensor_scan(T.iota[:], ap(one), ap(one), -1.0 - B, OP.mult, OP.add), [one], [V("iota")])
-    pm, pm0, pm1, pm2 = tmp(1), tmp(1), tmp(1), tmp(1)
-    ts(V("pcol2"), V("pcol"), 15, OP.bitwise_and)
-    copy(pm, V("pcol2", 0, 1))
-    scaled("s", pm0, pm, 1.0, -float(B))
-    scaled("s", pm1, pm, 1.0, 1.0 - B)
+    lane = tmp(3)
+    pm, lb, la = sub(lane, 0, 1), sub(lane, 1, 2), sub(lane, 2, 3)
+    ts(V("pcol2", 0, 1), V("pcol", 0, 1), 15, OP.bitwise_and)
+    if XW:
+        ts(V("pcol2", 1, 2), V("pcol", 0, 1), 3, OP.bitwise_and)
+        ts(V("pcol2", 2, 3), V("pcol", 0, 1), 15, OP.bitwise_and, 2, OP.logical_shift_right)
+    copy(sub(lane, 0, 1 + 2 * XW), V("pcol2", 0, 1 + 2 * XW))
+    pm2 = tmp(1)
     scaled("s", pm2, pm, 2.0, float(B))
-    k1, k2, lanes = tmp(16), tmp(16), lst(20)
-    ts(k1, V("iota", 0, 16), pm0, OP.not_equal)
-    ts(k2, V("iota", 0, 16), pm1, OP.is_equal, BIG, OP.mult)
-    tt(V("k16"), k1, k2, OP.add)
-    ts(lanes, V("iota", 0, 20), 0.0, OP.mult, pm, OP.add)
-    pick("s", V("kk"), V("k16"), lanes)
-    shift = [lst(2), lst(2)]
-    for t, (edge, far, near) in enumerate(((0.0, 48.0, -1.0), (15.0, 16.0, 1.0))):
-        const(V("go%d" % t, 8, 24), 0.0)
-        if ON["shift"] != "v": continue
-        c1, c2 = tmp(1), tmp(1)
-        ts(c1, pm, edge, OP.is_equal, far, OP.mult)
-        ts(c2, c1, pm, OP.add, B + near, OP.add)
-        ts(shift[t], V("iota", 0, 32, 16), c2, OP.add)
-    w, iw, iw2, iw1k, wv, wlo, w1k, no0 = [tmp(1) for k in range(8)]
-    ts(no0, pm, 15.0, OP.is_lt)
-    scaled("s", w, no0, BIG, 1.0)
+    for own, at, n, short, long in ((pm, pm, 16, "k16", "kk"), (la, lb, 4, "k4", "kw"))[:1 + XW]:
+        c0, c1, k1, k2, lanes = tmp(1), tmp(1), tmp(16), tmp(16), lst(20)
+        scaled("s", c0, own, 1.0, -float(B))
+        scaled("s", c1, own, 1.0, 1.0 - B)
+        ts(k1, V("iota", 0, 16), c0, OP.not_equal)
+        ts(k2, V("iota", 0, 16), c1, OP.is_equal, BIG, OP.mult)
+        tt(V(short), k1, k2, OP.add)
+        ts(lanes, V("iota", 0, 20), 0.0, OP.mult, at, OP.add)
+        pick("s", V(long), V(short), lanes)
+    for t in range(2):
+        const(V("go%d" % t, 8, 32), 0.0, "g")
+    w, iw, iw2, iw1k, wv, wlo, w1k, no0, no1, iq, iq4, lb1, lb2, wb = [tmp(1) for k in range(14)]
+    ts(no1, pm, 15.0, OP.is_lt)
+    scaled("s", w, no1, BIG, 1.0)
     ts(iw, pm, 15.0, OP.is_equal, 1.0 / BIG, OP.max)
     scaled("s", iw2, iw, 2.0)
     scaled("s", iw1k, iw, 1.0 / 1024)
     scaled("s", wv, w, 1025.0 * B)
-    scaled("s", wlo, w, float(B - PB))
-    scaled("s", w1k, w, 1000.0)
     ts(no0, pm, 0.0, OP.is_gt)
-    KB = tmp(20)
-    ts(sub(KB, 0, 10), V("iota", 1, C, 32), pm2, OP.add)
-    ts(sub(KB, 10, 20), V("iota", 1, C, 32), pm2, OP.add)
-    const(V("d0", 1, 120, 2), 1.0)
-    const(V("d0", 0, 120, 6), 0.0)
-    const(V("d0", 2, 120, 6), -1.0)
+    if XW:
+        ts(iq, la, 3.0, OP.is_equal, 1.0 / BIG, OP.max)
+        scaled("s", iq4, iq, 4.0)
+        scaled("s", lb1, lb, 1.0, 4.0 * B)
+    if ZW:
+        scaled("s", lb2, lb, 1.0, 4.0 * (B + MID))
+        for k in range(2):
+            scaled("s", V("vw%d" % k, 16 + k, 16 + k + B), V("iota", 0, B), 1.0, float(C + 1 - MID))
+        const(V("vw1", 16, 17), 0.0)
+        const(V("wf", 4 * C, 4 * C + 4), 0.0)
+    else:
+        scaled("s", wlo, w, float(B - PB))
+        scaled("s", w1k, w, C + 1.0 if EP else 1000.0)
+        const(V("wf", C, 4 * WD, WD), 0.0, ON["G2"])
+    KB, KBw = tmp(20), tmp(20)
+    for z in range(2):
+        scaled("s", sub(KB, 10 * z, 10 * z + 10), V("iota", 1, C, 32), 1.0, pm2)
+    scaled("s", wb, w, -float(B))
+    scaled("s", KBw, KB, w, wb)
+    const(V("d0", 1, 120, 2), 1.0, "g")
+    if ON["G"]: iota(V("d0", 0, 120, 2), [[0, 20], [-1, 3]], 0, 0)
+    else:
+        const(V("d0", 0, 120, 6), 0.0)
+        const(V("d0", 2, 120, 6), -1.0)
     six = lst(8)
     iota(V("six", 60, 128), [[0, 68]], -B, 0)
     for z, (step, first) in enumerate(((1, 0), (16, 15))):
         for j in range(3):
             iota(V("six", 64 * z + j, 64 * z + 60, 3), [[step * (10 - 20 * (j % 2)), 2], [step, 10]], first + 10 * step * (j % 2) - B, 0)
     ts(six, table(V("six", 0, 128), 128), iw, OP.mult, float(B), OP.add)
-    scaled("s", V("cw"), V("iota"), 1024.0)
-    const(V("cw", B, B + 1), 1.0)
-    for v in [V("tp1", 336, 337), V("dr1", 336, 337), V("er0", 16, 17), V("tq1", B, B + 1), V("wf", C, 4 * WD, WD)]:
-        const(v, 0.0)
+    if ON["G"]: iota(V("cw", 1, C), [[1024, C - 1]], 1024 * (1 - B), 0)
+    else: scaled("s", V("cw", 1, C), V("iota", 1, C), 1024.0)
+    const(V("cw", 0, 1), 1.0, ON["G2"])
+    for v in [V("er0", 16, 17), V("tdb")] + ([V("tp", 336, 337), V("td", 3 * B, 3 * B + 2)] if 1 in TD else [V("tp", 336, 337), V("dr1", 336, 337)]) if TD \
+            else [V("tp", 16, 337), V("dr1", 336, 337), V("er0", 16, 17)]:
+        const(v, 0.0, "s" if v[0] == "tdb" else ON["G2"])
+    for lo, hi in ((0, C - 1), (C + 2, 2 * C - 1)): const(V("sc", lo, hi, 2), 0.0, ON["G3"])
+    const(V("sc", C, C + 1), HUGE)
+    if TD:
+        const(V("tda", 0, 3 * B, 3), 0.0, "g")
+        const(V("tda", 2, 3 * B, 3), -1.0, "g")
     for b in range(4):
         quant(cols("eq", b), cols("ep", b), V("ect", 3 - b, 515 - b))
     ts(V("ulu"), V("iota", 0, 128, 16), float(B), OP.add)
 
-    onat, mnat, mu = lst(20), lst(20), [lst(20) for k in range(4)]
+    def mates(mr):
+        m4, mu = row(), lst(80)
+        scan(m4, mr, 4)
+        ts(sub(mu, 0, 40), sub(tab(m4, 4), 0, 40), iq4, OP.mult, lb, OP.add)
+        ts(sub(mu, 40, 80), sub(tab(m4, 4), 40, 80), iq4, OP.mult, lb1, OP.add)
+        return mu
+
+    onat, mnat, mrow = lst(20), lst(20), row()
     copy(onat, V("oi"))
     run("v", lambda: g.vector.tensor_copy(ind(V("prow"), onat), ap(V("iota"))), [V("iota"), onat], [V("prow")], "scat")
     copy(mnat, V("mi"))
-    ts(sub(mu[0], 0, 10), V("mi", 0, 10), -float(B), OP.add)
-    copy(sub(mu[0], 10, 20), V("mi", 10, 20))
     pick("s", V("orow"), V("iota"), onat)
-    for h in range(2):
+    XM = ON["x0"] == "m"
+    for h in range(0 if XM else 2):
         pick(ON["pm%d" % h], half("pmrow", h), V("prow"), sub(mnat, 10 * h, 10 * h + 10))
-    for h in range(2):
+    for h in range(0 if XM else 2):
         pick(ON["M%d" % h], half("Mrow", h), V("pmrow"), sub(onat, 10 * h, 10 * h + 10))
+    if XM or XW: pick("s", mrow, V("iota"), mnat)
+    if XW:
+        mu = mates(mrow)
+    else:
+        mu = [lst(10), sub(mnat, 10, 20)]
+        ts(mu[0], V("mi", 0, 10), -float(B), OP.add)
 
     def couples(name, first):
         out = row()
@@ -337,13 +389,21 @@ def rank_program(g, core, T, topo):
             scan(sub(out, B * e, B * e + B), V(name, e if first else 1 - e, C - 1 + (e if first else 1 - e), 2))
         return tab(out)
 
-    ts(V("cur0", 32, 52), couples("orow", True), iw2, OP.mult, 1.0, OP.add)
-    M0w = couples("Mrow", False)
+    scaled("v", V("cur0", 40, 60), couples("orow", True), iw2, 1.0)
+    if XM:
+        pick("s", V("xrow"), mrow, onat)
+        x0w, xu, M0w = couples("xrow", False), lst(20), row()
+        ts(xu, x0w, iw, OP.mult, float(B), OP.add)
+        for h in range(2):
+            pick(ON["M%d" % h], half("Mrow", h), V("prow"), sub(xu, 10 * h, 10 * h + 10))
+        M0w = table(V("Mrow"))
+    else: M0w = couples("Mrow", False)
     ts(V("vi0", 20, 40), M0w, iw, OP.mult, float(B), OP.add)
-    p0 = table(V("prow"))
-    P, pu = tmp(20), lst(20)
-    ts(P, p0, wlo, OP.add)
-    ts(pu, p0, iw, OP.mult, float(B), OP.add)
+    P, pu = table(V("prow")), lst(20)
+    ts(pu, P, iw, OP.mult, float(B), OP.add)
+    if not ZW:
+        p0, P = P, tmp(20)
+        scaled("s", P, p0, 1.0, wlo)
 
     quant(V("uq"), V("up"), V("ut"))
     run("s", lambda: g.scalar.activation(T.up16[:], T.up[:].indirect(T.ulu[:]), AF.Copy), [V("up"), V("ulu")], [V("up16")], "ind")
@@ -353,74 +413,90 @@ def rank_program(g, core, T, topo):
         k = t % 2
         cur = V("cur%d" % t)
         a = 1 if t < 2 else 0
-        oA, oB = sub(cur, 42 - 10 * a, 52 - 10 * a), sub(cur, 32 + 10 * a, 42 + 10 * a)
+        o0, o1 = sub(cur, 40, 50), sub(cur, 50, 60)
         vi = V("vi%d" % t)
-        M, uM = sub(vi, 20, 40), sub(cur, 52, 72)
+        M, uM = sub(vi, 20, 40), sub(cur, 60, 80)
         if t:
             copy(sub(vi, 0, 20), sub(cur, 0, 20))
             ts(M, sub(vi, 0, 20), 1023, OP.bitwise_and)
-        ts(sub(vi, 40, 60), sub(vi, 0, 20) if t else M, 1023, OP.bitwise_and, 1, OP.logical_shift_right)
-        tt(uM, M, KB, OP.subtract)
-        d, pr, nb, dob, oA2, mn, mn2, S, ix = tmp(30), tmp(30), tmp(10), tmp(10), tmp(10), tmp(10), tmp(10), tmp(10), tmp(10)
-        oAu, oBu, ixu, Mu2 = lst(10), lst(10), lst(10), lst(40)
+        if t not in TD: ts(sub(vi, 40, 60), sub(vi, 0, 20) if t else M, 1022, OP.bitwise_and)
+        if t: tt(uM, M, KB, OP.subtract)
+        else: tt(uM, M0w, KBw, OP.subtract)
+        d, pr, nb, dob, gap, m1, m2, res, S = [tmp(n) for n in (30, 30, 10, 10, 10, 10, 10, 10, 10)]
+        us, ixu, Mu2 = lst(20), lst(10), lst(40)
         Mu = sub(Mu2, 0, 20)
-        lo, hi = sub(cur, 32, 62), sub(cur, 42, 72)
-        if a: tt(d, hi, lo, OP.subtract)
-        else: tt(d, lo, hi, OP.subtract)
+        for c0, c1 in ((0, 30),) if t else ((0, 10), (20, 30)):
+            lo, hi = sub(cur, 40 + c0, 40 + c1), sub(cur, 50 + c0, 50 + c1)
+            tt(sub(pr, c0, c1), lo, hi, OP.mult)
+            if c0: lo, hi = sub(M0w, 0, 10), sub(M0w, 10, 20)
+            tt(sub(d, c0, c1), hi if a else lo, lo if a else hi, OP.subtract)
         do = sub(d, 0, 10)
         ts(nb, sub(uM, 10 * a, 10 * a + 10), 0.0, OP.not_equal)
-        if k: ts(sub(nb, 0, 1), sub(nb, 0, 1), no0, OP.mult)
-        tt(pr, lo, hi, OP.mult)
-        tt(dob, do, nb, OP.mult)
-        tt(mn, sub(pr, 0, 10), sub(pr, 20, 30), OP.min)
-        tt(oA2, oB, dob, OP.subtract)
-        tt(mn2, mn, sub(d, 20, 30), OP.min)
-        ts(oBu, oB, 0.5, OP.mult, 159.5, OP.add)
-        ts(S, mn2, 0.0, OP.is_gt)
-        ts(oAu, oA2, 0.5, OP.mult, 159.5, OP.add)
-        tt(ix, do, S, OP.mult)
-        copy(Mu2, sub(vi, 20, 60))
-        ts(ixu, ix, 0.5, OP.mult, float(B), OP.add)
+        if k: scaled("v", sub(nb, 0, 1), sub(nb, 0, 1), no0)
+        tt(sub(cur, 30, 40), o1, nb, OP.mult)
+        ts(us, sub(cur, 30, 50), float(C), OP.add)
+        if not a: const(V("sc", C, C + 1), -HUGE)
+        scaled("v", gap, do, 1.0 / 1024, B / 512.0)
+        tt(m1, sub(pr, 0, 10), gap, OP.min)
+        tt(m2, sub(pr, 20, 30) if t else m1, sub(d, 20, 30), OP.min)
+        tt(res, m1 if t else sub(pr, 20, 30), m2, OP.min)
+        ts(ixu, res, 512.0, OP.mult)
+        act(S, res, 1024.0, 0.0, AF.Relu)
+        ts(S, res, 1024.0, OP.mult, 0.0, OP.max)
+        either("v")
+        if t in TD:
+            ts(sub(Mu2, 20, 40), M, 1.5, OP.mult, 0.75, OP.add)
+            if not t and not XM: copy(Mu, M)
+        else: copy(Mu2, sub(vi, 20, 60))
         val, d1, sv = sub(cur, 0, 20), V("d1%d" % t, 0, 128, 2), sub(six, 0, 4)
         if t:
-            run("v", lambda: g.vector.tensor_scalar(ap(d1), ind(val, sv), ap(w), None, OP.mult), [val, sv, w], [d1], "ind")
+            pick("s", d1, val, sv, w)
         else:
             x0 = tmp(20)
-            pick(ON["x0"], V("xrow"), V("orow"), Mu)
-            ts(x0, table(V("xrow")), 1024.0, OP.mult, wv, OP.add)
+            if not XM: pick(ON["x0"], V("xrow"), V("orow"), Mu)
+            scaled("v", x0, x0w if XM else table(V("xrow")), 1024.0, wv)
             tt(val, x0, M0w, OP.add)
             pick("v", d1, val, sv)
         dr = "dr%d" % t
-        pick("s", place(dr, 0), V("cw"), ixu)
-        if t: scaled("v", place(dr, 1), place(dr, 0), -1.0)
-        else: pick("v", place(dr, 1), V("cw"), ixu, -1.0)
-        if t: pick("s", V("dm%d" % t), win0(dr, k), Mu)
-        for h in range(0 if t else 2):
-            pick("sv"[h], half("dm0", h), win0(dr, k), sub(Mu, 10 * h, 10 * h + 10))
-        return dict(a=a, dob=dob, S=S, oA=oA, oB=oB, oAu=oAu, oBu=oBu, Mf=sub(Mu2, 20, 40))
+        if t in TD: pick("s", V("tdb", 0, 3 * B, 3), V("cw"), ixu)
+        else:
+            pick("s", place(dr, 0), V("cw"), ixu)
+            if t: scaled("v", place(dr, 1), place(dr, 0), -1.0)
+            else: pick("v", place(dr, 1), V("cw"), ixu, -1.0)
+            if t: pick("s", V("dm%d" % t), win0(dr, k), Mu)
+            for h in range(0 if t else 2):
+                pick("sv"[h], half("dm0", h), win0(dr, k), sub(Mu, 10 * h, 10 * h + 10))
+        return dict(a=a, do=do, S=S, oA=o0 if a else o1, oB=o1 if a else o0, oAu=sub(us, 10 * a, 10 + 10 * a),
+                    oBu=sub(us, 10 - 10 * a, 20 - 10 * a), Mf=sub(Mu2, 20, 40))
 
     FB = [[0, 1, 2, 3], [5, 6, 7, 0]]
+    held = []
 
     def products(src, h, z, t):
         q, p = half("xq", h), half("xp", h)
-        quant(q, p, half(src, h, 0, 4))
+        quant(q, p, htile(src, h))
         mm(bank(4), V("uq16"), V("up16"), q, p)
-        scaled(ON["sc%d" % z], half("sc", h), bank(4), 1.0)
+        scaled(ON["sc%d" % z], V("sc", C * h + 1, C * h + C, 2), bank(4), 1.0)
+        qe, pe, lq, lp = [half(s + str(t), h) for s in ("qe", "pe", "lq", "lp")]
+        raw = (t, z) in RAW
+        if raw: send(t, "%d%d" % (t, z), [(lq, q, True), (lp, p, False)], 800)
+        while held: send(*held.pop())
         for b in range(4):
-            if ON["F"] == "halves":
-                mm(bank(FB[z][b]), cols("eq", b), cols("ep", b), q, p)
+            mm(bank(FB[z][b]), cols("eq", b), cols("ep", b), q, p)
+            if raw: scaled("s", wfF(b, h), bank(FB[z][b]), 0.5)
+            elif XW or ON["ft"]: scaled("s", el("ft", b, h), bank(FB[z][b]), 1.0)
+            else:
                 scaled("s", wfF(b, h), bank(FB[z][b]), 0.5)
-            elif z:
-                mm(bank(b, C), cols("eq", b), cols("ep", b), V("xq"), V("xp"))
-                scaled("s", wfF(b), bank(b, C), 0.5)
-        if ON["E"] == "F":
-            for b in range(4):
                 scaled("v", el("ft", b, h), wfF(b, h), 2.0)
-            qe, pe, lq, lp = [half(s + str(t), h) for s in ("qe", "pe", "lq", "lp")]
-            quant(qe, pe, half("ft", h, 0, 4))
-            send(t, "%d%d" % (t, z), [(lq, qe, True), (lp, pe, False)], 0.6 + 0.8 * (t + z == 0), 1.7)
+        if raw: return
+        quant(qe, pe, htile("ft", h))
+        held.append((t, "%d%d" % (t, z), [(lq, qe, True), (lp, pe, False)], 800))
+        if (t, 1) not in RAW or t not in ON["swap"]: send(*held.pop())
+        if ZW: scaled("v", htile("wf", h), htile("ft", h), 0.5)
+        elif XW or ON["ft"]:
+            for b in range(4): scaled("v", wfF(b, h), el("ft", b, h), 0.5)
 
-    def send(t, tag, pairs, cost, late):
+    def send(t, tag, pairs, size):
         dst = T.cores[rank ^ STEP[t]]
         rid, pid = topo.addr(dst)[:2]
         arr, loc, full = "arr" + tag, "loc" + tag, len(pairs) * len(topo.engines(core, dst))
@@ -434,13 +510,10 @@ def rank_program(g, core, T, topo):
             for land, src, codes in pairs:
                 log.setdefault(land[0], []).append((land, arr, full, True, "r"))
 
-        put("g", issue, [p[1] for p in pairs], [p[0] for p in pairs], cost, late)
-
-    def turned(out, a):
-        run("v", lambda: g.vector.transpose(ap(out), ap(a)), [a], [out])
-
-    def part(name, h, b):
-        return V(name, (4 * h + b) * B, (4 * h + b + 1) * B)
+        token = [("sent" + tag, 0, 1, 1), ("sends", 0, 1, 1)]
+        put("g", issue, [p[1] for p in pairs], token[:1], [len(pairs) * m["call"] + m["first"] * (not [c for c in calls if c[0] == "e"]) for m in MACHINES], 0.35)
+        put("e", lambda: None, [p[1] for p in pairs] + token[:1], [p[0] for p in pairs] + token[1:],
+            [128 * size / m["rate"] + 0.16 * len(pairs) for m in MACHINES], 0.3)
 
     r = static(0)
     products("x0", 0, 0, 0)
@@ -449,13 +522,26 @@ def rank_program(g, core, T, topo):
         k = t % 2
         nl = 5 + k
         a = r["a"]
-        tp, er = "tp%d" % t, "er%d" % t
-        pick(ON["sb"], V("sb"), V("sc"), r["oBu"])
-        tq = "tq%d" % t
-        tti(V(tq, 0, B), V("sc"), r["oAu"], V("sb"), OP.is_gt)
+        tp, er = "tp", "er%d" % t
+        if ON["sb"] == "2":
+            pick("s", V("sb", 0, 96), V("sc"), sub(r["oBu"], 0, 6))
+            pick("v", V("sb", 96, B), V("sc"), sub(r["oBu"], 6, 10))
+        else: pick(ON["sb"], V("sb"), V("sc"), r["oBu"])
+        tq = V("tda", 1, 3 * B, 3) if t in TD else place(tp, 0)
+        tti(tq, V("sc"), r["oAu"], V("sb"), OP.is_gt)
         ur, us, tc, eu, d1, e = row(), row(), tmp(10), lst(20), V("d1%d" % t), V("ne%d" % t, 5, 120, 6)
-        tti(ur, V(tq, 0, B + k), r["Mf"], V("dm%d" % t), OP.mult)
-        ts(tc, table(V(tq, 0, B), B), iw, OP.mult, 0.5, OP.is_gt)
+        if t in TD:
+            n3 = [V(z, 0, 3 * B) for z in ("td", "tda", "tdb")]
+            run("v", lambda n3=n3: g.vector.tensor_tensor_scan(ap(n3[0]), ap(n3[1]), ap(n3[2]), 0.0, OP.mult, OP.add), n3[1:], n3[:1])
+            n = ON["TD"]
+            for h in range(n):
+                pick("sv"[h], sub(ur, C // n * h, C // n * (h + 1)), V("td", 0, 3 * B + 2 * k), sub(r["Mf"], 20 // n * h, 20 // n * (h + 1)))
+            scaled(ON["tp"], place(tp, 0), tq, 1.0)
+        else: tti(ur, win0(tp, k), r["Mf"], V("dm%d" % t), OP.mult)
+        tw = table(tq, B)
+        act(tc, tw, iw2, -1.0, AF.Relu)
+        ts(tc, tw, iw, OP.mult, 0.5, OP.is_gt)
+        either("v")
         scan(us, ur)
         for z in range(2):
             tt(V("d0", 60 * z + 4, 60 * z + 60, 6), tc, r["S"], OP.is_gt)
@@ -464,48 +550,31 @@ def rank_program(g, core, T, topo):
         run("v", lambda n6=n6: g.vector.tensor_tensor_scan(ap(n6[0]), ap(n6[1]), ap(n6[2]), 0.0, OP.mult, OP.add), n6[1:], n6[:1])
         A, Bv = (10 * a, 10 * a + 10), (10 - 10 * a, 20 - 10 * a)
         ts(eu, e, iw1k, OP.mult)
-        for z in range(2):
-            scaled(ON["tp"], place(tp, z), V(tq, 0, B), 1.0 - 2.0 * z)
+        scaled(ON["tp"], place(tp, 1), tq, -1.0)
         euA, euB = sub(eu, *A), sub(eu, *Bv)
-        ne = NE[t]
-        if ON["E"] == "F":
-            le = V("le%d" % t)
-            send(t, "%d2" % t, [(le, eu, False)], 0.3, 1.5)
-        else:
-            for b in range(4):
-                pick("s", V("et", b, 128 * nl - 7 + b, 8), wfF(b), sub(euA, 0, nl), 2.0)
-                pick("v", V("et", 4 + b, 128 * nl - 3 + b, 8), wfF(b), sub(euB, 0, nl), 2.0)
-            qe, pe, lq, lp = [V(s + str(t), 0, ne) for s in ("qe", "pe", "lq", "lp")]
-            quant(qe, pe, V("et", 0, 4 * ne))
-            send(t, "%d0" % t, [(lq, qe, True), (lp, pe, False)], 0.6 + 0.8 * (t == 0), 1.7)
+        le = V("le%d" % t)
+        send(t, "%d2" % t, [(le, eu, False)], 40)
         t1 = tmp(10)
-        tt(t1, tc, r["dob"], OP.mult)
+        tt(t1, tc, r["do"], OP.mult)
         if t < 2:
-            nx, go, tw, tn = V("cur%d" % (t + 1)), V("go%d" % t), V("tw%d" % t), V("tn%d" % t)
+            nx, go = V("cur%d" % (t + 1)), V("go%d" % t)
             stay, move = (A, Bv) if t == 0 else (Bv, A)
             z = 1 - t
-            ts(sub(go, z, z + 10), sub(e, *move), iw, OP.mult, 1.0 - 2.0 * t, OP.add)
-            ts(sub(nx, 0, 10), sub(e, *stay), iw, OP.mult, 1.0 - 2.0 * t, OP.add)
-            tt(sub(nx, 42, 52) if t == 0 else sub(go, 22, 32), r["oA"], t1, OP.add)
-            tt(sub(go, 23, 33) if t == 0 else sub(nx, 42, 52), r["oB"], t1, OP.subtract)
-            if ON["shift"] == "v":
-                copy(sub(go, 10 * t, 10 * t + 23, 22), sub(go, 10 * z, 10 * z + 23, 22))
-                turned(sub(tw, 0, 32), sub(go, z, z + 32))
-                turned(sub(tw, 32, 64), sub(go, t, t + 32))
-                pick("v", tn, tw, shift[t])
-                turned(sub(nx, 10, 42), tn)
-            else:
-                sv, hv, pairs = T[go[0]], T[nx[0]], []
-                for q in range(0, 128, 16):
-                    pairs.append((hv[q + 1:q + 16, 10:42], sv[q:q + 15, 1:33]) if t == 0 else (hv[q:q + 15, 10:42], sv[q + 1:q + 16, 0:32]))
-                for y in (0, 22):
-                    if t == 0:
-                        pairs.append((hv[0:128:16, y + 11:y + 20], sv[15:128:16, y + 1:y + 10]))
-                        pairs.append((hv[0:128:16, y + 10:y + 11], sv[15:128:16, y + 10:y + 11]))
-                    else:
-                        pairs.append((hv[15:128:16, y + 10:y + 19], sv[0:128:16, y + 1:y + 10]))
-                        pairs.append((hv[15:128:16, y + 19:y + 20], sv[0:128:16, y:y + 1]))
-                dma("y", pairs, [go], [sub(nx, 0, 52)])
+            scaled("v", sub(go, z, z + 10), sub(e, *move), iw, 1.0 - 2.0 * t)
+            scaled("v", sub(nx, 0, 10), sub(e, *stay), iw, 1.0 - 2.0 * t)
+            tt(sub(nx, 50, 60) if t == 0 else sub(go, 30, 40), r["oA"], t1, OP.add)
+            tt(sub(go, 31, 41) if t == 0 else sub(nx, 50, 60), r["oB"], t1, OP.subtract)
+            sv, hv, pairs = T[go[0]], T[nx[0]], []
+            for q in range(0, 128, 16):
+                pairs.append((hv[q + 1:q + 16, 10:50], sv[q:q + 15, 1:41]) if t == 0 else (hv[q:q + 15, 10:50], sv[q + 1:q + 16, 0:40]))
+            for y in (0, 30):
+                if t == 0:
+                    pairs.append((hv[0:128:16, y + 11:y + 20], sv[15:128:16, y + 1:y + 10]))
+                    pairs.append((hv[0:128:16, y + 10:y + 11], sv[15:128:16, y + 10:y + 11]))
+                else:
+                    pairs.append((hv[15:128:16, y + 10:y + 19], sv[0:128:16, y + 1:y + 10]))
+                    pairs.append((hv[15:128:16, y + 19:y + 20], sv[0:128:16, y:y + 1]))
+            dma("y", pairs, [go], [sub(nx, 0, 60)])
         else:
             of, ofu = tmp(20), lst(20)
             tt(sub(of, 0, 10), r["oA"], t1, OP.add)
@@ -517,75 +586,118 @@ def rank_program(g, core, T, topo):
         pick("s", place(er, 0, kn - k), V("iota"), euA)
         pick("s", place(er, 1, kn - k), V("iota"), euB)
         if k: scaled("v", V(er, 16 + C - 1, 16 + C), V(er, 15, 16), 1.0)
-        pn, pf, pz, pu = tmp(20), tmp(20), tmp(20), lst(20)
+        pn, pu = tmp(20), lst(20)
         tt(pn, P, table(fr), OP.add)
         P = pn
         ts(pu, pn, iw, OP.mult, float(PB + kn), OP.add)
-        ts(pf, pn, wlo, OP.is_lt, w1k, OP.mult)
-        tt(pz, pf, pn, OP.add)
         pick(ON["mn"], mr, win0(er, kn), pu)
-        mn = table(mr)
-        vm, vl = tmp(20), lst(20)
-        tt(vm, pz, mn, OP.max)
-        ts(vl, vm, iw, OP.mult, float(B), OP.add)
-        ts(sub(mu[t + 1], 0, 10), sub(mn, 0, 10), iw, OP.mult)
-        ts(sub(mu[t + 1], 10, 20), sub(mn, 10, 20), iw, OP.mult, float(B), OP.add)
-        early = 1 - k if ALT else 1
+        if EP:
+            pv, vm, vl, mn = pu, tmp(20), lst(20), table(mr)
+            if t < 2:
+                pf = tmp(20)
+                ts(pf, pn, wlo, OP.is_lt, w1k, OP.mult)
+            if k:
+                pz, pv = tmp(20), lst(20)
+                tt(pz, pf, pn, OP.add)
+                ts(pv, pz, iw, OP.mult, float(PB + kn), OP.add)
+        elif not ZW:
+            pz, vm, vl, mn = tmp(20), tmp(20), lst(20), table(mr)
+            if t < 2:
+                pf = tmp(20)
+                ts(pf, pn, wlo, OP.is_lt, w1k, OP.mult)
+            tt(pz, pf, pn, OP.add)
+            tt(vm, pz, mn, OP.max)
+            ts(vl, vm, iw, OP.mult, float(B), OP.add)
+        if XW: mun = mates(mr)
+        else:
+            mun = lst(20)
+            ts(sub(mun, 0, 10), sub(mn, 0, 10), iw, OP.mult)
+            ts(sub(mun, 10, 20), sub(mn, 10, 20), iw, OP.mult, float(B), OP.add)
+            mun = [sub(mun, 0, 10), sub(mun, 10, 20)]
+        early = 1 - k
         for h in (early, 1 - early):
-            for b in range(4):
-                pick("s", part("ah", h, b), wfF(b, 1 - h), sub(mu[t], 10 * h, 10 * h + 10))
-            ah, af = half("ah", h, 0, 4), half("af", h, 0, 4)
+            ah, af = htile("ah", h), htile("af", h)
+            if XW: pick("s", ah, htile("ft", 1 - h), sub(mu, 40 * h, 40 * h + 40), 0.5)
+            else:
+                for b in range(4): pick("s", part("ah", h, b), wfF(b, 1 - h), mu[h])
             q = ON["af%d" % (h != early)]
             if q == "d":
                 dma("y", [(ap(af), ap(ah))], [ah], [af])
                 dma("g", [(ap(af), ap(ah))], [ah, af], [af], 2.5, True)
             else:
                 scaled(q, af, ah, 2.0)
-        zs = (1 - early, early) if ALT else (1, 0)
-        for b in range(4 if ON["E"] != "F" else 0):
-            mm(bank(b, ne), cols("eq", b), cols("ep", b), lq, lp)
-            scaled("s", V("wf", b * WD + C + 1 - k, b * WD + C + 1 - k + ne), bank(b, ne), 0.5)
-        if ON["E"] == "F":
-            for z, h in enumerate((1 - early, early) if ALT else (0, 1)):
-                for b in range(4):
-                    n = FB[1][b] if z == 0 else b + 1
-                    mm(bank(n), cols("eq", b), cols("ep", b), half("lq%d" % t, h), half("lp%d" % t, h))
-                    scaled("s", half("w2", h, b), bank(n), 0.5)
+        mu = mun
+        zs = (1 - early, early)
+        lq, lp = "lq%d" % t, "lp%d" % t
+        for z, h in enumerate(zs if ON["F2"] == 2 else (0,)):
             for b in range(4):
-                for z, blk in enumerate((A, Bv)):
-                    at = b * WD + C + 1 - k + z
-                    pick("sv"[z], V("wf", at, at + 32 * nl - 1, 2), V("w2", b * C, b * C + C), sub(le, blk[0], blk[0] + nl))
+                n = bank(FB[1][b] if z == ON["bank"] else b + 1) if ON["F2"] == 2 else bank((1, 2, 3, 5)[b], C)
+                q, p = (half(lq, h), half(lp, h)) if ON["F2"] == 2 else (V(lq), V(lp))
+                if (t, z) in RAW:
+                    for c in range(0 if b else 4):
+                        n2 = bank(c + 1 if z == 0 else FB[1][c])
+                        mm(n2, cols("eq", c), cols("ep", c), q, p)
+                        scaled("s", el("ft", c, h), n2, 1.0)
+                    if z: n = bank(b + 1)
+                    q, p = half("qe%d" % t, h), half("pe%d" % t, h)
+                    if not b: quant(q, p, htile("ft", h))
+                mm(n, cols("eq", b), cols("ep", b), q, p)
+                at = ("wf", b * WD + C + 1 + B * h) if EP else ("w2", b * C + B * h)
+                scaled("s", V(at[0], at[1], at[1] + n[2]), n, 0.5)
+        if EP:
+            for z, blk in enumerate((A, Bv)):
+                pick("sv"[z], place(er, z, kn - k + (C + 1) * k, 16 * nl), V("iota"), sub(le, blk[0], blk[0] + nl))
+            vwin, n = V(er, 16, 16 + C + 1 + B) if k else win0(er, kn), ON["PH"]
+            for h in range(n) if n == 1 else zs:
+                c0, c1 = 20 // n * h, 20 // n * (h + 1)
+                pick("s", V("vr", 16 * c0, 16 * c1), vwin, sub(pv, c0, c1))
+                scan(V("vt4", 16 * c0, 16 * c1), V("vr", 16 * c0, 16 * c1))
+                tt(sub(vm, c0, c1), tab(V("vt4", 16 * c0, 16 * c1)), sub(pf, c0, c1), OP.add)
+                ts(V("vl%d" % t, c0, c1), sub(vm, c0, c1), iw, OP.mult, float(B), OP.add)
+            vl = V("vl%d" % t, 0, 20)
+        for b in range(0 if EP else 4):
+            for z, blk in enumerate((A, Bv)):
+                at, step = (4 * (C + 1 - k + z) + b, 8) if ZW else (b * WD + C + 1 - k + z, 2)
+                pick("sv"[z], V("wf", at, at + step * (16 * nl - 1) + 1, step), V("w2", b * C, b * C + C), sub(le, blk[0], blk[0] + nl))
+        if ZW:
+            vwin, vl = win0("vw%d" % kn, kn), V("vl%d" % t)
+            scaled("v", V(vwin[0], 16 + kn + B, 16 + kn + C), V(er, 16 + kn + B, 16 + kn + C), 1.0, -float(MID))
+            pick("s", V("vr"), vwin, pu)
+            scan(V("vt4"), V("vr"), 4)
+            ts(vl, tab(V("vt4"), 4), iq4, OP.mult, lb2, OP.add)
         for z, h in enumerate(zs):
-            for b in range(4):
-                tti(el("zt", b, h), wf(b), sub(vl, 10 * h, 10 * h + 10), part("ah", h, b), OP.add)
-            quant(half("zq", h), half("zp", h), half("zt", h, 0, 4))
+            if ZW: tti(htile("zt", h), V("wf", 0, 4 * (C + 1 + B)), sub(vl, 40 * h, 40 * h + 40), htile("ah", h), OP.add)
+            else:
+                for b in range(4):
+                    tti(el("zt", b, h), V("wf", b * WD, b * WD + C + 1 + (C if EP else B)), sub(vl, 10 * h, 10 * h + 10), part("ah", h, b), OP.add)
+            quant(half("zq", h), half("zp", h), htile("zt", h))
             for b in range(4):
                 n = 4 * z + b
                 mm(bank(n), cols("wq", b), cols("wp", b), half("zq", h), half("zp", h))
-                scaled("s", half("gs", h, b), bank(n), 0.0078125)
+                scaled("s", part("gs", h, b), bank(n), 0.0078125)
         if t < 2:
             r = static(t + 1)
         else:
             quant(V("vq"), V("vp"), V("vt"))
-            actb(V("romo", 0, C - 1, 2), V("iota"), sub(ofu, 0, 10), float(B))
-            actb(V("romo", 1, C, 2), V("iota"), sub(ofu, 10, 20), float(B))
-            act(V("romm"), mr, 1.0, float(B))
-            ts(V("romm"), mr, float(B), OP.add)
-            either("s")
+            pick("s", V("romo", 0, C - 1, 2), V("iota"), sub(ofu, 0, 10), bias=float(B))
+            pick("s", V("romo", 1, C, 2), V("iota"), sub(ofu, 10, 20), bias=float(B))
+            scaled("s", V("romm"), mr, 1.0, float(B))
             dma("y", [(T.om[:, 0:C], T.romo[0:128:16, :]), (T.om[:, C:2 * C], T.romm[0:128:16, :])], [V("romo"), V("romm")], [])
         for z, h in enumerate(zs[::-1]):
-            for b in range(4):
-                tti(el("xt", b, h), half("gs", 1 - h, b), sub(mu[t + 1], 10 * h, 10 * h + 10), part("af", h, b), OP.add)
+            if XW: tti(htile("xt", h), htile("gs", 1 - h), sub(mu, 40 * h, 40 * h + 40), htile("af", h), OP.add)
+            else:
+                for b in range(4):
+                    tti(el("xt", b, h), part("gs", 1 - h, b), mu[h], part("af", h, b), OP.add)
             if t < 2:
                 products("xt", h, z, t + 1)
             else:
                 q, p = half("xq", h), half("xp", h)
-                quant(q, p, half("xt", h, 0, 4))
+                quant(q, p, htile("xt", h))
                 mm(bank(h), V("vq"), V("vp"), q, p)
                 dma("y", [(T.oc[:, 4 * B * h:4 * B * h + 4 * B], by(q))]
                     + [(T.osc[4 * z:4 * z + 4, B * h:B * h + B], T.xp[32 * z:32 * z + 4, B * h:B * h + B]) for z in range(4)], [q, p], [], 2.5)
                 scaled("s", half("ysb", h), bank(h), 1.0)
-                dma("s", [(T.y[:, B * h:B * h + B], ap(half("ysb", h)))], [half("ysb", h)], [], 2.5)
+                dma("ys"[z], [(T.y[:, B * h:B * h + B], ap(half("ysb", h)))], [half("ysb", h)], [], 2.5)
     if "plan" not in PLAN:
         seen, before = {}, []
         for i, (q, issue, reads, writes, cost, late, other) in enumerate(calls):
@@ -596,9 +708,10 @@ def rank_program(g, core, T, topo):
                         if v[0][:2] == "ps" or ((isw or oldw) and clash(v, old)): p.add(j)
             for vs, isw in ((reads, False), (writes, True)):
                 for v in vs: seen.setdefault(v[0], []).append((v, i, isw))
+            if q == "g" and late: p.update(j for j in range(i) if calls[j][0] == "g" and not calls[j][5])
             before.append(sorted(p))
         PLAN["plan"] = plan([(c[0], c[4], c[5]) for c in calls], before, [c[6] and (c[6][0], c[6][4]) for c in calls])
-    for i, q in PLAN["plan"]:
+    for i, q in sorted(PLAN["plan"], key=lambda c: min(c[0], first)):
         (calls[i] if calls[i][0] == q else calls[i][6])[1]()
     for sem, n in count.items():
         know("g", sem, n)
@@ -607,10 +720,11 @@ def rank_program(g, core, T, topo):
 PLAN = {}
 WAKE, OWN = 0.22, 0.17
 PASSES = 6
+QUEUES = "vstgye"
 
 
 def lay(ops, before, rank, back):
-    at, busy = [0.0] * len(ops), {q: [] for q in "vstgy"}
+    at, busy = [0.0] * len(ops), {q: [] for q in QUEUES}
     for i in rank:
         q, cost, late = ops[i]
         t = late if back and not before[i] else 0.0
@@ -627,7 +741,8 @@ def lay(ops, before, rank, back):
 
 
 def plan(ops, before, other):
-    n = len(ops)
+    n, every = len(ops), ops
+    ops = [(q, cost[0], late) for q, cost, late in ops]
     after = [[] for i in range(n)]
     for i in range(n):
         for j in before[i]: after[j].append(i)
@@ -642,16 +757,21 @@ def plan(ops, before, other):
         late = lay(ops, after, sorted(range(n), key=lambda i: (-at[i] - ops[i][1], -i)), True)
         rank = sorted(range(n), key=lambda i: (-late[i] - ops[i][1], i))
     PLAN["end"] = best[0]
-    return polish(ops, before, after, other, sorted(range(n), key=lambda i: (best[1][i], i)))
+    seq = sorted(range(n), key=lambda i: (best[1][i], i))
+    best = min(polish(every, before, after, other, seq, SEED + k) for k in range(STARTS))
+    PLAN["ends"] = best[2:]
+    return best[1]
 
 
-MACHINES = [(1.0, 0.0, 0.17, 0.2, True), (1.0, -0.3, 0.17, 0.23, False), (1.35, 1.3, 0.15, 0.2, False)]
-TRIES, SOON, HEAT, REACH, AIM = 240000, 0.2, 0.0002, 30, 0.5
+MACHINES = [dict(zip(("compute", "gather", "act", "product", "call", "rate", "more", "own", "wake", "hide", "first"), m)) for m in (
+    (1.0, 1.25, 0.07, 1.3, 0.3, 200e3, 0.15, 0.17, 0.2, True, 0.8), (1.0, 1.15, 0.06, 1.2, 0.3, 200e3, 0.0, 0.2, 0.23, False, 0.8),
+    (1.4, 1.5, 0.09, 1.4, 0.4, 150e3, 0.5, 0.17, 0.2, False, 0.8))]
+TRIES, SOON, HEAT, REACH, AIM, SEED, STARTS = 300000, 0.2, 0.0005, 30, 0.5, 5, 1
 
 
-def polish(ops, before, after, other, seq):
+def polish(ops, before, after, other, seq, seed):
     n = len(ops)
-    qn = ["vstgy".index(o[0]) for o in ops]
+    qn = [QUEUES.index(o[0]) for o in ops]
     known, need = [0] * n, []
     for i in range(n):
         keep, a = [], 0
@@ -662,23 +782,32 @@ def polish(ops, before, after, other, seq):
         known[i] = a
         need.append(keep)
     sets = []
-    for fac, more, own, wake, hide in MACHINES:
-        cost = [{qn[i]: ops[i][1] * (fac if ops[i][0] in "vst" else 1.0)} for i in range(n)]
+    for k, m in enumerate(MACHINES):
+        cost = [{qn[i]: ops[i][1][k]} for i in range(n)]
         for i in range(n):
-            if other[i]: cost[i]["vs".index(other[i][0])] = other[i][1] * fac
-        sets.append((cost, [o[2] + more if o[2] else 0.0 for o in ops], own, wake, hide))
+            if other[i]: cost[i]["vs".index(other[i][0])] = other[i][1][k]
+        sets.append((cost, [o[2] + m["more"] if o[2] else 0.0 for o in ops], m["own"], m["wake"], m["hide"]))
 
-    def walk(seq, lo, end, m):
-        cost, late, own, wake, hide = m
-        free, k, left = [0.0] * 5, lo - 1, set(range(5))
+    def tops(seq, lo):
+        top, k, left = [-1] * 6, lo - 1, 7
         while left and k >= 0:
             i = seq[k]
-            if qn[i] in left:
-                left.discard(qn[i])
-                free[qn[i]] = end[i] - late[i]
+            if left >> qn[i] & 1:
+                left &= ~(1 << qn[i])
+                top[qn[i]] = i
             k -= 1
+        for q in (3, 4, 5):
+            k = -1
+            for i in rare[q]:
+                if k < pos[i] < lo: k, top[q] = pos[i], i
+        return top
+
+    def walk(seq, lo, hi, end, m, top, moved=63):
+        cost, late, own, wake, hide = m
+        free = [end[i] - late[i] if i >= 0 else 0.0 for i in top]
         end = list(end)
-        for i in seq[lo:]:
+        for k in range(lo, n):
+            i = seq[k]
             q = qn[i]
             t = f = free[q]
             for j in need[i]:
@@ -688,25 +817,36 @@ def polish(ops, before, after, other, seq):
                     if e > t: t = e
             t += cost[i][q]
             free[q] = t
-            end[i] = t + late[i]
+            t += late[i]
+            if t != end[i]:
+                end[i] = t
+                moved |= 1 << q
+                if reach[i] > hi: hi = reach[i]
+            elif k > hi:
+                moved &= ~(1 << q)
+                if not moved: break
         return end
 
     def worth(end):
         return max(end) + SOON * sum(end) / n
 
-    ends = [walk(seq, 0, [0.0] * n, m) for m in sets]
-    base = [worth(e) for e in ends]
-    now, rng = 1.0, np.random.RandomState(4)
-    best = (now, seq, list(qn))
-    pos = [0] * n
+    pos, users = [0] * n, [[] for i in range(n)]
     for k, i in enumerate(seq): pos[i] = k
+    for i in range(n):
+        for j in need[i]: users[j].append(i)
+    reach = [max([pos[j] for j in users[i]] + [0]) + 1 for i in range(n)]
+    rare = [[i for i in range(n) if qn[i] == q] for q in range(6)]
+    ends = [walk(seq, 0, n, [0.0] * n, m, [-1] * 6) for m in sets]
+    base = [worth(e) for e in ends]
+    now, rng, last = 1.0, np.random.RandomState(seed), [1.0] * len(sets)
+    best = (now, seq, list(qn), [max(e) for e in ends])
     for turn in range(TRIES):
         if turn % 100 == 0:
             m = turn // 100 % len(sets)
-            end, cost, late, last, prev, block = ends[m], sets[m][0], sets[m][1], {}, {}, []
+            end, cost, late, top, prev, block = ends[m], sets[m][0], sets[m][1], {}, {}, []
             for j in seq:
-                prev[j] = last.get(qn[j], -1)
-                last[qn[j]] = j
+                prev[j] = top.get(qn[j], -1)
+                top[qn[j]] = j
             i = end.index(max(end))
             while i >= 0:
                 p, t = prev[i], end[i] - late[i] - cost[i][qn[i]]
@@ -727,17 +867,19 @@ def polish(ops, before, after, other, seq):
         elif b == a or not [j for j in seq[min(a, b):max(a, b) + 1] if j != i and qn[j] == qn[i]]: continue
         new = seq[:a] + seq[a + 1:]
         new.insert(b, i)
-        total, got = 0.0, []
+        total, got, top = 0.0, [], tops(seq, min(a, b))
         for m, e, w in zip(sets, ends, base):
-            got.append(walk(new, min(a, b), e, m))
+            got.append(walk(new, min(a, b), max(a, b, reach[i]), e, m, top, 3 | 1 << qn[i]))
             r = worth(got[-1]) / w
             total += r / len(sets)
-            if r > lim + 0.03: total += 9.0
+            if r > last[len(got) - 1] + 0.006: total += 9.0
             if total > lim: break
         if total <= lim:
             now, seq, ends = total, new, got
+            last = [worth(e) / w for e, w in zip(ends, base)]
             for k in range(min(a, b), max(a, b) + 1): pos[seq[k]] = k
-            if now < best[0]: best = (now, seq, list(qn))
+            for k in range(min(a, b), max(a, b) + 1):
+                for j in need[seq[k]]: reach[j] = max([pos[u] for u in users[j]]) + 1
+            if now < best[0]: best = (now, seq, list(qn), [max(e) for e in ends])
         elif flip: qn[i] = 1 - qn[i]
-    PLAN["gain"] = best[0]
-    return [(i, "vstgy"[best[2][i]]) for i in best[1]]
+    return best[0], [(i, QUEUES[best[2][i]]) for i in best[1]], best[3]

import math
import numpy as np
from concourse.mybir import dt, AluOpType as OP, ActivationFunctionType as AF

C, B = 320, 160
STEP = [1, 2, 4]
F8, BF, F32, U16, U8, I32 = "float8_e4m3fn_x4", "bfloat16", "float32", "uint16", "uint8", "int32"
CYCLE = 0.00093
BIG = 2.0 ** 40
HUGE = 2.0 ** 90
WD = C + 208
MID = 81
ON = {"sb": "2", "p": "s", "mn": "s", "af0": "s", "af1": "v", "pm0": "v", "pm1": "s", "M0": "v", "M1": "s",
      "x0": "s", "sc0": "s", "sc1": "v", "tp": "v", "X": "n", "Z": "n", "F2": 2, "late": 1, "ft": 1, "E": "e", "PH": 2, "TD": 2, "G": 1, "bank": 1, "G2": "s", "G3": "g", "swap": (0, 1, 2)}
TD = (0, 1, 2)
RAW = [(1, 1), (2, 1)]
XW, ZW, EP = ON["X"] == "w", ON["Z"] == "w", ON["E"] == "p"
WD = 2 * C + 16 if EP else WD
PB = B if ZW else 839

SCRATCH = {
    "oi": ("sbuf", [128, 20], I32), "mi": ("sbuf", [128, 20], I32),
    "x0": ("sbuf", [128, 4 * C], BF), "ut": ("sbuf", [128, 512], BF), "vt": ("sbuf", [128, 512], BF),
    "wq": ("sbuf", [128, 512], F8), "wp": ("sbuf", [128, 512], U8),
    "uq": ("sbuf", [128, 128], F8), "up": ("sbuf", [128, 128], U8),
    "uq16": ("sbuf", [128, 128], F8), "up16": ("sbuf", [128, 128], U8),
    "vq": ("sbuf", [128, 128], F8), "vp": ("sbuf", [128, 128], U8),
    "ect": ("sbuf", [128, 516], BF), "ones": ("sbuf", [128, 516], BF),
    "eq": ("sbuf", [128, 512], F8), "ep": ("sbuf", [128, 512], U8),
    "iota": ("sbuf", [128, C], BF), "cw": ("sbuf", [128, C], BF),
    "six": ("sbuf", [128, 128], BF), "d0": ("sbuf", [128, 128], F32),
    "k16": ("sbuf", [128, 16], BF), "kk": ("sbuf", [128, C], BF), "k4": ("sbuf", [128, 16], BF), "kw": ("sbuf", [128, C], BF),
    "pcol": ("sbuf", [128, 8], I32), "pcol2": ("sbuf", [128, 8], I32), "ulu": ("sbuf", [128, 8], U16),
    "tb": ("sbuf", [128, 3000], F32), "ub": ("sbuf", [128, 1400], U16),
    "orow": ("sbuf", [128, C], BF), "prow": ("sbuf", [128, C], BF),
    "pmrow": ("sbuf", [128, C], BF), "xrow": ("sbuf", [128, C], BF), "Mrow": ("sbuf", [128, C], BF),
    "wf": ("sbuf", [128, 4 * WD], BF), "w2": ("sbuf", [128, 4 * C], BF), "ft": ("sbuf", [128, 4 * C], BF),
    "ah": ("sbuf", [128, 4 * C], BF), "af": ("sbuf", [128, 4 * C], BF),
    "zt": ("sbuf", [128, 4 * C], BF), "xt": ("sbuf", [128, 4 * C], BF),
    "zq": ("sbuf", [128, C], F8), "zp": ("sbuf", [128, C], U8),
    "xq": ("sbuf", [128, C], F8), "xp": ("sbuf", [128, C], U8),
    "gs": ("sbuf", [128, 4 * C], F32), "sc": ("sbuf", [128, 2 * C], F32), "sb": ("sbuf", [128, B], F32),
    "ysb": ("sbuf", [128, C], F32), "romo": ("sbuf", [128, C], F32), "romm": ("sbuf", [128, C], F32),
    "vr": ("sbuf", [128, C], BF), "vt4": ("sbuf", [128, C], BF), "tp": ("sbuf", [128, 352], BF),
    "td": ("sbuf", [128, 496], BF), "tda": ("sbuf", [128, 480], BF), "tdb": ("sbuf", [128, 480], BF),
}
for _t in range(3):
    for _n, _d in (("qe", F8), ("pe", U8), ("lq", F8), ("lp", U8)):
        SCRATCH[_n + str(_t)] = ("sbuf", [128, C], _d)
    SCRATCH["le%d" % _t] = ("sbuf", [128, 20], U16)
    SCRATCH["vl%d" % _t] = ("sbuf", [128, 80], U16)
    for _n, _w, _d in (("dr", 352, BF), ("er", 560, BF), ("dm", C, BF), ("cur", 80, F32),
                       ("d1", 128, F32), ("ne", 128, F32), ("vi", 60, I32)):
        SCRATCH[_n + str(_t)] = ("sbuf", [128, _w], _d)
for _t in range(2):
    SCRATCH["go%d" % _t] = ("sbuf", [128, 48], F32)
    SCRATCH["vw%d" % _t] = ("sbuf", [128, 352], BF)
SCRATCH["rows"] = ("sbuf", [128, 33 * C], BF)
for _k in range(8):
    SCRATCH["ps%d" % _k] = ("psum", [128, 512], F32)
SEMAPHORES = ["vs", "ss", "ts", "gs"] + ["d%d" % k for k in range(32)] + [s + "%d%d" % (t, k) for s in ("arr", "loc") for t in range(3) for k in range(3)]


def rank_program(g, core, T, topo):
    rank = T.rank_of(core)
    if rank is None:
        return
    queue = {"v": g.vector, "s": g.scalar, "t": g.tensor, "g": g, "y": g.sync}
    semof = {"v": "vs", "s": "ss", "t": "ts", "g": "gs"}
    count = {}
    clock = {q: {} for q in queue}
    snap = {}
    log = {}
    ndma = [0]

    def V(name, lo=0, hi=None, step=1):
        return (name, lo, SCRATCH[name][1][1] if hi is None else hi, step)

    def ap(v):
        if not isinstance(v, tuple): return v
        return T[v[0]][:, v[1]:v[2]:v[3]] if v[3] != 1 else T[v[0]][:, v[1]:v[2]]

    def by(v):
        return ap(v).bitcast(dt.uint8)

    def ind(win, off):
        return ap(win).indirect(ap(off))

    def views(*a):
        return [v for v in a if isinstance(v, tuple)]

    def clash(a, b):
        if a[1] >= b[2] or b[1] >= a[2]: return False
        if a[3] == b[3] and a[3] > 1: return (a[1] - b[1]) % a[3] == 0
        return True

    def know(q, sem, val):
        if clock[q].get(sem, 0) >= val: return
        queue[q].wait_ge(T.sem[sem], val)
        for s, n in list(snap.get((sem, val), {}).items()) + [(sem, val)]:
            if clock[q].get(s, 0) < n: clock[q][s] = n

    def order(q, reads, writes):
        need = {}
        for vs, isw in ((reads, False), (writes, True)):
            for v in vs:
                psum = v[0][:2] == "ps"
                for (w, sem, val, oldw, oq) in log.get(v[0], ()):
                    if (isw or oldw or (psum and oq != q)) and (psum or clash(v, w)):
                        if need.get(sem, 0) < val: need[sem] = val
        for sem, val in sorted(need.items(), key=lambda k: -k[1]):
            know(q, sem, val)

    def note(q, sem, val, reads, writes):
        snap[(sem, val)] = dict(clock.get(q, {}))
        for vs, isw in ((reads, False), (writes, True)):
            for v in vs:
                old = log.setdefault(v[0], [])
                if isw:
                    old[:] = [r for r in old if not (v[3] == 1 and v[1] <= r[0][1] and r[0][2] <= v[2])]
                old.append((v, sem, val, isw, q))

    calls = []

    def put(q, issue, reads, writes, cost, late=0.0):
        calls.append((q, issue, reads, writes, cost, late, None))

    def run(q, fn, reads, writes, kind=""):
        def issue():
            order(q, reads, writes)
            s = semof[q]
            count[s] = count.get(s, 0) + 1
            fn().then_inc(T.sem[s], 1)
            note(q, s, count[s], reads, writes)
        o = writes[0]
        n = (o[2] - o[1] + o[3] - 1) // o[3]
        narrow = all(SCRATCH[v[0]][2] in (BF, U16) for v in reads + writes if v[2] - v[1] > 1)
        psum = any(v[0][:2] == "ps" for v in reads)
        cs = []
        for m in MACHINES:
            if kind == "ind": c = 0.06 + m["gather"] * CYCLE * n
            elif kind == "scat": c = 3.0 * m["gather"] * CYCLE * n
            elif kind == "q": c = 0.015 + 4 * 0.00025 * n
            elif q == "t": c = (n + 16) * CYCLE * m["product"]
            elif q == "g": c = 0.18 + 2 * CYCLE * n
            elif q == "s": c = CYCLE * max(n, 64) + m["act"]
            else: c = 0.01 + CYCLE * max(64, n * (2 if kind == "tt" and not psum else 0.5 if narrow else 1))
            cs.append(c * m["compute"])
        put(q, issue, reads, writes, cs)

    def dma(q, pairs, reads, writes, late=2.2, add=False):
        def issue():
            order(q, reads, writes)
            s = "d%d" % ndma[0]
            ndma[0] += 1
            for o, i in pairs:
                (g.dma_start(o, i, accum_op=OP.add) if add else queue[q].dma_start(o, i)).then_inc(T.sem[s], 16)
            count[s] = 16 * len(pairs)
            note(q, s, count[s], reads, writes)
        put(q, issue, reads, writes, [(1.0 if add else 0.07) * len(pairs) for m in MACHINES], late)

    def copy(out, a):
        run("v", lambda: g.vector.tensor_copy(ap(out), ap(a)), [a], [out])

    def tt(out, a, b, op):
        run("v", lambda: g.vector.tensor_tensor(ap(out), ap(a), ap(b), op), [a, b], [out], "tt")

    def ts(out, a, s1, op0, s2=None, op1=None):
        if op1 is None:
            run("v", lambda: g.vector.tensor_scalar(ap(out), ap(a), ap(s1), None, op0), [a] + views(s1), [out])
        else:
            run("v", lambda: g.vector.tensor_scalar(ap(out), ap(a), ap(s1), ap(s2), op0, op1), [a] + views(s1, s2), [out])

    def tti(out, win, off, b, op):
        run("v", lambda: g.vector.tensor_tensor(ap(out), ind(win, off), ap(b), op), [win, off, b], [out], "ind")

    def fill(out, c):
        run("v", lambda: g.vector.memset(ap(out), c), [], [out])

    def act(out, a, scale=1.0, bias=None, fn=None):
        if bias is None and not views(scale) and not fn: run("s", lambda: g.scalar.activation(ap(out), ap(a), AF.Copy, scale=scale), [a], [out])
        else: run("s", lambda: g.scalar.activation(ap(out), ap(a), fn or AF.Identity, bias=ap(bias or 0.0), scale=ap(scale)), [a] + views(scale, bias), [out])

    def either(q):
        v, s = calls.pop(), calls.pop()
        calls.append((s if q == "s" else v)[:6] + ((v if q == "s" else s),))

    def scaled(q, out, a, scale, bias=None):
        act(out, a, scale, bias)
        if bias is None: ts(out, a, scale, OP.mult)
        else: ts(out, a, scale, OP.mult, bias, OP.add)
        either(q)

    def const(out, c, q="s"):
        if q == "g" and ON["G"]: return iota(out, [[0, (out[2] - out[1] + out[3] - 1) // out[3]]], int(c), 0)
        scaled("s", out, V("ones", 0, (out[2] - out[1] + out[3] - 1) // out[3]), c)

    def pick(q, out, win, off, scale=1.0, bias=None):
        r = [win, off] + views(scale)
        if bias is not None:
            run("s", lambda: g.scalar.activation(ap(out), ind(win, off), AF.Identity, bias=bias), r, [out], "ind")
            run("v", lambda: g.vector.tensor_scalar(ap(out), ind(win, off), bias, None, OP.add), r, [out], "ind")
        else:
            run("s", lambda: g.scalar.activation(ap(out), ind(win, off), AF.Identity if views(scale) else AF.Copy, scale=ap(scale)), r, [out], "ind")
            if scale == 1.0: run("v", lambda: g.vector.tensor_copy(ap(out), ind(win, off)), r, [out], "ind")
            else: run("v", lambda: g.vector.tensor_scalar(ap(out), ind(win, off), ap(scale), None, OP.mult), r, [out], "ind")
        either(q)

    def quant(q, p, a):
        run("v", lambda: g.vector.quantize_mx(ap(q), ap(p), ap(a)), [a], [q, p], "q")

    def mm(out, l, lp, r, rp):
        run("t", lambda: g.tensor.matmul_mx(ap(out), ap(l), ap(lp), ap(r), ap(rp), True, True), [l, lp, r, rp], [out])

    def iota(out, pattern, base, cm):
        run("g", lambda: g.iota(ap(out), pattern, base, cm, allow_small_or_imprecise_dtypes=True), [], [out])

    ntb, nub, nrow = [0], [0], [0]

    def tmp(n):
        ntb[0] += n
        return V("tb", ntb[0] - n, ntb[0])

    def lst(n):
        nub[0] += n + n % 2
        return V("ub", nub[0] - n - n % 2, nub[0] - n % 2)

    def row(n=C):
        nrow[0] += 1
        return V("rows", C * (nrow[0] - 1), C * (nrow[0] - 1) + n)

    def sub(v, lo, hi, step=1):
        if v[3] == 1: return (v[0], v[1] + lo, v[1] + hi, step)
        return (v[0], v[1] + lo * v[3], min(v[2], v[1] + (hi - 1) * v[3] + 1), v[3] * step)

    def tab(v, n=16):
        return (v[0], v[1] + n - 1, v[2], n)

    def scan(out, data, n=16):
        h = V("kk" if n == 16 else "kw", 0, out[2] - out[1])
        run("v", lambda: g.vector.tensor_tensor_scan(ap(out), ap(h), ap(data), 0.0, OP.mult, OP.add), [h, data], [out])

    def table(data, n=C):
        out = row(n)
        scan(out, data)
        return tab(out)

    def win0(name, k):
        return V(name, 16, 16 + C + k)

    def place(name, e, s=0, n=B):
        return V(name, 16 + e + s, 16 + e + s + 2 * n - 1, 2)

    def el(name, b, h, n=1):
        return V(name, 4 * B * h + b, 4 * B * (h + n) - 3 + b, 4)

    def half(name, h, b=0, w=1):
        return V(name, (b * C + B * h) * w, (b * C + B * h + B) * w)

    def htile(name, h):
        return half(name, h, 0, 4)

    def part(name, h, b):
        return el(name, b, h) if XW else V(name, (4 * h + b) * B, (4 * h + b + 1) * B)

    def wfF(b, h):
        return el("wf", b, h) if ZW else V("wf", b * WD + B * h, b * WD + B * h + B)

    def cols(name, b, n=128):
        return V(name, n * b, n * b + n)

    def bank(k, n=B):
        return V("ps%d" % k, 0, n)

    dma("y", [(T.oi[:], T.o[:])], [], [V("oi")], 1.9)
    dma("s", [(T.mi[:], T.m[:])], [], [V("mi")], 1.9)
    dma("y", [(T.ut[:], T.u[:])], [], [V("ut")], 2.6)
    dma("s", [(T.x0[:, 0:4 * B], T.x[:, 0:4 * B])], [], [htile("x0", 0)], 3.0)
    dma("y", [(T.x0[:, 4 * B:4 * C], T.x[:, 4 * B:4 * C])], [], [htile("x0", 1)], 3.6)
    first = len(calls)
    behind = [V("x0")] if ON["late"] else []
    dma("y", [(by(V("wq")), T.wc[:]), (T.wp[:], T.ws[:]), (T.vt[:], T.v[:])], behind, [V("wq"), V("wp"), V("vt")], 4.0)

    iota(V("pcol"), [[0, 8]], 0, 1)
    fill(V("ones"), 1.0)
    run("g", lambda: g.affine_select(T.ect[:], T.ones[:], [[1, 516]], OP.is_equal, 0.0, -3, -4), [V("ones")], [V("ect")])
    one = V("ones", 0, C)
    run("v", lambda: g.vector.tensor_tensor_scan(T.iota[:], ap(one), ap(one), -1.0 - B, OP.mult, OP.add), [one], [V("iota")])
    lane = tmp(3)
    pm, lb, la = sub(lane, 0, 1), sub(lane, 1, 2), sub(lane, 2, 3)
    ts(V("pcol2", 0, 1), V("pcol", 0, 1), 15, OP.bitwise_and)
    if XW:
        ts(V("pcol2", 1, 2), V("pcol", 0, 1), 3, OP.bitwise_and)
        ts(V("pcol2", 2, 3), V("pcol", 0, 1), 15, OP.bitwise_and, 2, OP.logical_shift_right)
    copy(sub(lane, 0, 1 + 2 * XW), V("pcol2", 0, 1 + 2 * XW))
    pm2 = tmp(1)
    scaled("s", pm2, pm, 2.0, float(B))
    for own, at, n, short, long in ((pm, pm, 16, "k16", "kk"), (la, lb, 4, "k4", "kw"))[:1 + XW]:
        c0, c1, k1, k2, lanes = tmp(1), tmp(1), tmp(16), tmp(16), lst(20)
        scaled("s", c0, own, 1.0, -float(B))
        scaled("s", c1, own, 1.0, 1.0 - B)
        ts(k1, V("iota", 0, 16), c0, OP.not_equal)
        ts(k2, V("iota", 0, 16), c1, OP.is_equal, BIG, OP.mult)
        tt(V(short), k1, k2, OP.add)
        ts(lanes, V("iota", 0, 20), 0.0, OP.mult, at, OP.add)
        pick("s", V(long), V(short), lanes)
    for t in range(2):
        const(V("go%d" % t, 8, 32), 0.0, "g")
    w, iw, iw2, iw1k, wv, wlo, w1k, no0, no1, iq, iq4, lb1, lb2, wb = [tmp(1) for k in range(14)]
    ts(no1, pm, 15.0, OP.is_lt)
    scaled("s", w, no1, BIG, 1.0)
    ts(iw, pm, 15.0, OP.is_equal, 1.0 / BIG, OP.max)
    scaled("s", iw2, iw, 2.0)
    scaled("s", iw1k, iw, 1.0 / 1024)
    scaled("s", wv, w, 1025.0 * B)
    ts(no0, pm, 0.0, OP.is_gt)
    if XW:
        ts(iq, la, 3.0, OP.is_equal, 1.0 / BIG, OP.max)
        scaled("s", iq4, iq, 4.0)
        scaled("s", lb1, lb, 1.0, 4.0 * B)
    if ZW:
        scaled("s", lb2, lb, 1.0, 4.0 * (B + MID))
        for k in range(2):
            scaled("s", V("vw%d" % k, 16 + k, 16 + k + B), V("iota", 0, B), 1.0, float(C + 1 - MID))
        const(V("vw1", 16, 17), 0.0)
        const(V("wf", 4 * C, 4 * C + 4), 0.0)
    else:
        scaled("s", wlo, w, float(B - PB))
        scaled("s", w1k, w, C + 1.0 if EP else 1000.0)
        const(V("wf", C, 4 * WD, WD), 0.0, ON["G2"])
    KB, KBw = tmp(20), tmp(20)
    for z in range(2):
        scaled("s", sub(KB, 10 * z, 10 * z + 10), V("iota", 1, C, 32), 1.0, pm2)
    scaled("s", wb, w, -float(B))
    scaled("s", KBw, KB, w, wb)
    const(V("d0", 1, 120, 2), 1.0, "g")
    if ON["G"]: iota(V("d0", 0, 120, 2), [[0, 20], [-1, 3]], 0, 0)
    else:
        const(V("d0", 0, 120, 6), 0.0)
        const(V("d0", 2, 120, 6), -1.0)
    six = lst(8)
    iota(V("six", 60, 128), [[0, 68]], -B, 0)
    for z, (step, first) in enumerate(((1, 0), (16, 15))):
        for j in range(3):
            iota(V("six", 64 * z + j, 64 * z + 60, 3), [[step * (10 - 20 * (j % 2)), 2], [step, 10]], first + 10 * step * (j % 2) - B, 0)
    ts(six, table(V("six", 0, 128), 128), iw, OP.mult, float(B), OP.add)
    if ON["G"]: iota(V("cw", 1, C), [[1024, C - 1]], 1024 * (1 - B), 0)
    else: scaled("s", V("cw", 1, C), V("iota", 1, C), 1024.0)
    const(V("cw", 0, 1), 1.0, ON["G2"])
    for v in [V("er0", 16, 17), V("tdb")] + ([V("tp", 336, 337), V("td", 3 * B, 3 * B + 2)] if 1 in TD else [V("tp", 336, 337), V("dr1", 336, 337)]) if TD \
            else [V("tp", 16, 337), V("dr1", 336, 337), V("er0", 16, 17)]:
        const(v, 0.0, "s" if v[0] == "tdb" else ON["G2"])
    for lo, hi in ((0, C - 1), (C + 2, 2 * C - 1)): const(V("sc", lo, hi, 2), 0.0, ON["G3"])
    const(V("sc", C, C + 1), HUGE)
    if TD:
        const(V("tda", 0, 3 * B, 3), 0.0, "g")
        const(V("tda", 2, 3 * B, 3), -1.0, "g")
    for b in range(4):
        quant(cols("eq", b), cols("ep", b), V("ect", 3 - b, 515 - b))
    ts(V("ulu"), V("iota", 0, 128, 16), float(B), OP.add)

    def mates(mr):
        m4, mu = row(), lst(80)
        scan(m4, mr, 4)
        ts(sub(mu, 0, 40), sub(tab(m4, 4), 0, 40), iq4, OP.mult, lb, OP.add)
        ts(sub(mu, 40, 80), sub(tab(m4, 4), 40, 80), iq4, OP.mult, lb1, OP.add)
        return mu

    onat, mnat, mrow = lst(20), lst(20), row()
    copy(onat, V("oi"))
    run("v", lambda: g.vector.tensor_copy(ind(V("prow"), onat), ap(V("iota"))), [V("iota"), onat], [V("prow")], "scat")
    copy(mnat, V("mi"))
    pick("s", V("orow"), V("iota"), onat)
    XM = ON["x0"] == "m"
    for h in range(0 if XM else 2):
        pick(ON["pm%d" % h], half("pmrow", h), V("prow"), sub(mnat, 10 * h, 10 * h + 10))
    for h in range(0 if XM else 2):
        pick(ON["M%d" % h], half("Mrow", h), V("pmrow"), sub(onat, 10 * h, 10 * h + 10))
    if XM or XW: pick("s", mrow, V("iota"), mnat)
    if XW:
        mu = mates(mrow)
    else:
        mu = [lst(10), sub(mnat, 10, 20)]
        ts(mu[0], V("mi", 0, 10), -float(B), OP.add)

    def couples(name, first):
        out = row()
        for e in range(2):
            scan(sub(out, B * e, B * e + B), V(name, e if first else 1 - e, C - 1 + (e if first else 1 - e), 2))
        return tab(out)

    scaled("v", V("cur0", 40, 60), couples("orow", True), iw2, 1.0)
    if XM:
        pick("s", V("xrow"), mrow, onat)
        x0w, xu, M0w = couples("xrow", False), lst(20), row()
        ts(xu, x0w, iw, OP.mult, float(B), OP.add)
        for h in range(2):
            pick(ON["M%d" % h], half("Mrow", h), V("prow"), sub(xu, 10 * h, 10 * h + 10))
        M0w = table(V("Mrow"))
    else: M0w = couples("Mrow", False)
    ts(V("vi0", 20, 40), M0w, iw, OP.mult, float(B), OP.add)
    P, pu = table(V("prow")), lst(20)
    ts(pu, P, iw, OP.mult, float(B), OP.add)
    if not ZW:
        p0, P = P, tmp(20)
        scaled("s", P, p0, 1.0, wlo)

    quant(V("uq"), V("up"), V("ut"))
    run("s", lambda: g.scalar.activation(T.up16[:], T.up[:].indirect(T.ulu[:]), AF.Copy), [V("up"), V("ulu")], [V("up16")], "ind")
    run("v", lambda: g.vector.tensor_copy(T.uq16[:].bitcast(dt.uint32), T.uq[:].bitcast(dt.uint32).indirect(T.ulu[:])), [V("uq"), V("ulu")], [V("uq16")], "ind")

    def static(t):
        k = t % 2
        cur = V("cur%d" % t)
        a = 1 if t < 2 else 0
        o0, o1 = sub(cur, 40, 50), sub(cur, 50, 60)
        vi = V("vi%d" % t)
        M, uM = sub(vi, 20, 40), sub(cur, 60, 80)
        if t:
            copy(sub(vi, 0, 20), sub(cur, 0, 20))
            ts(M, sub(vi, 0, 20), 1023, OP.bitwise_and)
        if t not in TD: ts(sub(vi, 40, 60), sub(vi, 0, 20) if t else M, 1022, OP.bitwise_and)
        if t: tt(uM, M, KB, OP.subtract)
        else: tt(uM, M0w, KBw, OP.subtract)
        d, pr, nb, dob, gap, m1, m2, res, S = [tmp(n) for n in (30, 30, 10, 10, 10, 10, 10, 10, 10)]
        us, ixu, Mu2 = lst(20), lst(10), lst(40)
        Mu = sub(Mu2, 0, 20)
        for c0, c1 in ((0, 30),) if t else ((0, 10), (20, 30)):
            lo, hi = sub(cur, 40 + c0, 40 + c1), sub(cur, 50 + c0, 50 + c1)
            tt(sub(pr, c0, c1), lo, hi, OP.mult)
            if c0: lo, hi = sub(M0w, 0, 10), sub(M0w, 10, 20)
            tt(sub(d, c0, c1), hi if a else lo, lo if a else hi, OP.subtract)
        do = sub(d, 0, 10)
        ts(nb, sub(uM, 10 * a, 10 * a + 10), 0.0, OP.not_equal)
        if k: scaled("v", sub(nb, 0, 1), sub(nb, 0, 1), no0)
        tt(sub(cur, 30, 40), o1, nb, OP.mult)
        ts(us, sub(cur, 30, 50), float(C), OP.add)
        if not a: const(V("sc", C, C + 1), -HUGE)
        scaled("v", gap, do, 1.0 / 1024, B / 512.0)
        tt(m1, sub(pr, 0, 10), gap, OP.min)
        tt(m2, sub(pr, 20, 30) if t else m1, sub(d, 20, 30), OP.min)
        tt(res, m1 if t else sub(pr, 20, 30), m2, OP.min)
        ts(ixu, res, 512.0, OP.mult)
        act(S, res, 1024.0, 0.0, AF.Relu)
        ts(S, res, 1024.0, OP.mult, 0.0, OP.max)
        either("v")
        if t in TD:
            ts(sub(Mu2, 20, 40), M, 1.5, OP.mult, 0.75, OP.add)
            if not t and not XM: copy(Mu, M)
        else: copy(Mu2, sub(vi, 20, 60))
        val, d1, sv = sub(cur, 0, 20), V("d1%d" % t, 0, 128, 2), sub(six, 0, 4)
        if t:
            pick("s", d1, val, sv, w)
        else:
            x0 = tmp(20)
            if not XM: pick(ON["x0"], V("xrow"), V("orow"), Mu)
            scaled("v", x0, x0w if XM else table(V("xrow")), 1024.0, wv)
            tt(val, x0, M0w, OP.add)
            pick("v", d1, val, sv)
        dr = "dr%d" % t
        if t in TD: pick("s", V("tdb", 0, 3 * B, 3), V("cw"), ixu)
        else:
            pick("s", place(dr, 0), V("cw"), ixu)
            if t: scaled("v", place(dr, 1), place(dr, 0), -1.0)
            else: pick("v", place(dr, 1), V("cw"), ixu, -1.0)
            if t: pick("s", V("dm%d" % t), win0(dr, k), Mu)
            for h in range(0 if t else 2):
                pick("sv"[h], half("dm0", h), win0(dr, k), sub(Mu, 10 * h, 10 * h + 10))
        return dict(a=a, do=do, S=S, oA=o0 if a else o1, oB=o1 if a else o0, oAu=sub(us, 10 * a, 10 + 10 * a),
                    oBu=sub(us, 10 - 10 * a, 20 - 10 * a), Mf=sub(Mu2, 20, 40))

    FB = [[0, 1, 2, 3], [5, 6, 7, 0]]
    held = []

    def products(src, h, z, t):
        q, p = half("xq", h), half("xp", h)
        quant(q, p, htile(src, h))
        mm(bank(4), V("uq16"), V("up16"), q, p)
        scaled(ON["sc%d" % z], V("sc", C * h + 1, C * h + C, 2), bank(4), 1.0)
        qe, pe, lq, lp = [half(s + str(t), h) for s in ("qe", "pe", "lq", "lp")]
        raw = (t, z) in RAW
        if raw: send(t, "%d%d" % (t, z), [(lq, q, True), (lp, p, False)], 800)
        while held: send(*held.pop())
        for b in range(4):
            mm(bank(FB[z][b]), cols("eq", b), cols("ep", b), q, p)
            if raw: scaled("s", wfF(b, h), bank(FB[z][b]), 0.5)
            elif XW or ON["ft"]: scaled("s", el("ft", b, h), bank(FB[z][b]), 1.0)
            else:
                scaled("s", wfF(b, h), bank(FB[z][b]), 0.5)
                scaled("v", el("ft", b, h), wfF(b, h), 2.0)
        if raw: return
        quant(qe, pe, htile("ft", h))
        held.append((t, "%d%d" % (t, z), [(lq, qe, True), (lp, pe, False)], 800))
        if (t, 1) not in RAW or t not in ON["swap"]: send(*held.pop())
        if ZW: scaled("v", htile("wf", h), htile("ft", h), 0.5)
        elif XW or ON["ft"]:
            for b in range(4): scaled("v", wfF(b, h), el("ft", b, h), 0.5)

    def send(t, tag, pairs, size):
        dst = T.cores[rank ^ STEP[t]]
        rid, pid = topo.addr(dst)[:2]
        arr, loc, full = "arr" + tag, "loc" + tag, len(pairs) * len(topo.engines(core, dst))

        def issue():
            order("g", [p[1] for p in pairs], [])
            for land, src, codes in pairs:
                g.remote_dma(by(land) if codes else ap(land), by(src) if codes else ap(src), T.sem[arr], T.sem[loc], pid, rid, topo.mask(core, dst))
            count[arr] = count[loc] = full
            note("g", loc, full, [p[1] for p in pairs], [])
            for land, src, codes in pairs:
                log.setdefault(land[0], []).append((land, arr, full, True, "r"))

        token = [("sent" + tag, 0, 1, 1), ("sends", 0, 1, 1)]
        put("g", issue, [p[1] for p in pairs], token[:1], [len(pairs) * m["call"] + m["first"] * (not [c for c in calls if c[0] == "e"]) for m in MACHINES], 0.35)
        put("e", lambda: None, [p[1] for p in pairs] + token[:1], [p[0] for p in pairs] + token[1:],
            [128 * size / m["rate"] + 0.16 * len(pairs) for m in MACHINES], 0.3)

    r = static(0)
    products("x0", 0, 0, 0)
    products("x0", 1, 1, 0)
    for t in range(3):
        k = t % 2
        nl = 5 + k
        a = r["a"]
        tp, er = "tp", "er%d" % t
        if ON["sb"] == "2":
            pick("s", V("sb", 0, 96), V("sc"), sub(r["oBu"], 0, 6))
            pick("v", V("sb", 96, B), V("sc"), sub(r["oBu"], 6, 10))
        else: pick(ON["sb"], V("sb"), V("sc"), r["oBu"])
        tq = V("tda", 1, 3 * B, 3) if t in TD else place(tp, 0)
        tti(tq, V("sc"), r["oAu"], V("sb"), OP.is_gt)
        ur, us, tc, eu, d1, e = row(), row(), tmp(10), lst(20), V("d1%d" % t), V("ne%d" % t, 5, 120, 6)
        if t in TD:
            n3 = [V(z, 0, 3 * B) for z in ("td", "tda", "tdb")]
            run("v", lambda n3=n3: g.vector.tensor_tensor_scan(ap(n3[0]), ap(n3[1]), ap(n3[2]), 0.0, OP.mult, OP.add), n3[1:], n3[:1])
            n = ON["TD"]
            for h in range(n):
                pick("sv"[h], sub(ur, C // n * h, C // n * (h + 1)), V("td", 0, 3 * B + 2 * k), sub(r["Mf"], 20 // n * h, 20 // n * (h + 1)))
            scaled(ON["tp"], place(tp, 0), tq, 1.0)
        else: tti(ur, win0(tp, k), r["Mf"], V("dm%d" % t), OP.mult)
        tw = table(tq, B)
        act(tc, tw, iw2, -1.0, AF.Relu)
        ts(tc, tw, iw, OP.mult, 0.5, OP.is_gt)
        either("v")
        scan(us, ur)
        for z in range(2):
            tt(V("d0", 60 * z + 4, 60 * z + 60, 6), tc, r["S"], OP.is_gt)
        pick("v", sub(d1, 1, 128, 2), us, sub(six, 4, 8))
        n6 = [V(z, 0, 120) for z in ("ne%d" % t, "d0", d1[0])]
        run("v", lambda n6=n6: g.vector.tensor_tensor_scan(ap(n6[0]), ap(n6[1]), ap(n6[2]), 0.0, OP.mult, OP.add), n6[1:], n6[:1])
        A, Bv = (10 * a, 10 * a + 10), (10 - 10 * a, 20 - 10 * a)
        ts(eu, e, iw1k, OP.mult)
        scaled(ON["tp"], place(tp, 1), tq, -1.0)
        euA, euB = sub(eu, *A), sub(eu, *Bv)
        le = V("le%d" % t)
        send(t, "%d2" % t, [(le, eu, False)], 40)
        t1 = tmp(10)
        tt(t1, tc, r["do"], OP.mult)
        if t < 2:
            nx, go = V("cur%d" % (t + 1)), V("go%d" % t)
            stay, move = (A, Bv) if t == 0 else (Bv, A)
            z = 1 - t
            scaled("v", sub(go, z, z + 10), sub(e, *move), iw, 1.0 - 2.0 * t)
            scaled("v", sub(nx, 0, 10), sub(e, *stay), iw, 1.0 - 2.0 * t)
            tt(sub(nx, 50, 60) if t == 0 else sub(go, 30, 40), r["oA"], t1, OP.add)
            tt(sub(go, 31, 41) if t == 0 else sub(nx, 50, 60), r["oB"], t1, OP.subtract)
            sv, hv, pairs = T[go[0]], T[nx[0]], []
            for q in range(0, 128, 16):
                pairs.append((hv[q + 1:q + 16, 10:50], sv[q:q + 15, 1:41]) if t == 0 else (hv[q:q + 15, 10:50], sv[q + 1:q + 16, 0:40]))
            for y in (0, 30):
                if t == 0:
                    pairs.append((hv[0:128:16, y + 11:y + 20], sv[15:128:16, y + 1:y + 10]))
                    pairs.append((hv[0:128:16, y + 10:y + 11], sv[15:128:16, y + 10:y + 11]))
                else:
                    pairs.append((hv[15:128:16, y + 10:y + 19], sv[0:128:16, y + 1:y + 10]))
                    pairs.append((hv[15:128:16, y + 19:y + 20], sv[0:128:16, y:y + 1]))
            dma("y", pairs, [go], [sub(nx, 0, 60)])
        else:
            of, ofu = tmp(20), lst(20)
            tt(sub(of, 0, 10), r["oA"], t1, OP.add)
            tt(sub(of, 10, 20), r["oB"], t1, OP.subtract)
            ts(ofu, of, 0.5, OP.mult, 159.5, OP.add)
        fr, mr = row(), row()
        kn = (t + 1) % 2 if t < 2 else 0
        pick(ON["p"], fr, win0(tp, k), pu)
        pick("s", place(er, 0, kn - k), V("iota"), euA)
        pick("s", place(er, 1, kn - k), V("iota"), euB)
        if k: scaled("v", V(er, 16 + C - 1, 16 + C), V(er, 15, 16), 1.0)
        pn, pu = tmp(20), lst(20)
        tt(pn, P, table(fr), OP.add)
        P = pn
        ts(pu, pn, iw, OP.mult, float(PB + kn), OP.add)
        pick(ON["mn"], mr, win0(er, kn), pu)
        if EP:
            pv, vm, vl, mn = pu, tmp(20), lst(20), table(mr)
            if t < 2:
                pf = tmp(20)
                ts(pf, pn, wlo, OP.is_lt, w1k, OP.mult)
            if k:
                pz, pv = tmp(20), lst(20)
                tt(pz, pf, pn, OP.add)
                ts(pv, pz, iw, OP.mult, float(PB + kn), OP.add)
        elif not ZW:
            pz, vm, vl, mn = tmp(20), tmp(20), lst(20), table(mr)
            if t < 2:
                pf = tmp(20)
                ts(pf, pn, wlo, OP.is_lt, w1k, OP.mult)
            tt(pz, pf, pn, OP.add)
            tt(vm, pz, mn, OP.max)
            ts(vl, vm, iw, OP.mult, float(B), OP.add)
        if XW: mun = mates(mr)
        else:
            mun = lst(20)
            ts(sub(mun, 0, 10), sub(mn, 0, 10), iw, OP.mult)
            ts(sub(mun, 10, 20), sub(mn, 10, 20), iw, OP.mult, float(B), OP.add)
            mun = [sub(mun, 0, 10), sub(mun, 10, 20)]
        early = 1 - k
        for h in (early, 1 - early):
            ah, af = htile("ah", h), htile("af", h)
            if XW: pick("s", ah, htile("ft", 1 - h), sub(mu, 40 * h, 40 * h + 40), 0.5)
            else:
                for b in range(4): pick("s", part("ah", h, b), wfF(b, 1 - h), mu[h])
            q = ON["af%d" % (h != early)]
            if q == "d":
                dma("y", [(ap(af), ap(ah))], [ah], [af])
                dma("g", [(ap(af), ap(ah))], [ah, af], [af], 2.5, True)
            else:
                scaled(q, af, ah, 2.0)
        mu = mun
        zs = (1 - early, early)
        lq, lp = "lq%d" % t, "lp%d" % t
        for z, h in enumerate(zs if ON["F2"] == 2 else (0,)):
            for b in range(4):
                n = bank(FB[1][b] if z == ON["bank"] else b + 1) if ON["F2"] == 2 else bank((1, 2, 3, 5)[b], C)
                q, p = (half(lq, h), half(lp, h)) if ON["F2"] == 2 else (V(lq), V(lp))
                if (t, z) in RAW:
                    for c in range(0 if b else 4):
                        n2 = bank(c + 1 if z == 0 else FB[1][c])
                        mm(n2, cols("eq", c), cols("ep", c), q, p)
                        scaled("s", el("ft", c, h), n2, 1.0)
                    if z: n = bank(b + 1)
                    q, p = half("qe%d" % t, h), half("pe%d" % t, h)
                    if not b: quant(q, p, htile("ft", h))
                mm(n, cols("eq", b), cols("ep", b), q, p)
                at = ("wf", b * WD + C + 1 + B * h) if EP else ("w2", b * C + B * h)
                scaled("s", V(at[0], at[1], at[1] + n[2]), n, 0.5)
        if EP:
            for z, blk in enumerate((A, Bv)):
                pick("sv"[z], place(er, z, kn - k + (C + 1) * k, 16 * nl), V("iota"), sub(le, blk[0], blk[0] + nl))
            vwin, n = V(er, 16, 16 + C + 1 + B) if k else win0(er, kn), ON["PH"]
            for h in range(n) if n == 1 else zs:
                c0, c1 = 20 // n * h, 20 // n * (h + 1)
                pick("s", V("vr", 16 * c0, 16 * c1), vwin, sub(pv, c0, c1))
                scan(V("vt4", 16 * c0, 16 * c1), V("vr", 16 * c0, 16 * c1))
                tt(sub(vm, c0, c1), tab(V("vt4", 16 * c0, 16 * c1)), sub(pf, c0, c1), OP.add)
                ts(V("vl%d" % t, c0, c1), sub(vm, c0, c1), iw, OP.mult, float(B), OP.add)
            vl = V("vl%d" % t, 0, 20)
        for b in range(0 if EP else 4):
            for z, blk in enumerate((A, Bv)):
                at, step = (4 * (C + 1 - k + z) + b, 8) if ZW else (b * WD + C + 1 - k + z, 2)
                pick("sv"[z], V("wf", at, at + step * (16 * nl - 1) + 1, step), V("w2", b * C, b * C + C), sub(le, blk[0], blk[0] + nl))
        if ZW:
            vwin, vl = win0("vw%d" % kn, kn), V("vl%d" % t)
            scaled("v", V(vwin[0], 16 + kn + B, 16 + kn + C), V(er, 16 + kn + B, 16 + kn + C), 1.0, -float(MID))
            pick("s", V("vr"), vwin, pu)
            scan(V("vt4"), V("vr"), 4)
            ts(vl, tab(V("vt4"), 4), iq4, OP.mult, lb2, OP.add)
        for z, h in enumerate(zs):
            if ZW: tti(htile("zt", h), V("wf", 0, 4 * (C + 1 + B)), sub(vl, 40 * h, 40 * h + 40), htile("ah", h), OP.add)
            else:
                for b in range(4):
                    tti(el("zt", b, h), V("wf", b * WD, b * WD + C + 1 + (C if EP else B)), sub(vl, 10 * h, 10 * h + 10), part("ah", h, b), OP.add)
            quant(half("zq", h), half("zp", h), htile("zt", h))
            for b in range(4):
                n = 4 * z + b
                mm(bank(n), cols("wq", b), cols("wp", b), half("zq", h), half("zp", h))
                scaled("s", part("gs", h, b), bank(n), 0.0078125)
        if t < 2:
            r = static(t + 1)
        else:
            quant(V("vq"), V("vp"), V("vt"))
            pick("s", V("romo", 0, C - 1, 2), V("iota"), sub(ofu, 0, 10), bias=float(B))
            pick("s", V("romo", 1, C, 2), V("iota"), sub(ofu, 10, 20), bias=float(B))
            scaled("s", V("romm"), mr, 1.0, float(B))
            dma("y", [(T.om[:, 0:C], T.romo[0:128:16, :]), (T.om[:, C:2 * C], T.romm[0:128:16, :])], [V("romo"), V("romm")], [])
        for z, h in enumerate(zs[::-1]):
            if XW: tti(htile("xt", h), htile("gs", 1 - h), sub(mu, 40 * h, 40 * h + 40), htile("af", h), OP.add)
            else:
                for b in range(4):
                    tti(el("xt", b, h), part("gs", 1 - h, b), mu[h], part("af", h, b), OP.add)
            if t < 2:
                products("xt", h, z, t + 1)
            else:
                q, p = half("xq", h), half("xp", h)
                quant(q, p, htile("xt", h))
                mm(bank(h), V("vq"), V("vp"), q, p)
                dma("y", [(T.oc[:, 4 * B * h:4 * B * h + 4 * B], by(q))]
                    + [(T.osc[4 * z:4 * z + 4, B * h:B * h + B], T.xp[32 * z:32 * z + 4, B * h:B * h + B]) for z in range(4)], [q, p], [], 2.5)
                scaled("s", half("ysb", h), bank(h), 1.0)
                dma("ys"[z], [(T.y[:, B * h:B * h + B], ap(half("ysb", h)))], [half("ysb", h)], [], 2.5)
    if "plan" not in PLAN:
        seen, before = {}, []
        for i, (q, issue, reads, writes, cost, late, other) in enumerate(calls):
            p = set()
            for vs, isw in ((reads, False), (writes, True)):
                for v in vs:
                    for old, j, oldw in seen.get(v[0], ()):
                        if v[0][:2] == "ps" or ((isw or oldw) and clash(v, old)): p.add(j)
            for vs, isw in ((reads, False), (writes, True)):
                for v in vs: seen.setdefault(v[0], []).append((v, i, isw))
            if q == "g" and late: p.update(j for j in range(i) if calls[j][0] == "g" and not calls[j][5])
            before.append(sorted(p))
        PLAN["plan"] = plan([(c[0], c[4], c[5]) for c in calls], before, [c[6] and (c[6][0], c[6][4]) for c in calls])
    for i, q in sorted(PLAN["plan"], key=lambda c: min(c[0], first)):
        (calls[i] if calls[i][0] == q else calls[i][6])[1]()
    for sem, n in count.items():
        know("g", sem, n)


PLAN = {}
WAKE, OWN = 0.22, 0.17
PASSES = 6
QUEUES = "vstgye"


def lay(ops, before, rank, back):
    at, busy = [0.0] * len(ops), {q: [] for q in QUEUES}
    for i in rank:
        q, cost, late = ops[i]
        t = late if back and not before[i] else 0.0
        for j in before[i]:
            p = i if back else j
            t = max(t, at[j] + ops[j][1] + ops[p][2] + (OWN if ops[j][0] == q and not ops[p][2] else WAKE))
        k, row = 0, busy[q]
        for k in range(len(row) + 1):
            if k == len(row) or t + cost <= row[k][0] + 1e-9: break
            t = max(t, row[k][1])
        row.insert(k, (t, t + cost))
        at[i] = t
    return at


def plan(ops, before, other):
    n, every = len(ops), ops
    ops = [(q, cost[0], late) for q, cost, late in ops]
    after = [[] for i in range(n)]
    for i in range(n):
        for j in before[i]: after[j].append(i)
    urge = [0.0] * n
    for i in range(n - 1, -1, -1):
        urge[i] = ops[i][1] + ops[i][2] + max([urge[j] + WAKE for j in after[i]] + [0.0])
    rank, best = sorted(range(n), key=lambda i: (-urge[i], i)), None
    for turn in range(PASSES):
        at = lay(ops, before, rank, False)
        end = max(at[i] + ops[i][1] + ops[i][2] for i in range(n))
        if best is None or end < best[0]: best = (end, at)
        late = lay(ops, after, sorted(range(n), key=lambda i: (-at[i] - ops[i][1], -i)), True)
        rank = sorted(range(n), key=lambda i: (-late[i] - ops[i][1], i))
    PLAN["end"] = best[0]
    seq = sorted(range(n), key=lambda i: (best[1][i], i))
    best = min(polish(every, before, after, other, seq, SEED + k) for k in range(STARTS))
    PLAN["ends"] = best[2:]
    return best[1]


MACHINES = [dict(zip(("compute", "gather", "act", "product", "call", "rate", "more", "own", "wake", "hide", "first"), m)) for m in (
    (1.0, 1.25, 0.07, 1.3, 0.3, 200e3, 0.15, 0.17, 0.2, True, 0.8), (1.0, 1.15, 0.06, 1.2, 0.3, 200e3, 0.0, 0.2, 0.23, False, 0.8),
    (1.4, 1.5, 0.09, 1.4, 0.4, 150e3, 0.5, 0.17, 0.2, False, 0.8))]
TRIES, SOON, HEAT, REACH, AIM, SEED, STARTS = 300000, 0.2, 0.0005, 30, 0.5, 5, 1


def polish(ops, before, after, other, seq, seed):
    n = len(ops)
    qn = [QUEUES.index(o[0]) for o in ops]
    known, need = [0] * n, []
    for i in range(n):
        keep, a = [], 0
        for j in sorted(before[i], reverse=True):
            if not (a >> j) & 1:
                keep.append(j)
                a |= known[j] | (1 << j)
        known[i] = a
        need.append(keep)
    sets = []
    for k, m in enumerate(MACHINES):
        cost = [{qn[i]: ops[i][1][k]} for i in range(n)]
        for i in range(n):
            if other[i]: cost[i]["vs".index(other[i][0])] = other[i][1][k]
        sets.append((cost, [o[2] + m["more"] if o[2] else 0.0 for o in ops], m["own"], m["wake"], m["hide"]))

    def tops(seq, lo):
        top, k, left = [-1] * 6, lo - 1, 7
        while left and k >= 0:
            i = seq[k]
            if left >> qn[i] & 1:
                left &= ~(1 << qn[i])
                top[qn[i]] = i
            k -= 1
        for q in (3, 4, 5):
            k = -1
            for i in rare[q]:
                if k < pos[i] < lo: k, top[q] = pos[i], i
        return top

    def walk(seq, lo, hi, end, m, top, moved=63):
        cost, late, own, wake, hide = m
        free = [end[i] - late[i] if i >= 0 else 0.0 for i in top]
        end = list(end)
        for k in range(lo, n):
            i = seq[k]
            q = qn[i]
            t = f = free[q]
            for j in need[i]:
                e = end[j]
                if e + wake > t and (e >= f - 1e-9 or not hide):
                    e += own if qn[j] == q else wake
                    if e > t: t = e
            t += cost[i][q]
            free[q] = t
            t += late[i]
            if t != end[i]:
                end[i] = t
                moved |= 1 << q
                if reach[i] > hi: hi = reach[i]
            elif k > hi:
                moved &= ~(1 << q)
                if not moved: break
        return end

    def worth(end):
        return max(end) + SOON * sum(end) / n

    pos, users = [0] * n, [[] for i in range(n)]
    for k, i in enumerate(seq): pos[i] = k
    for i in range(n):
        for j in need[i]: users[j].append(i)
    reach = [max([pos[j] for j in users[i]] + [0]) + 1 for i in range(n)]
    rare = [[i for i in range(n) if qn[i] == q] for q in range(6)]
    ends = [walk(seq, 0, n, [0.0] * n, m, [-1] * 6) for m in sets]
    base = [worth(e) for e in ends]
    now, rng, last = 1.0, np.random.RandomState(seed), [1.0] * len(sets)
    best = (now, seq, list(qn), [max(e) for e in ends])
    for turn in range(TRIES):
        if turn % 100 == 0:
            m = turn // 100 % len(sets)
            end, cost, late, top, prev, block = ends[m], sets[m][0], sets[m][1], {}, {}, []
            for j in seq:
                prev[j] = top.get(qn[j], -1)
                top[qn[j]] = j
            i = end.index(max(end))
            while i >= 0:
                p, t = prev[i], end[i] - late[i] - cost[i][qn[i]]
                if p >= 0 and end[p] - late[p] > t - 1e-6:
                    if p not in need[i]: block += [(p, 1), (i, -1)]
                    i = p
                else:
                    i = max(need[i], key=lambda j: end[j]) if need[i] else -1
        i, way = block[int(rng.randint(len(block)))] if block and rng.rand() < AIM else (int(rng.randint(n)), 1 if rng.rand() < 0.5 else -1)
        a = pos[i]
        lo = max([pos[j] for j in before[i]] + [-1]) + 1
        hi = min([pos[j] for j in after[i]] + [n]) - 1
        b = a + int(rng.randint(1, REACH)) * way
        b = max(lo, min(hi, b))
        lim = now - HEAT * max(0.0, 1.0 - 1.2 * turn / TRIES) * math.log(rng.rand() + 1e-12)
        flip = other[i] and rng.rand() < 0.3
        if flip: qn[i] = 1 - qn[i]
        elif b == a or not [j for j in seq[min(a, b):max(a, b) + 1] if j != i and qn[j] == qn[i]]: continue
        new = seq[:a] + seq[a + 1:]
        new.insert(b, i)
        total, got, top = 0.0, [], tops(seq, min(a, b))
        for m, e, w in zip(sets, ends, base):
            got.append(walk(new, min(a, b), max(a, b, reach[i]), e, m, top, 3 | 1 << qn[i]))
            r = worth(got[-1]) / w
            total += r / len(sets)
            if r > last[len(got) - 1] + 0.006: total += 9.0
            if total > lim: break
        if total <= lim:
            now, seq, ends = total, new, got
            last = [worth(e) / w for e, w in zip(ends, base)]
            for k in range(min(a, b), max(a, b) + 1): pos[seq[k]] = k
            for k in range(min(a, b), max(a, b) + 1):
                for j in need[seq[k]]: reach[j] = max([pos[u] for u in users[j]]) + 1
            if now < best[0]: best = (now, seq, list(qn), [max(e) for e in ends])
        elif flip: qn[i] = 1 - qn[i]
    return best[0], [(i, QUEUES[best[2][i]]) for i in best[1]], best[3]
